import numpy as np, ml_dtypes
CORES = [24,25,26,27,28,29,30,31]
N = 8
BF = ml_dtypes.bfloat16
def gentries(a):
    return np.ascontiguousarray(a.reshape(8, 16, -1).transpose(0, 2, 1)).reshape(8, -1)
def gtable(e):
    e = np.asarray(e); return np.ascontiguousarray(e.reshape(8, -1, 16).transpose(0, 2, 1)).reshape(128, -1).astype(np.int32)
W, R, PG, V, H = 2048, 32, 128, 6, 3
K = PG * R
def parts(rng):
    x = rng.integers(0, 256, (N, 8, 16, W)); e = rng.integers(0, 256, (N, 8, 16, PG)); w = rng.integers(0, 16, (N, 8, 16))
    h = rng.choice(np.array([1000, 1300, 1600, 1900]), (N, 8, 1)) + rng.integers(-300, 301, (N, 8, 16))
    l = rng.integers(0, W, (N, 8, K)); share = np.repeat(rng.choice(np.array([0.0, 0.3, 0.6, 0.9]), (N, 8, PG)), R, axis=2)
    s = np.where(rng.random((N, 8, K)) < share, l, rng.integers(0, W, (N, 8, K)))
    c = rng.random((N, 8, K)); p = np.where(c < 0.3, s, np.where(c < 0.4, l, rng.integers(0, W, (N, 8, K))))
    return x, e, w, h, p, s, l, rng.integers(0, W, (N, 8, K))
def pack(x, e, w, h, p, s, l, q):
    r = {"xt": x.reshape(N, 128, W).astype(np.float32).astype(BF), "ed": e.reshape(N, 128, PG).astype(np.float32).astype(BF),
         "wt": np.ascontiguousarray(w.reshape(N, 128, 1)).astype(np.int32), "th": np.ascontiguousarray(h.reshape(N, 128, 1)).astype(np.int32)}
    for k, z in (("pl", p), ("sl", s), ("ll", l), ("ql", q)): r[k] = np.stack([gtable(a) for a in z])
    return r
def setup_inputs(rng):
    return pack(*parts(rng))
def setup_inputs_spread(rng):
    x, e, w, h, p, s, l, q = parts(rng)
    x = np.minimum((np.exp2(8 * rng.random((N, 8, 1, W))) * rng.random((N, 8, 16, W))).astype(np.int64), 255)
    e = np.minimum((np.exp2(8 * rng.random((N, 8, 1, PG))) * rng.random((N, 8, 16, PG))).astype(np.int64), 255)
    w = (16 * rng.random((N, 8, 16)) ** 3).astype(np.int64); h = np.minimum(np.exp2(12 * rng.random((N, 8, 16))).astype(np.int64) - 1, 4080)
    p, s, l, q = [(W * rng.random((N, 8, K)) ** 3).astype(np.int64) for z in range(4)]
    s = np.where(rng.random((N, 8, K)) < np.repeat(rng.random((N, 8, PG)), R, axis=2), l, s)
    return pack(x, e, w, h, p, s, l, q)
def setup_inputs_ends(rng):
    x = 255 * rng.integers(0, 2, (N, 8, 16, W)); e = 255 * rng.integers(0, 2, (N, 8, 16, PG)); w = 15 * rng.integers(0, 2, (N, 8, 16)); h = 4080 * rng.integers(0, 2, (N, 8, 16))
    kind = rng.integers(0, 3, (N, 8, 1)); kind[:, 7] = 0; kind[0, 0] = 0; kind[1, 1] = 1
    x[..., 0] = np.where(kind == 0, 0, np.where(kind == 1, 255, x[..., 0])); x[..., W - 1] = np.where(kind == 0, 255, np.where(kind == 1, 0, x[..., W - 1]))
    w[:, :, 5] = 0; w[:, 7] = 15; w[:, :, 2] = 15; w[:, :, 13] = 15
    h[:, :, 0] = 0; h[:, :, 15] = 0; h[:, :, 1] = 4080; h[:, :, 14] = 4080
    p, s, l, q = [np.where(rng.random((N, 8, K)) < 0.75, (W - 1) * rng.integers(0, 2, (N, 8, K)), rng.integers(0, W, (N, 8, K))) for z in range(4)]
    pv, sv, lv = [z.reshape(N, 8, PG, R) for z in (p, s, l)]; k = np.arange(R)
    for i in (0, 1, 2, 3, PG - 4, PG - 3, PG - 2, PG - 1):
        pv[:, :, i] = 0; sv[:, :, i] = W - 1; lv[:, :, i] = W - 1
    lv[:, :, [0, PG - 1]] = np.where(k % 4 == 1, 0, W - 1)
    lv[:, :, [1, PG - 2]] = np.where((k % 4 == 1) | (k == 2), 0, W - 1)
    lv[:, :, [3, PG - 4]] = 0
    e[..., [0, PG - 1]] = 0; e[:, :, 2, [0, PG - 1]] = 255; e[:, :, 13, [0, PG - 1]] = 18
    e[..., [2, PG - 3]] = 0; e[..., [3, PG - 4]] = 255
    return pack(x, e, w, h, p, s, l, q)
def setup_inputs_corners(rng):
    x, e, w, h, p, s, l, q = parts(rng)
    cnt = np.roll(np.array([31, 32, 0, 8 * PG, 33, 1, 8 * PG - 1, 64])[:N], int(rng.integers(0, N))); fl = np.zeros((N, 8 * PG), bool)
    for r in range(N): fl[r, rng.permutation(8 * PG)[:int(cnt[r])]] = True
    fr = np.repeat(fl.reshape(N, 8, PG), R, axis=2)
    lv = l.reshape(N, 8, PG, R); lv[:, :, [0, PG - 1]] = (W - 1) * rng.integers(0, 2, (N, 8, 2, R))
    far = (l + rng.integers(1, W, l.shape)) % W; half = np.repeat(rng.random((N, 8, PG)) < 0.5, R, axis=2)
    s = np.where(fr, far, l); p = np.where(fr | half, l, rng.integers(0, W, l.shape))
    for g in range(8):
        if g % 4 < 3: q[:, g] = (l, s, p)[g % 4][:, g]
    w[:, 0] = 0; w[:, 7] = 15; w[:, 4] = 15; w[:, 3] = 0; w[:, 3, 15] = 15; w[:, 5] = 0; w[:, 5, 0] = 1
    h = np.where(rng.random(h.shape) < 0.5, rng.choice(np.array([0, 1, 4079, 4080]), h.shape), h)
    e[..., [0, PG - 1]] = 0; e[:, :, 2, [0, PG - 1]] = 255; e[:, :, 13, [0, PG - 1]] = 18
    e[..., 1] = 255; e[..., PG - 2] = 0
    return pack(x, e, w, h, p, s, l, q)
def setup_inputs_alike(rng):
    x, e, w, h, p, s, l, q = parts(rng)
    step = rng.choice(np.array([1, 4, 8, 32]), (N, 8, 1, 1)); lane = rng.integers(0, 8, (N, 8, 16, 1))
    x = step * (rng.integers(0, 8, (N, 8, 1, W)) ^ lane); e = step * (rng.integers(0, 8, (N, 8, 1, PG)) ^ lane)
    h = step[..., 0] * rng.integers(20, 81, (N, 8, 16))
    return pack(x, e, w, h, p, s, l, q)
def setup_inputs_near(rng):
    x, e, w, h, p, s, l, q = parts(rng); n = np.arange(N); f = rng.integers(0, 16, N); k = np.arange(R)
    s[:, 0] = l[:, 0]; h[:, 0] = 0
    h[:, 7] = 4080; x[:, 7, :, :2] = 0; x[:, 7, :, W - 2:] = 255; x[n, 7, f, 1] = 1; x[n, 7, f, W - 2] = 254
    pv, sv, lv, qv = [z.reshape(N, 8, PG, R)[:, 7] for z in (p, s, l, q)]
    for z in (pv, sv, lv): z[:, PG - 1] = W - 1; z[:, PG - 3] = W - 1
    pv[:, PG - 1, R - 4:] = 0; sv[:, PG - 1, R - 4:] = 0; qv[:, PG - 1, R - 4:] = W - 2
    pv[:, PG - 2] = 0; sv[:, PG - 2] = W - 1; sv[:, PG - 2, 0] = W - 2; lv[:, PG - 2] = np.where(k % 4 == 1, 0, W - 1)
    e[:, 7, :, PG - 3] = 0; e[n, 7, f, PG - 3] = 1
    pv[:, PG - 4] = 1; sv[:, PG - 4] = 0; lv[:, PG - 4] = W - 1
    return pack(x, e, w, h, p, s, l, q)
def check_inputs(d):
    bad = []
    for k, hi in (("xt", 255), ("ed", 255), ("wt", 15), ("th", 4080), ("pl", W - 1), ("sl", W - 1), ("ll", W - 1), ("ql", W - 1)):
        v = np.asarray(d[k]).astype(np.float64)
        if not (np.min(v) >= 0 and np.max(v) <= hi): bad.append("range of " + k)
        elif np.any(v != np.floor(v)): bad.append("whole numbers of " + k)
    return bad
def dist(y, z):
    return np.add.reduce(np.abs(y - z), axis=1, dtype=np.int32)
def reference(xt, ed, wt, th, pl, sl, ll, ql):
    x = xt.astype(np.float32).astype(np.int16).reshape(N, 8, 16, W); e = ed.astype(np.float32).astype(np.int16).reshape(N, 8, 16, PG)
    w = wt.astype(np.int32).reshape(N, 8, 16, 1); h = th.astype(np.int32).reshape(N, 8, 16)[:, :, np.arange(K) % 16]
    p, s, l, q = [np.stack([gentries(a) for a in z]).astype(np.int64) for z in (pl, sl, ll, ql)]
    more = 37 * (np.arange(K) % R); A = np.zeros(N, np.int64)
    for t in range(V):
        new = np.zeros_like(l); failed = np.zeros((N, 8, PG), bool); m = np.zeros((N, 8, 16, PG), np.int16)
        for r in range(N):
            vp, vs, vl, vq = [np.take_along_axis(x[r], z[r][:, None, :], 2) for z in (p, s, l, q)]
            a = dist(vp, vs); b = dist(vs, vl); c = dist(vp, vl); d = dist(vq, vs); o = dist(vl, np.repeat(e[r], R, axis=2))
            failed[r] = 2 * np.sum((c - b).reshape(8, PG, R), axis=2) < np.sum(a.reshape(8, PG, R), axis=2)
            u = np.repeat(np.sum(w[r] * e[r], axis=1) & (W - 1), R, axis=1).astype(np.int64)
            change = ((l[r] * u >> 5) + l[r] + more + A[r]) & (W - 1)
            new[r] = np.where(np.repeat(failed[r], R, axis=1) & (c < b), p[r], np.where(d < b, q[r], np.where(o >= h[r], change, l[r])))
            m[r] = np.max(vl.reshape(8, 16, PG, R), axis=3)
        got = np.roll(m, N // 2, axis=0)
        e = np.where(failed[:, :, None, :], np.abs(e - got), (e + got) >> 1)
        A = np.sum(failed, axis=(1, 2)).astype(np.int64) & 31
        q = np.where(new != l, l, q); p, s, l = s, l, new
        if t < V - 1: p, s, l, q = [np.roll(z, H, axis=0) for z in (p, s, l, q)]
    out = [np.stack([gtable(a) for a in z]).astype(np.float32) for z in (p, s, l, q)]
    return {"yp": out[0], "ys": out[1], "yl": out[2], "yq": out[3], "ye": e.reshape(N, 128, PG).astype(np.float32).astype(BF)}

@@ -1,0 +1,594 @@
+import numpy as np
+from concourse.mybir import AluOpType as OP, ActivationFunctionType as AF, AxisListType
+
+NV, HOP, NC = 6, 3, 8
+W = 2048
+WX = W + 384
+CH = 2048
+BIG = 8192.0
+DABS = {(t, 0) for t in range(5)}
+ASTAT, BSPLIT = True, True
+FIRST = {"s": -5.0, "l": -5.0, "dq": 5.0, "rq": -10.0, "vb": -5.0, "vc": -5.0, "vo": -10.0, "R": -10.0, "SB": -5.0, "MB": -5.0}
+
+FT = {}
+IT = {}
+
+
+def _fields(d, items):
+    o = 0
+    for k, n in items:
+        d[k] = (o, n)
+        o += n
+    return o
+
+
+NF = _fields(FT, [("LU", 128), ("CHp", 128), ("r3", 128), ("r2", 128), ("w", 64), ("PF", 128), ("LQ", 128),
+                  ("Csb", 128), ("Bsb", 128), ("As1", 8), ("As2", 64), ("junk", 64), ("cnt", 8)])
+NI = _fields(IT, [("ui", 64), ("ua", 64), ("LUi", 128), ("CHi", 128), ("r1", 128), ("h", 64)])
+
+SCRATCH = {
+    "tp": ("sbuf", [128, 256], "int32"), "tsx": ("sbuf", [128, 256], "int32"),
+    "tl": ("sbuf", [128, 256], "int32"), "tq": ("sbuf", [128, 256], "int32"),
+    "Lnum": ("sbuf", [128, 6 * 256], "int32"), "Loff": ("sbuf", [128, 9 * 256], "uint16"),
+    "Qoff": ("sbuf", [128, 6 * 256], "uint16"), "Qv": ("sbuf", [128, 6 * 256], "float32"),
+    "L6": ("sbuf", [128, 6 * 256], "float32"),
+    "finPS": ("sbuf", [128, 512], "float32"), "finLQ": ("sbuf", [128, 512], "float32"),
+    "fPS": ("sbuf", [128, 512], "float32"), "fLQ": ("sbuf", [128, 512], "float32"),
+    "tf": ("sbuf", [128, 4 * NF], "float32"), "ti": ("sbuf", [128, 4 * NI], "int32"),
+    "E0": ("sbuf", [128, 128], "bfloat16"),
+    "mmsg": ("sbuf", [128, 12 * 64], "bfloat16"), "mland": ("sbuf", [128, 12 * 64], "bfloat16"),
+    "emsg": ("sbuf", [128, 12 * 80], "bfloat16"), "eland": ("sbuf", [128, 12 * 80], "bfloat16"),
+    "idf": ("sbuf", [128, 128], "float32"), "grp8": ("sbuf", [128, 128], "float32"), "pair": ("sbuf", [128, 64], "float32"),
+    "pr0": ("sbuf", [128, 64], "bfloat16"), "pr1": ("sbuf", [128, 64], "bfloat16"),
+    "gr0": ("sbuf", [128, 128], "bfloat16"), "gr1": ("sbuf", [128, 128], "bfloat16"),
+    "ETs": ("sbuf", [128, 4 * 128], "bfloat16"),
+    "Ind": ("sbuf", [128, 2048], "bfloat16"), "maskz": ("sbuf", [128, 2048], "bfloat16"),
+    "one": ("sbuf", [128, 2048], "bfloat16"), "idn": ("sbuf", [128, 128], "bfloat16"),
+    "nidn": ("sbuf", [128, 128], "bfloat16"), "blk0": ("sbuf", [128, 128], "bfloat16"),
+    "blk": ("sbuf", [128, 128], "bfloat16"), "blkP": ("sbuf", [128, 128], "bfloat16"),
+    "blkN": ("sbuf", [128, 128], "bfloat16"), "blk2": ("sbuf", [128, 128], "float32"),
+    "Bp": ("sbuf", [128, 144], "bfloat16"), "Bn": ("sbuf", [128, 144], "bfloat16"),
+    "o16": ("sbuf", [128, 128], "bfloat16"),
+    "kin": ("sbuf", [128, 16], "int32"), "k37": ("sbuf", [128, 8], "float32"),
+    "wti": ("sbuf", [128, 8], "int32"), "thi": ("sbuf", [128, 8], "int32"),
+    "tci": ("sbuf", [128, 16], "int32"), "tcf": ("sbuf", [128, 16], "float32"),
+    "ai": ("sbuf", [128, 6 * 16], "int32"), "af": ("sbuf", [128, 6 * 16], "float32"),
+    "R0": ("psum", [128, 1024], "float32"), "R1": ("psum", [128, 1024], "float32"),
+    "SB": ("psum", [128, 512], "float32"), "CB": ("psum", [128, 512], "float32"),
+    "ZB": ("psum", [128, 512], "float32"), "MB": ("psum", [128, 512], "float32"),
+}
+for _t in range(NV):
+    SCRATCH["win%d" % _t] = ("sbuf", [128, WX], "bfloat16")
+for _z in range(4):
+    for _n in ("s", "dp", "ra"):
+        SCRATCH["%s%d" % (_n, _z)] = ("sbuf", [128, CH], "bfloat16")
+for _z in range(2):
+    for _n in ("l", "dq", "rq", "vb", "vc", "vo", "sc"):
+        SCRATCH["%s%d" % (_n, _z)] = ("sbuf", [128, CH], "bfloat16")
+
+SEMAPHORES = (["sV", "sS", "sP", "sG", "lsem", "fa", "fb", "fc"] + ["w%d" % t for t in range(1, NV)]
+              + ["m%d" % i for i in range(12)] + ["e%d" % i for i in range(12)]
+              + ["ld%d" % i for i in range(9)] + ["st%d" % i for i in range(10)])
+
+CYC = 0.83e-3 * 1.2
+PEC = 0.417e-3 * 1.2
+GAM = 1.5
+
+
+def rank_program(g, core, T, topo):
+    rank = T.rank_of(core)
+    if rank is None:
+        return
+    ENG = {"V": g.vector, "S": g.scalar, "P": g.tensor, "G": g, "Y": g.sync}
+    ESEM = {"V": "sV", "S": "sS", "P": "sP", "G": "sG"}
+    PSUM = ("R0", "R1", "SB", "CB", "ZB", "MB")
+    ops = []
+    acc = {}
+    boost = [1000.0]
+
+    def R(b, lo, hi, st=1, p=None):
+        return (b, lo, hi, st, p)
+
+    def ap(r):
+        b, lo, hi, st, p = r
+        sl = slice(lo, hi, st) if st != 1 else slice(lo, hi)
+        return T[b][p[0]:p[1], sl] if p else T[b][:, sl]
+
+    def n_of(r):
+        return (r[2] - r[1] + r[3] - 1) // r[3]
+
+    def ps(r):
+        return r[0] in PSUM
+
+    def overlap(a, b):
+        if a[1] >= b[2] or b[1] >= a[2]:
+            return False
+        if a[3] == b[3] and a[3] > 1 and (a[1] - b[1]) % a[3] != 0:
+            return False
+        return True
+
+    def op(eng, emit, rd, wr, occ, lat=None, sem=None, inc=0, deps=()):
+        k = len(ops)
+        dep = set(deps)
+        for w, regs in ((False, rd), (True, wr)):
+            for r in regs:
+                lst = acc.setdefault(r[0], [])
+                psb = r[0] in PSUM
+                for (k2, r2, w2) in lst:
+                    if k2 == k:
+                        continue
+                    if psb and ops[k2]["eng"] != eng:
+                        if r[1] // 512 <= (r2[2] - 1) // 512 and r2[1] // 512 <= (r[2] - 1) // 512:
+                            dep.add(k2)
+                            continue
+                    if (w or w2) and overlap(r, r2):
+                        dep.add(k2)
+        for w, regs in ((False, rd), (True, wr)):
+            for r in regs:
+                lst = acc[r[0]]
+                if w and r[3] == 1 and r[0] not in PSUM:
+                    lst[:] = [x for x in lst if x[0] == k or not (x[1][1] >= r[1] and x[1][2] <= r[2])]
+                lst.append((k, r, w))
+        ops.append({"eng": eng, "emit": emit, "dep": dep, "occ": occ, "lat": occ + 0.03 if lat is None else lat,
+                    "sem": sem, "inc": inc, "boost": boost[0] + FIRST.get((wr[0][0] if wr else "-").rstrip("0123456789"), 0.0)})
+        return k
+
+    def vcost(n, f=1.0):
+        return 0.06 + max(64, n * f) * CYC
+
+    def two(*rs):
+        for r in rs:
+            if not (r[0] in SCRATCH and SCRATCH[r[0]][2] in ("bfloat16", "uint16", "float16")) or ps(r):
+                return 1.0
+        return 0.5
+
+    def vtt(out, a, b, alu):
+        f = 1.0 if (ps(a) or ps(b)) else 2.0
+        return op("V", lambda e: [e.tensor_tensor(out=ap(out), in0=ap(a), in1=ap(b), op=alu)], [a, b], [out], vcost(n_of(out), f))
+
+    def vts(out, a, s1, op0, s2=None, op1=None):
+        cols = [x for x in (s1, s2) if isinstance(x, tuple)]
+
+        def em(e):
+            x1 = ap(s1) if isinstance(s1, tuple) else s1
+            x2 = ap(s2) if isinstance(s2, tuple) else s2
+            if op1 is None:
+                return [e.tensor_scalar(out=ap(out), in0=ap(a), scalar1=x1, scalar2=None, op0=op0)]
+            return [e.tensor_scalar(out=ap(out), in0=ap(a), scalar1=x1, scalar2=x2, op0=op0, op1=op1)]
+        return op("V", em, [a] + cols, [out], vcost(n_of(out), two(out, a)))
+
+    def vcopy(out, a):
+        return op("V", lambda e: [e.tensor_copy(out=ap(out), in_=ap(a))], [a], [out], vcost(n_of(out), two(out, a)))
+
+    def vset(out, c):
+        return op("V", lambda e: [e.memset(ap(out), c)], [], [out], vcost(n_of(out), two(out)))
+
+    def act(out, a, func, scale=1.0, acc_out=None):
+        def em(e):
+            if acc_out is not None:
+                return [e.activation(out=ap(out), in_=ap(a), func=func, accum_out=ap(acc_out))]
+            return [e.activation(out=ap(out), in_=ap(a), func=func)]
+        return op("S", em, [a], [out] + ([acc_out] if acc_out else []), 0.08 + max(64, n_of(out)) * CYC)
+
+    def gath_s(out, win, off):
+        return op("S", lambda e: [e.activation(out=ap(out), in_=ap(win).indirect(ap(off)), func=AF.Copy)], [win, off], [out],
+                  0.08 + n_of(out) * GAM * CYC)
+
+    def gath_sub(out, win, off, b):
+        return op("V", lambda e: [e.tensor_tensor(out=ap(out), in0=ap(win).indirect(ap(off)), in1=ap(b), op=OP.subtract)],
+                  [win, off, b], [out], 0.06 + n_of(out) * GAM * CYC)
+
+    def pe(mms):
+        rd, wr, cost = [], [], 0.0
+        for (o, l, r, a, z) in mms:
+            for x in (l, r):
+                if x not in rd:
+                    rd.append(x)
+            if o not in wr:
+                wr.append(o)
+            f = 4.0 if SCRATCH[r[0]][2] == "float32" else 1.0
+            cost += f * max(min(64, n_of(l)), n_of(r)) * PEC
+
+        def em(e):
+            return [e.matmul(out=ap(o), lhsT=ap(l), rhs=ap(r), start=a, stop=z) for (o, l, r, a, z) in mms]
+        rd2 = {}
+        for x in rd:
+            key = x[0]
+            if key in rd2:
+                rd2[key] = (key, min(rd2[key][1], x[1]), max(rd2[key][2], x[2]), 1, None)
+            else:
+                rd2[key] = x
+        return op("P", em, list(rd2.values()), wr, cost + 0.03, cost + 0.1)
+
+    def gsel(out, a, pattern, cmp, base, cm):
+        return op("G", lambda e: [e.affine_select(out=ap(out), in_=ap(a), pattern=pattern, compare_op=cmp, fill=0.0, base=base,
+                                                  channel_multiplier=cm)], [a], [out], 0.2 + 2 * n_of(out) * CYC)
+
+    def load(q, out, name, sem):
+        occ = 0.1
+        return op(q, lambda e: [e.dma_start(out=ap(out), in_=T[name][:])], [], [out], occ, 3.0, sem=sem, inc=16)
+
+    def store(q, name, lo, hi, src, sem):
+        return op(q, lambda e: [e.dma_start(out=T[name][:, lo:hi], in_=ap(src))], [src], [("out_" + name, lo, hi, 1, None)], 0.1, 3.0,
+                  sem=sem, inc=16)
+
+    nsent = [0]
+
+    def send(dst_rank, out, src, sem, lat=2.5, occ=0.8):
+        dst = T.cores[dst_rank % NC]
+        rid, pid = topo.addr(dst)[0], topo.addr(dst)[1]
+        mask = topo.mask(core, dst)
+        n = len(topo.engines(core, dst))
+        nsent[0] += n
+        k = op("G", lambda e: [e.remote_dma(ap(out), ap(src), T.sem[sem], T.sem.lsem, pid, rid, mask)], [src], [], occ, occ,
+               sem="lsem", inc=0)
+        return op("N", None, [], [out], 0.0, lat, sem=sem, inc=n, deps=(k,))
+
+    def send_columns(t):
+        send(rank - HOP * t, R("win%d" % t, 0, WX), R("win0", 0, WX), "w%d" % t, 7.0)
+
+    I, NIDN, ONE, BLK = R("idn", 0, 128), R("nidn", 0, 128), R("one", 0, 128), R("blk", 0, 128)
+    load("Y", R("win0", 0, W), "xt", "ld0")
+    load("S", R("tsx", 0, 256), "sl", "ld1")
+    load("S", R("tp", 0, 256), "pl", "ld2")
+    load("Y", R("wti", 0, 1), "wt", "ld3")
+    load("Y", R("thi", 0, 1), "th", "ld4")
+    load("S", R("tl", 0, 256), "ll", "ld5")
+    load("S", R("tq", 0, 256), "ql", "ld6")
+    load("Y", R("E0", 0, 128), "ed", "ld7")
+    vset(R("one", 0, 128), 1.0)
+    gsel(I, ONE, [[-1, 128]], OP.is_equal, 0, 1)
+    gsel(R("blk0", 0, 128), ONE, [[-16, 8], [0, 16]], OP.is_ge, 0, 1)
+    gsel(BLK, R("blk0", 0, 128), [[16, 8], [0, 16]], OP.is_ge, 15, -1)
+    vcopy(R("tcf", 0, 1), R("wti", 0, 1))
+    vts(R("tci", 0, 1), R("thi", 0, 1), -1, OP.add)
+    vts(R("tci", 4, 5), R("tci", 0, 1), 4, OP.arith_shift_right)
+    vts(R("tci", 8, 9), R("tci", 0, 1), 15, OP.bitwise_and)
+    vcopy(R("tcf", 4, 5), R("tci", 4, 5))
+    vcopy(R("tcf", 8, 9), R("tci", 8, 9))
+    vts(R("win0", W, W + 128), BLK, R("tcf", 0, 1), OP.mult)
+    vts(R("win0", W + 128, W + 256), I, R("tcf", 4, 5), OP.mult, -16.0 * BIG, OP.mult)
+    vts(R("win0", W + 256, W + 384), I, R("tcf", 8, 9), OP.mult, -BIG, OP.mult)
+    send_columns(1)
+    boost[0] = 0.0
+    vset(R("one", 128, 2048), 1.0)
+    op("G", lambda e: [e.iota(ap(R("kin", 0, 1)), [[0, 1]], 0, 1)], [], [R("kin", 0, 1)], 0.2)
+    gsel(R("Ind", 0, 2048, 1, (0, 64)), R("one", 0, 2048, 1, (0, 64)), [[-1, 64], [0, 32]], OP.is_equal, 0, 1)
+    if ASTAT:
+        P8 = (0, 8)
+        gsel(R("pr0", 0, 64), R("one", 0, 64), [[-2, 64]], OP.is_ge, 0, 1)
+        gsel(R("pr1", 0, 64), R("pr0", 0, 64), [[2, 64]], OP.is_ge, 1, -1)
+        vcopy(R("pair", 0, 64), R("pr1", 0, 64))
+        gsel(R("gr0", 0, 128, 1, P8), R("one", 0, 128, 1, P8), [[1, 128]], OP.is_ge, 0, -16)
+        gsel(R("gr1", 0, 128, 1, P8), R("gr0", 0, 128, 1, P8), [[-1, 128]], OP.is_ge, 15, 16)
+        vcopy(R("grp8", 0, 128, 1, P8), R("gr1", 0, 128, 1, P8))
+    if BSPLIT:
+        vcopy(R("idf", 0, 128), I)
+    vts(NIDN, I, -1.0, OP.mult)
+    vset(R("Bp", 0, 144), 0.0)
+    vset(R("Bn", 0, 144), 0.0)
+    vts(R("Bp", 15, 128, 16), R("blk", 0, 128, 16), BIG, OP.mult)
+    vts(R("Bn", 15, 128, 16), R("blk", 0, 128, 16), -BIG, OP.mult)
+    vts(R("blkP", 0, 128), BLK, BIG, OP.mult)
+    vts(R("blkN", 0, 128), BLK, -BIG, OP.mult)
+    vts(R("blk2", 0, 128), BLK, 2.0, OP.mult)
+    vset(R("o16", 0, 128), 0.0625)
+    vset(R("maskz", 0, CH), 1.0)
+    vset(R("maskz", 0, CH, 32), 0.0)
+    vset(R("emsg", 0, 12 * 80), 0.0)
+    vts(R("kin", 8, 9), R("kin", 0, 1), 15, OP.bitwise_and)
+    vts(R("k37", 0, 1), R("kin", 8, 9), 32.0 * 37.0, OP.mult)
+    vts(R("k37", 1, 2), R("kin", 8, 9), 32.0 * 37.0, OP.mult, 32.0 * 37.0 * 16.0, OP.add)
+
+    def Ln(k, X):
+        if k <= 0:
+            return R(("tp", "tsx", "tl")[k + 2], 128 * X, 128 * X + 128)
+        return R("Lnum", (k - 1) * 256 + 128 * X, (k - 1) * 256 + 128 * X + 128)
+
+    def Lu(k, X, h):
+        o = (k + 2) * 256 + 128 * X
+        return R("Loff", o, o + 128) if h is None else R("Loff", o + 64 * h, o + 64 * h + 64)
+
+    def Qu(t, X, h):
+        o = t * 256 + 128 * X
+        return R("Qoff", o, o + 128) if h is None else R("Qoff", o + 64 * h, o + 64 * h + 64)
+
+    def Qv(t, X):
+        return R("Qv", t * 256 + 128 * X, t * 256 + 128 * X + 128)
+
+    def L6(k, X):
+        return R("L6", (k + 2) * 256 + 128 * X, (k + 2) * 256 + 128 * X + 128)
+
+    def every(r, h):
+        return R(r[0], r[1] + h, r[2], 2)
+
+    for k, nm in ((-1, "tsx"), (-2, "tp"), (0, "tl")):
+        vcopy(R("Loff", (k + 2) * 256, (k + 2) * 256 + 256), R(nm, 0, 256))
+    vcopy(R("Qoff", 0, 256), R("tq", 0, 256))
+    vts(R("Qv", 0, 256), R("tq", 0, 256), 4096.0, OP.add)
+    for k, nm in ((-2, "tp"), (-1, "tsx"), (0, "tl")):
+        vts(R("L6", (k + 2) * 256, (k + 2) * 256 + 256), R(nm, 0, 256), 6144.0, OP.add)
+
+    def sums(out, parts, extra=()):
+        mm = []
+        for (coef, tile, base) in parts:
+            for i in range(16):
+                mm.append([out, R(coef, 15 - i, 143 - i), R(tile, base + i, base + 1024, 16)])
+        for (lt, rh) in extra:
+            mm.append([out, lt, rh])
+        return [(o, l, r, j == 0, j == len(mm) - 1) for j, (o, l, r) in enumerate(mm)]
+
+    for t in range(NV):
+        wn = "win%d" % t
+        WIN = R(wn, 0, W)
+        for X in range(2):
+            z, y, sl = (t % 2) * 2 + X, X, 2 * t + X
+
+            def F(nm):
+                o, n = FT[nm]
+                return R("tf", z * NF + o, z * NF + o + n)
+
+            def J(nm):
+                o, n = IT[nm]
+                return R("ti", z * NI + o, z * NI + o + n)
+
+            def tile(nm, q, h=None):
+                return R("%s%d" % (nm, q), 0, CH) if h is None else R("%s%d" % (nm, q), 1024 * h, 1024 * h + 1024)
+
+            E = R("E0", 64 * X, 64 * X + 64) if t == 0 else R("eland", (sl - 2) * 80, (sl - 2) * 80 + 64)
+            for h in range(2):
+                gath_s(tile("s", z, h), WIN, Lu(t - 1, X, h))
+            for h in range(2):
+                gath_sub(tile("dp", z, h), WIN, Lu(t - 2, X, h), tile("s", z, h))
+            vts(tile("ra", z), tile("dp", z), 0.0, OP.max, 2.0, OP.mult)
+            if ASTAT:
+                A1, A2 = R("ZB", 448, 456), R("ZB", 448, 512, 1, (0, 8))
+                mm = []
+                for k in range(16):
+                    mm.append((A1, R("ra%d" % z, k, CH, 16), R("blkP", 0, 128, 16), k == 0, False))
+                    mm.append((A1, R("dp%d" % z, k, CH, 16), R("blkN", 0, 128, 16), False, k == 15))
+                pe(mm)
+                act(F("As1"), A1, AF.Copy)
+                pe([(A2, F("As1"), R("pair", 0, 64), True, True)])
+                act(R(F("As2")[0], F("As2")[1], F("As2")[2], 1, (0, 8)), A2, AF.Copy)
+            pe([(R("MB", 0, 128, 1, (0, 64)), E, NIDN, True, True), (R("MB", 128, 192), R(wn, W, W + 128), E, True, True)])
+            ET = R("ETs", z * 128, z * 128 + 128, 1, (0, 64))
+            act(ET, R("MB", 0, 128, 1, (0, 64)), AF.Copy)
+            vcopy(J("ui"), R("MB", 128, 192))
+            vts(J("ua"), J("ui"), 2047, OP.bitwise_and)
+            U32, L4 = R("ZB", 128, 192), R("ZB", 192, 320)
+            vts(U32, J("ua"), 32.0, OP.add)
+            L = Ln(t, X)
+            for h in range(2):
+                vtt(every(F("LU"), h), every(L, h), U32, OP.mult)
+            vts(L4, L, 4096.0, OP.add)
+            vtt(F("LQ"), L4, Qv(t, X), OP.subtract)
+            for h in range(2):
+                gath_s(tile("l", y, h), WIN, Lu(t, X, h))
+            for h in range(2):
+                gath_sub(tile("dq", y, h), WIN, Qu(t, X, h), tile("s", z, h))
+            if (t, X) in DABS:
+                for h in range(2):
+                    act(tile("rq", y, h), tile("dq", y, h), AF.Abs)
+            else:
+                vts(tile("rq", y), tile("dq", y), 0.0, OP.max, 2.0, OP.mult)
+            op("V", lambda e, a=tile("sc", y), b=R("maskz", 0, CH), c=tile("l", y): [e.tensor_tensor_scan(
+                out=ap(a), data0=ap(b), data1=ap(c), initial=0.0, op0=OP.mult, op1=OP.max)],
+                [R("maskz", 0, CH), tile("l", y)], [tile("sc", y)], vcost(CH, 0.5))
+            M = R("mmsg", sl * 64, sl * 64 + 64)
+            act(M, R("sc%d" % y, 31, CH, 32), AF.Copy)
+            MR = R("mland", sl * 64, sl * 64 + 64)
+            send(rank + 4, MR, M, "m%d" % sl)
+            if X == 1 and t + 2 < NV:
+                send_columns(t + 2)
+            for h in range(2):
+                rb = "R%d" % h
+                mm = []
+                for j in range(2):
+                    o, c0 = R(rb, 512 * j, 512 * j + 512), 1024 * h + 512 * j
+                    mm.append((o, I, R("s%d" % z, c0, c0 + 512), True, False))
+                    mm.append((o, NIDN, R("l%d" % y, c0, c0 + 512), False, True))
+                pe(mm)
+                act(tile("vb", y, h), R(rb, 0, 1024), AF.Abs)
+            for h in range(2):
+                rb = "R%d" % h
+                mm = []
+                for j in range(2):
+                    o, c0 = R(rb, 512 * j, 512 * j + 512), 1024 * h + 512 * j
+                    mm.append((o, I, R("s%d" % z, c0, c0 + 512), True, False))
+                    mm.append((o, I, R("dp%d" % z, c0, c0 + 512), False, False))
+                    mm.append((o, NIDN, R("l%d" % y, c0, c0 + 512), False, True))
+                pe(mm)
+                act(tile("vc", y, h), R(rb, 0, 1024), AF.Abs)
+            for h in range(2):
+                rb = "R%d" % h
+                mm = []
+                for j in range(2):
+                    o, c0 = R(rb, 512 * j, 512 * j + 512), 1024 * h + 512 * j
+                    mm.append((o, I, R("l%d" % y, c0, c0 + 512), True, False))
+                    mm.append((o, ET, R("Ind", c0, c0 + 512, 1, (0, 64)), False, True))
+                pe(mm)
+                act(tile("vo", y, h), R(rb, 0, 1024), AF.Abs)
+            if BSPLIT:
+                for h in range(2):
+                    pe(sums(R("ZB", 320 + 64 * h, 384 + 64 * h), [("Bp", "vb%d" % y, 1024 * h)]))
+                act(F("Bsb"), R("ZB", 320, 448), AF.Copy)
+            for h in range(2):
+                q = [("Bn", "rq%d" % y, 1024 * h)] + ([] if (t, X) in DABS else [("Bp", "dq%d" % y, 1024 * h)])
+                bs = [(R("idf", 0, 128), R(F("Bsb")[0], F("Bsb")[1] + 64 * h, F("Bsb")[1] + 64 * h + 64))]
+                b = [("Bp", "vb%d" % y, 1024 * h)]
+                pe(sums(R("SB", 64 * h, 64 * h + 64), q + ([] if BSPLIT else b), bs if BSPLIT else ()))
+            for h in range(2):
+                bs = [(R("idf", 0, 128), R(F("Bsb")[0], F("Bsb")[1] + 64 * h, F("Bsb")[1] + 64 * h + 64))]
+                b = [("Bp", "vb%d" % y, 1024 * h)]
+                pe(sums(R("CB", 64 * h, 64 * h + 64), ([] if BSPLIT else b) + [("Bn", "vc%d" % y, 1024 * h)], bs if BSPLIT else ()))
+            act(F("Csb"), R("CB", 0, 128), AF.Copy)
+            Z = R("ZB", 0, 64)
+            zc = [(Z, R("blk2", 0, 128), every(F("Csb"), 0), False, False),
+                  (Z, R("blk2", 0, 128), every(F("Csb"), 1), False, True)]
+            if ASTAT:
+                zc[0] = zc[0][:3] + (True, False)
+                zc[1] = zc[1][:3] + (False, False)
+                zc.append((Z, R("grp8", 0, 128, 1, (0, 8)), R(F("As2")[0], F("As2")[1], F("As2")[2], 1, (0, 8)), False, True))
+            else:
+                mm = []
+                for k in range(32):
+                    mm.append((Z, R("blkP", 0, 128), R("ra%d" % z, k, CH, 32), k == 0, False))
+                    mm.append((Z, R("blkN", 0, 128), R("dp%d" % z, k, CH, 32), False, False))
+                pe(mm)
+            pe(zc)
+            for h in range(2):
+                pe(sums(R("SB", 128 + 64 * h, 192 + 64 * h), [("Bp", "vo%d" % y, 1024 * h)],
+                        [(R(wn, W + 128, W + 256), R("one", 0, 64)), (R(wn, W + 256, W + 384), R("one", 0, 64))]))
+            if t == 0:
+                colA = "k37"
+                cb = 0
+            else:
+                colA, cb = "af", t * 16 + 8
+                if X == 0:
+                    cn = R("MB", 192, 193)
+                    pe([(cn, R("o16", 0, 128), R("eland", (sl - 2) * 80 + 64, (sl - 2) * 80 + 65), True, False),
+                        (cn, R("o16", 0, 128), R("eland", (sl - 1) * 80 + 64, (sl - 1) * 80 + 65), False, True)])
+                    vcopy(R("ai", t * 16, t * 16 + 1), cn)
+                    vts(R("ai", t * 16 + 8, t * 16 + 9), R("ai", t * 16, t * 16 + 1), 31, OP.bitwise_and)
+                    vts(R("af", t * 16, t * 16 + 1), R("ai", t * 16 + 8, t * 16 + 9), 32.0, OP.mult)
+                    vts(R("af", t * 16 + 8, t * 16 + 10), R("k37", 0, 2), R("af", t * 16, t * 16 + 1), OP.add)
+            for h in range(2):
+                vts(every(J("LUi"), h), every(F("LU"), h), R(colA, cb + h, cb + h + 1), OP.add)
+            vts(J("CHi"), J("LUi"), 5, OP.arith_shift_right, 2047, OP.bitwise_and)
+            vts(F("CHp"), J("CHi"), 2048.0, OP.add)
+            pe([(R("MB", 256, 320), I, E, True, False), (R("MB", 256, 320), NIDN, MR, False, True),
+                (R("MB", 320, 384), I, E, True, False), (R("MB", 320, 384), I, MR, False, True)])
+            ABE, WE2 = R("MB", 384, 448), R("CB", 384, 448)
+            act(ABE, R("MB", 256, 320), AF.Abs)
+            vts(J("h"), R("MB", 320, 384), 0.5, OP.mult, -0.25, OP.add)
+            vtt(F("w"), ABE, J("h"), OP.subtract)
+            D, O, C = R("SB", 0, 128), R("SB", 128, 256), R("CB", 0, 128)
+            vtt(D, Qv(t, X), D, OP.min)
+            FAIL = R("ZB", 64, 128)
+            vts(FAIL, Z, 0.0, OP.is_gt)
+            for h in range(2):
+                vtt(every(F("PF"), h), every(L6(t - 2, X), h), FAIL, OP.mult)
+            vtt(C, F("PF"), C, OP.min)
+            vtt(F("r3"), L, D, OP.max)
+            vtt(F("r2"), F("r3"), C, OP.max)
+            vtt(O, F("CHp"), O, OP.min)
+            vtt(J("r1"), F("r2"), O, OP.max)
+            NEW = Ln(t + 1, X)
+            vts(NEW, J("r1"), 2047, OP.bitwise_and)
+            last = t == NV - 1
+            if not last:
+                vcopy(Lu(t + 1, X, None), NEW)
+                if t + 1 <= NV - 3:
+                    vts(L6(t + 1, X), NEW, 6144.0, OP.add)
+            q1, q2 = R("CB", 128, 256), R("CB", 256, 384)
+            vtt(q1, NEW, L, OP.not_equal)
+            vtt(q2, F("LQ"), q1, OP.mult)
+            if not last:
+                vtt(Qv(t + 1, X), Qv(t, X), q2, OP.add)
+                vts(Qu(t + 1, X, None), Qv(t + 1, X), -4096.0, OP.add)
+            EM = R("emsg", sl * 80, sl * 80 + 64)
+            vtt(WE2, F("w"), FAIL, OP.mult)
+            vtt(EM, J("h"), WE2, OP.add)
+            c8 = F("cnt")
+            if not last:
+                act(F("junk"), FAIL, AF.Copy, acc_out=R(c8[0], c8[1], c8[1] + 1))
+                act(R("emsg", sl * 80 + 64, sl * 80 + 65), R(c8[0], c8[1], c8[1] + 1), AF.Copy)
+            send(rank - HOP if not last else rank - 1, R("eland", sl * 80, sl * 80 + 72), R("emsg", sl * 80, sl * 80 + 72), "e%d" % sl)
+            if last:
+                q3 = R("tf", z * NF + FT["r2"][0], z * NF + FT["r2"][0] + 128)
+                vtt(q3, Qv(t, X), q2, OP.add)
+                vcopy(R("finLQ", 256 * X, 256 * X + 128), NEW)
+                vts(R("finLQ", 256 * X + 128, 256 * X + 256), q3, -4096.0, OP.add)
+                send(rank - 1, R("fLQ", 256 * X, 256 * X + 256), R("finLQ", 256 * X, 256 * X + 256), "fb" if X == 0 else "fc")
+                if X == 0:
+                    vcopy(R("finPS", 0, 256), R("Lnum", 3 * 256, 4 * 256))
+                    vcopy(R("finPS", 256, 512), R("Lnum", 4 * 256, 5 * 256))
+                    send(rank - 1, R("fPS", 0, 512), R("finPS", 0, 512), "fa")
+                    store("Y", "yp", 0, 256, R("fPS", 0, 256), "st0")
+                    store("Y", "ys", 0, 256, R("fPS", 256, 512), "st1")
+                store("Y", "yl", 128 * X, 128 * X + 128, R("fLQ", 256 * X, 256 * X + 128), "st%d" % (2 + 4 * X))
+                store("S", "yq", 128 * X, 128 * X + 128, R("fLQ", 256 * X + 128, 256 * X + 256), "st%d" % (3 + 4 * X))
+                store("Y", "ye", 64 * X, 64 * X + 64, R("eland", sl * 80, sl * 80 + 64), "st%d" % (4 + 4 * X))
+
+    n = len(ops)
+    succ = [[] for _ in range(n)]
+    for k in range(n):
+        for d in ops[k]["dep"]:
+            succ[d].append(k)
+    prio = [0.0] * n
+    for k in range(n - 1, -1, -1):
+        prio[k] = ops[k]["lat"] + max([prio[s] + 0.08 for s in succ[k]] + [0.0])
+    left = [len(ops[k]["dep"]) for k in range(n)]
+    rdy = [0.0] * n
+    free = {"V": 0.0, "S": 0.0, "P": 0.0, "G": 0.0, "Y": 0.0}
+    pool = {"V": [], "S": [], "P": [], "G": [], "Y": [], "N": []}
+    for k in range(n):
+        if left[k] == 0:
+            pool[ops[k]["eng"]].append(k)
+    order = []
+    while len(order) < n:
+        best = None
+        for e in pool:
+            if pool[e]:
+                m = min(rdy[k] for k in pool[e])
+                s = m if e == "N" else max(free[e], m)
+                if best is None or s < best[0]:
+                    best = (s, e)
+        s, e = best
+        k = max([k for k in pool[e] if rdy[k] <= s + 1e-9], key=lambda q: (prio[q] + ops[q]["boost"], -q))
+        pool[e].remove(k)
+        order.append(k)
+        if e != "N":
+            free[e] = s + ops[k]["occ"]
+        fin = s + ops[k]["lat"]
+        for q in succ[k]:
+            left[q] -= 1
+            rdy[q] = max(rdy[q], fin + 0.08)
+            if left[q] == 0:
+                pool[ops[q]["eng"]].append(q)
+
+    known = {e: {} for e in ENG}
+    count = {"sV": 0, "sS": 0, "sP": 0, "sG": 0}
+    event = [None] * n
+    snap = [None] * n
+    total = {}
+    pos = {k: i for i, k in enumerate(order)}
+    for k in order:
+        o = ops[k]
+        e = o["eng"]
+        if e == "N":
+            event[k] = (o["sem"], o["inc"])
+            total[o["sem"]] = o["inc"]
+            snap[k] = {}
+            continue
+        kn = known[e]
+        for d in sorted(o["dep"], key=lambda q: -pos[q]):
+            if event[d] is None:
+                continue
+            sm, v = event[d]
+            if kn.get(sm, 0) >= v:
+                continue
+            ENG[e].wait_ge(T.sem[sm], v)
+            kn[sm] = v
+            for a, b in snap[d].items():
+                if kn.get(a, 0) < b:
+                    kn[a] = b
+        ins = o["emit"](ENG[e])
+        if o["sem"] is None:
+            sm = ESEM[e]
+            for x in ins:
+                x.then_inc(T.sem[sm], 1)
+            count[sm] += len(ins)
+            event[k] = (sm, count[sm])
+            total[sm] = count[sm]
+        elif o["inc"]:
+            for x in ins:
+                x.then_inc(T.sem[o["sem"]], o["inc"])
+            event[k] = (o["sem"], o["inc"])
+            total[o["sem"]] = o["inc"]
+        snap[k] = dict(kn)
+    total["lsem"] = nsent[0]
+    for sm in total:
+        if known["G"].get(sm, 0) < total[sm]:
+            g.wait_ge(T.sem[sm], total[sm])

@@ -3,12 +3,13 @@ from concourse.mybir import AluOpType as OP, ActivationFunctionType as AF, AxisL
 
 NV, HOP, NC = 6, 3, 8
 W = 2048
-WX = W + 384
+WX = W + 128 + 16
 CH = 2048
-BIG = 8192.0
-DABS = {(t, 0) for t in range(5)}
-ASTAT, BSPLIT = True, True
-FIRST = {"s": -5.0, "l": -5.0, "dq": 5.0, "rq": -10.0, "vb": -5.0, "vc": -5.0, "vo": -10.0, "R": -10.0, "SB": -5.0, "MB": -5.0}
+BIG = 2.0 ** 19
+HUGE = 2.0 ** 50
+OFF = 2.0 ** 18
+KIND = {0: "AA", 1: "AA"}
+FIRST = {"Dn": -30.0, "eq": -30.0, "Rq": -30.0}
 
 FT = {}
 IT = {}
@@ -22,39 +23,40 @@ def _fields(d, items):
     return o
 
 
-NF = _fields(FT, [("LU", 128), ("CHp", 128), ("r3", 128), ("r2", 128), ("w", 64), ("PF", 128), ("LQ", 128),
-                  ("Csb", 128), ("Bsb", 128), ("As1", 8), ("As2", 64), ("junk", 64), ("cnt", 8)])
-NI = _fields(IT, [("ui", 64), ("ua", 64), ("LUi", 128), ("CHi", 128), ("r1", 128), ("h", 64)])
+NF = _fields(FT, [("LU", 128), ("CD", 256), ("Cb", 128), ("B1", 128), ("C2", 128), ("ABE", 64), ("y", 64)])
+NI = _fields(IT, [("CH", 128), ("r", 128), ("nh", 64)])
 
 SCRATCH = {
     "tp": ("sbuf", [128, 256], "int32"), "tsx": ("sbuf", [128, 256], "int32"),
     "tl": ("sbuf", [128, 256], "int32"), "tq": ("sbuf", [128, 256], "int32"),
     "Lnum": ("sbuf", [128, 6 * 256], "int32"), "Loff": ("sbuf", [128, 9 * 256], "uint16"),
-    "Qoff": ("sbuf", [128, 6 * 256], "uint16"), "Qv": ("sbuf", [128, 6 * 256], "float32"),
-    "L6": ("sbuf", [128, 6 * 256], "float32"),
+    "Vk": ("sbuf", [128, 8 * 256], "float32"),
+    "Dn": ("sbuf", [128, 6 * 256], "float16"), "eq": ("sbuf", [128, 6 * 256], "float16"),
+    "Rq": ("sbuf", [128, 6 * 256], "float16"),
     "finPS": ("sbuf", [128, 512], "float32"), "finLQ": ("sbuf", [128, 512], "float32"),
     "fPS": ("sbuf", [128, 512], "float32"), "fLQ": ("sbuf", [128, 512], "float32"),
     "tf": ("sbuf", [128, 4 * NF], "float32"), "ti": ("sbuf", [128, 4 * NI], "int32"),
     "E0": ("sbuf", [128, 128], "bfloat16"),
     "mmsg": ("sbuf", [128, 12 * 64], "bfloat16"), "mland": ("sbuf", [128, 12 * 64], "bfloat16"),
-    "emsg": ("sbuf", [128, 12 * 80], "bfloat16"), "eland": ("sbuf", [128, 12 * 80], "bfloat16"),
-    "idf": ("sbuf", [128, 128], "float32"), "grp8": ("sbuf", [128, 128], "float32"), "pair": ("sbuf", [128, 64], "float32"),
-    "pr0": ("sbuf", [128, 64], "bfloat16"), "pr1": ("sbuf", [128, 64], "bfloat16"),
-    "gr0": ("sbuf", [128, 128], "bfloat16"), "gr1": ("sbuf", [128, 128], "bfloat16"),
-    "ETs": ("sbuf", [128, 4 * 128], "bfloat16"),
+    "emsg": ("sbuf", [128, 12 * 128], "bfloat16"), "eland": ("sbuf", [128, 12 * 128], "bfloat16"),
+    "ETs": ("sbuf", [128, 4 * 128], "bfloat16"), "Js": ("sbuf", [128, 4 * 64], "bfloat16"),
     "Ind": ("sbuf", [128, 2048], "bfloat16"), "maskz": ("sbuf", [128, 2048], "bfloat16"),
     "one": ("sbuf", [128, 2048], "bfloat16"), "idn": ("sbuf", [128, 128], "bfloat16"),
-    "nidn": ("sbuf", [128, 128], "bfloat16"), "blk0": ("sbuf", [128, 128], "bfloat16"),
+    "nidn": ("sbuf", [128, 128], "bfloat16"), "kidn": ("sbuf", [128, 128], "bfloat16"),
+    "nkidn": ("sbuf", [128, 128], "bfloat16"), "uidn": ("sbuf", [128, 128], "bfloat16"),
+    "blk0": ("sbuf", [128, 128], "bfloat16"),
     "blk": ("sbuf", [128, 128], "bfloat16"), "blkP": ("sbuf", [128, 128], "bfloat16"),
     "blkN": ("sbuf", [128, 128], "bfloat16"), "blk2": ("sbuf", [128, 128], "float32"),
-    "Bp": ("sbuf", [128, 144], "bfloat16"), "Bn": ("sbuf", [128, 144], "bfloat16"),
-    "o16": ("sbuf", [128, 128], "bfloat16"),
+    "Bp": ("sbuf", [128, 144], "bfloat16"), "Bn": ("sbuf", [128, 144], "bfloat16"), "Be": ("sbuf", [128, 144], "bfloat16"),
+    "cz": ("sbuf", [128, 128], "bfloat16"), "cu": ("sbuf", [128, 128], "bfloat16"),
+    "cc": ("sbuf", [128, 128], "bfloat16"), "o32": ("sbuf", [128, 128], "bfloat16"),
     "kin": ("sbuf", [128, 16], "int32"), "k37": ("sbuf", [128, 8], "float32"),
     "wti": ("sbuf", [128, 8], "int32"), "thi": ("sbuf", [128, 8], "int32"),
     "tci": ("sbuf", [128, 16], "int32"), "tcf": ("sbuf", [128, 16], "float32"),
-    "ai": ("sbuf", [128, 6 * 16], "int32"), "af": ("sbuf", [128, 6 * 16], "float32"),
+    "ai": ("sbuf", [128, 6 * 8], "int32"), "af": ("sbuf", [128, 6 * 16], "float32"),
+    "junk": ("sbuf", [128, 64], "bfloat16"),
     "R0": ("psum", [128, 1024], "float32"), "R1": ("psum", [128, 1024], "float32"),
-    "SB": ("psum", [128, 512], "float32"), "CB": ("psum", [128, 512], "float32"),
+    "SB": ("psum", [128, 512], "float32"), "VB": ("psum", [128, 512], "float32"),
     "ZB": ("psum", [128, 512], "float32"), "MB": ("psum", [128, 512], "float32"),
 }
 for _t in range(NV):
@@ -70,8 +72,8 @@ SEMAPHORES = (["sV", "sS", "sP", "sG", "lsem", "fa", "fb", "fc"] + ["w%d" % t fo
               + ["m%d" % i for i in range(12)] + ["e%d" % i for i in range(12)]
               + ["ld%d" % i for i in range(9)] + ["st%d" % i for i in range(10)])
 
-CYC = 0.83e-3 * 1.2
-PEC = 0.417e-3 * 1.2
+CYC = 0.83e-3 * 1.15
+PEC = 0.417e-3 * 1.15
 GAM = 1.5
 
 
@@ -81,7 +83,7 @@ def rank_program(g, core, T, topo):
         return
     ENG = {"V": g.vector, "S": g.scalar, "P": g.tensor, "G": g, "Y": g.sync}
     ESEM = {"V": "sV", "S": "sS", "P": "sP", "G": "sG"}
-    PSUM = ("R0", "R1", "SB", "CB", "ZB", "MB")
+    PSUM = ("R0", "R1", "SB", "VB", "ZB", "MB")
     ops = []
     acc = {}
     boost = [1000.0]
@@ -134,7 +136,7 @@ def rank_program(g, core, T, topo):
         return k
 
     def vcost(n, f=1.0):
-        return 0.06 + max(64, n * f) * CYC
+        return 0.05 + max(64, n * f) * CYC
 
     def two(*rs):
         for r in rs:
@@ -163,20 +165,30 @@ def rank_program(g, core, T, topo):
     def vset(out, c):
         return op("V", lambda e: [e.memset(ap(out), c)], [], [out], vcost(n_of(out), two(out)))
 
-    def act(out, a, func, scale=1.0, acc_out=None):
+    def vscan(out, a, b, op0, op1):
+        return op("V", lambda e: [e.tensor_tensor_scan(out=ap(out), data0=ap(a), data1=ap(b), initial=0.0, op0=op0, op1=op1)],
+                  [a, b], [out], vcost(n_of(out), two(out, a, b)))
+
+    def act(out, a, func, scale=None, bias=None, acc_out=None):
         def em(e):
+            kw = {}
+            if scale is not None:
+                kw["scale"] = scale
+            if bias is not None:
+                kw["bias"] = ap(bias) if isinstance(bias, tuple) else bias
             if acc_out is not None:
-                return [e.activation(out=ap(out), in_=ap(a), func=func, accum_out=ap(acc_out))]
-            return [e.activation(out=ap(out), in_=ap(a), func=func)]
-        return op("S", em, [a], [out] + ([acc_out] if acc_out else []), 0.08 + max(64, n_of(out)) * CYC)
+                kw["accum_out"] = ap(acc_out)
+            return [e.activation(out=ap(out), in_=ap(a), func=func, **kw)]
+        return op("S", em, [a] + ([bias] if isinstance(bias, tuple) else []), [out] + ([acc_out] if acc_out else []),
+                  0.065 + max(64, n_of(out)) * CYC)
 
     def gath_s(out, win, off):
         return op("S", lambda e: [e.activation(out=ap(out), in_=ap(win).indirect(ap(off)), func=AF.Copy)], [win, off], [out],
-                  0.08 + n_of(out) * GAM * CYC)
+                  0.065 + n_of(out) * GAM * CYC)
 
     def gath_sub(out, win, off, b):
         return op("V", lambda e: [e.tensor_tensor(out=ap(out), in0=ap(win).indirect(ap(off)), in1=ap(b), op=OP.subtract)],
-                  [win, off, b], [out], 0.06 + n_of(out) * GAM * CYC)
+                  [win, off, b], [out], 0.05 + n_of(out) * GAM * CYC)
 
     def pe(mms):
         rd, wr, cost = [], [], 0.0
@@ -198,7 +210,10 @@ def rank_program(g, core, T, topo):
                 rd2[key] = (key, min(rd2[key][1], x[1]), max(rd2[key][2], x[2]), 1, None)
             else:
                 rd2[key] = x
-        return op("P", em, list(rd2.values()), wr, cost + 0.03, cost + 0.1)
+        return op("P", em, list(rd2.values()), wr, cost + 0.01, cost + 0.1)
+
+    def group(out, terms):
+        return [(out, l, r, j == 0, j == len(terms) - 1) for j, (l, r) in enumerate(terms)]
 
     def gsel(out, a, pattern, cmp, base, cm):
         return op("G", lambda e: [e.affine_select(out=ap(out), in_=ap(a), pattern=pattern, compare_op=cmp, fill=0.0, base=base,
@@ -214,7 +229,7 @@ def rank_program(g, core, T, topo):
 
     nsent = [0]
 
-    def send(dst_rank, out, src, sem, lat=2.5, occ=0.8):
+    def send(dst_rank, out, src, sem, lat=2.5, occ=0.7):
         dst = T.cores[dst_rank % NC]
         rid, pid = topo.addr(dst)[0], topo.addr(dst)[1]
         mask = topo.mask(core, dst)
@@ -227,7 +242,8 @@ def rank_program(g, core, T, topo):
     def send_columns(t):
         send(rank - HOP * t, R("win%d" % t, 0, WX), R("win0", 0, WX), "w%d" % t, 7.0)
 
-    I, NIDN, ONE, BLK = R("idn", 0, 128), R("nidn", 0, 128), R("one", 0, 128), R("blk", 0, 128)
+    I, NIDN, KI, NKI = R("idn", 0, 128), R("nidn", 0, 128), R("kidn", 0, 128), R("nkidn", 0, 128)
+    ONE, BLK, ONE64 = R("one", 0, 128), R("blk", 0, 128), R("one", 0, 64)
     load("Y", R("win0", 0, W), "xt", "ld0")
     load("S", R("tsx", 0, 256), "sl", "ld1")
     load("S", R("tp", 0, 256), "pl", "ld2")
@@ -237,269 +253,271 @@ def rank_program(g, core, T, topo):
     load("S", R("tq", 0, 256), "ql", "ld6")
     load("Y", R("E0", 0, 128), "ed", "ld7")
     vset(R("one", 0, 128), 1.0)
-    gsel(I, ONE, [[-1, 128]], OP.is_equal, 0, 1)
+    vset(R("win0", W + 128, WX), 0.0)
     gsel(R("blk0", 0, 128), ONE, [[-16, 8], [0, 16]], OP.is_ge, 0, 1)
     gsel(BLK, R("blk0", 0, 128), [[16, 8], [0, 16]], OP.is_ge, 15, -1)
+    gsel(I, ONE, [[-1, 128]], OP.is_equal, 0, 1)
     vcopy(R("tcf", 0, 1), R("wti", 0, 1))
     vts(R("tci", 0, 1), R("thi", 0, 1), -1, OP.add)
     vts(R("tci", 4, 5), R("tci", 0, 1), 4, OP.arith_shift_right)
     vts(R("tci", 8, 9), R("tci", 0, 1), 15, OP.bitwise_and)
-    vcopy(R("tcf", 4, 5), R("tci", 4, 5))
-    vcopy(R("tcf", 8, 9), R("tci", 8, 9))
+    vts(R("win0", W + 128, W + 129), R("tci", 4, 5), -16.0 * BIG, OP.mult)
+    vts(R("win0", W + 129, W + 130), R("tci", 8, 9), -BIG, OP.mult)
     vts(R("win0", W, W + 128), BLK, R("tcf", 0, 1), OP.mult)
-    vts(R("win0", W + 128, W + 256), I, R("tcf", 4, 5), OP.mult, -16.0 * BIG, OP.mult)
-    vts(R("win0", W + 256, W + 384), I, R("tcf", 8, 9), OP.mult, -BIG, OP.mult)
     send_columns(1)
     boost[0] = 0.0
     vset(R("one", 128, 2048), 1.0)
     op("G", lambda e: [e.iota(ap(R("kin", 0, 1)), [[0, 1]], 0, 1)], [], [R("kin", 0, 1)], 0.2)
     gsel(R("Ind", 0, 2048, 1, (0, 64)), R("one", 0, 2048, 1, (0, 64)), [[-1, 64], [0, 32]], OP.is_equal, 0, 1)
-    if ASTAT:
-        P8 = (0, 8)
-        gsel(R("pr0", 0, 64), R("one", 0, 64), [[-2, 64]], OP.is_ge, 0, 1)
-        gsel(R("pr1", 0, 64), R("pr0", 0, 64), [[2, 64]], OP.is_ge, 1, -1)
-        vcopy(R("pair", 0, 64), R("pr1", 0, 64))
-        gsel(R("gr0", 0, 128, 1, P8), R("one", 0, 128, 1, P8), [[1, 128]], OP.is_ge, 0, -16)
-        gsel(R("gr1", 0, 128, 1, P8), R("gr0", 0, 128, 1, P8), [[-1, 128]], OP.is_ge, 15, 16)
-        vcopy(R("grp8", 0, 128, 1, P8), R("gr1", 0, 128, 1, P8))
-    if BSPLIT:
-        vcopy(R("idf", 0, 128), I)
     vts(NIDN, I, -1.0, OP.mult)
-    vset(R("Bp", 0, 144), 0.0)
-    vset(R("Bn", 0, 144), 0.0)
-    vts(R("Bp", 15, 128, 16), R("blk", 0, 128, 16), BIG, OP.mult)
-    vts(R("Bn", 15, 128, 16), R("blk", 0, 128, 16), -BIG, OP.mult)
+    vts(KI, I, HUGE, OP.mult)
+    vts(NKI, I, -HUGE, OP.mult)
+    vts(R("uidn", 0, 128), I, -2048.0, OP.mult)
+    for nm, c in (("Bp", BIG), ("Bn", -BIG), ("Be", BIG / HUGE)):
+        vset(R(nm, 0, 144), 0.0)
+        vts(R(nm, 15, 128, 16), R("blk", 0, 128, 16), c, OP.mult)
     vts(R("blkP", 0, 128), BLK, BIG, OP.mult)
     vts(R("blkN", 0, 128), BLK, -BIG, OP.mult)
     vts(R("blk2", 0, 128), BLK, 2.0, OP.mult)
-    vset(R("o16", 0, 128), 0.0625)
+    vset(R("cz", 0, 128), -BIG / 512.0)
+    vset(R("cu", 0, 128, 1, (0, 64)), 129.0 * 32.0)
+    vset(R("cu", 0, 128, 1, (64, 128)), 0.5)
+    vset(R("o32", 0, 128), 1.0 / 32.0)
+    vset(R("cc", 0, 128), -15.5 / 8192.0)
     vset(R("maskz", 0, CH), 1.0)
     vset(R("maskz", 0, CH, 32), 0.0)
-    vset(R("emsg", 0, 12 * 80), 0.0)
     vts(R("kin", 8, 9), R("kin", 0, 1), 15, OP.bitwise_and)
-    vts(R("k37", 0, 1), R("kin", 8, 9), 32.0 * 37.0, OP.mult)
-    vts(R("k37", 1, 2), R("kin", 8, 9), 32.0 * 37.0, OP.mult, 32.0 * 37.0 * 16.0, OP.add)
+    for h in range(2):
+        c = 37.0 * 16 * h + 2048.0 - 31.0 / 64.0
+        vts(R("k37", h, h + 1), R("kin", 8, 9), 37.0, OP.mult, c, OP.add)
+        vts(R("k37", 2 + h, 3 + h), R("kin", 8, 9), 37.0, OP.mult, c + 15.5, OP.add)
 
     def Ln(k, X):
         if k <= 0:
-            return R(("tp", "tsx", "tl")[k + 2], 128 * X, 128 * X + 128)
+            return R(("tq", "tp", "tsx", "tl")[k + 3], 128 * X, 128 * X + 128)
         return R("Lnum", (k - 1) * 256 + 128 * X, (k - 1) * 256 + 128 * X + 128)
 
-    def Lu(k, X, h):
-        o = (k + 2) * 256 + 128 * X
+    def Lu(k, X, h=None):
+        o = (k + 3) * 256 + 128 * X
         return R("Loff", o, o + 128) if h is None else R("Loff", o + 64 * h, o + 64 * h + 64)
 
-    def Qu(t, X, h):
-        o = t * 256 + 128 * X
-        return R("Qoff", o, o + 128) if h is None else R("Qoff", o + 64 * h, o + 64 * h + 64)
+    def Vk(k, X):
+        return R("Vk", (k + 3) * 256 + 128 * X, (k + 3) * 256 + 128 * X + 128)
 
-    def Qv(t, X):
-        return R("Qv", t * 256 + 128 * X, t * 256 + 128 * X + 128)
+    def voff(k):
+        return OFF + 2048.0 * (8 - (k if k > -3 else -1))
 
-    def L6(k, X):
-        return R("L6", (k + 2) * 256 + 128 * X, (k + 2) * 256 + 128 * X + 128)
+    def slot(b, X, j):
+        return R(b, 768 * X + j, 768 * X + 768, 6)
 
     def every(r, h):
         return R(r[0], r[1] + h, r[2], 2)
 
-    for k, nm in ((-1, "tsx"), (-2, "tp"), (0, "tl")):
-        vcopy(R("Loff", (k + 2) * 256, (k + 2) * 256 + 256), R(nm, 0, 256))
-    vcopy(R("Qoff", 0, 256), R("tq", 0, 256))
-    vts(R("Qv", 0, 256), R("tq", 0, 256), 4096.0, OP.add)
-    for k, nm in ((-2, "tp"), (-1, "tsx"), (0, "tl")):
-        vts(R("L6", (k + 2) * 256, (k + 2) * 256 + 256), R(nm, 0, 256), 6144.0, OP.add)
+    for X in range(2):
+        for k in (-1, -2, 0, -3):
+            vcopy(Lu(k, X), Ln(k, X))
+        for k in (-2, -3, -1, 0):
+            vts(Vk(k, X), Ln(k, X), voff(k), OP.add)
+        vtt(slot("Dn", X, 0), Ln(-3, X), Ln(0, X), OP.subtract)
 
-    def sums(out, parts, extra=()):
+    def sums(out, parts):
+        pe(group(out, [(R(coef, 15 - i, 143 - i), R(tile[0], tile[1] + i, tile[2], 16)) for (coef, tile) in parts for i in range(16)]))
+
+    nreg = [0]
+
+    def size(out, terms):
+        rb = "R%d" % (nreg[0] % 2)
+        nreg[0] += 1
         mm = []
-        for (coef, tile, base) in parts:
-            for i in range(16):
-                mm.append([out, R(coef, 15 - i, 143 - i), R(tile, base + i, base + 1024, 16)])
-        for (lt, rh) in extra:
-            mm.append([out, lt, rh])
-        return [(o, l, r, j == 0, j == len(mm) - 1) for j, (o, l, r) in enumerate(mm)]
+        for j in range(2):
+            mm += group(R(rb, 512 * j, 512 * j + 512), [(l, R(r[0], r[1] + 512 * j, r[1] + 512 * j + 512, 1, r[4])) for (l, r) in terms])
+        pe(mm)
+        act(out, R(rb, 0, 1024), AF.Abs)
+
+    def relu2(out, a):
+        vts(out, a, 0.0, OP.max, 2.0, OP.mult)
 
     for t in range(NV):
         wn = "win%d" % t
         WIN = R(wn, 0, W)
+        last = t == NV - 1
+        TH = R("af", t * 16 + 12, t * 16 + 13)
+        vts(TH, R(wn, W + 128, W + 129), R(wn, W + 129, W + 130), OP.add)
         for X in range(2):
             z, y, sl = (t % 2) * 2 + X, X, 2 * t + X
+            kind = "SS" if t == 0 else KIND[X]
 
-            def F(nm):
+            def F(nm, lo=0, hi=None):
                 o, n = FT[nm]
-                return R("tf", z * NF + o, z * NF + o + n)
+                return R("tf", z * NF + o + lo, z * NF + o + (n if hi is None else hi))
 
             def J(nm):
                 o, n = IT[nm]
                 return R("ti", z * NI + o, z * NI + o + n)
 
-            def tile(nm, q, h=None):
-                return R("%s%d" % (nm, q), 0, CH) if h is None else R("%s%d" % (nm, q), 1024 * h, 1024 * h + 1024)
+            def tile(nm, h):
+                q = z if nm in ("s", "dp", "ra") else y
+                return R("%s%d" % (nm, q), 1024 * h, 1024 * h + 1024)
 
-            E = R("E0", 64 * X, 64 * X + 64) if t == 0 else R("eland", (sl - 2) * 80, (sl - 2) * 80 + 64)
-            for h in range(2):
-                gath_s(tile("s", z, h), WIN, Lu(t - 1, X, h))
-            for h in range(2):
-                gath_sub(tile("dp", z, h), WIN, Lu(t - 2, X, h), tile("s", z, h))
-            vts(tile("ra", z), tile("dp", z), 0.0, OP.max, 2.0, OP.mult)
-            if ASTAT:
-                A1, A2 = R("ZB", 448, 456), R("ZB", 448, 512, 1, (0, 8))
-                mm = []
-                for k in range(16):
-                    mm.append((A1, R("ra%d" % z, k, CH, 16), R("blkP", 0, 128, 16), k == 0, False))
-                    mm.append((A1, R("dp%d" % z, k, CH, 16), R("blkN", 0, 128, 16), False, k == 15))
-                pe(mm)
-                act(F("As1"), A1, AF.Copy)
-                pe([(A2, F("As1"), R("pair", 0, 64), True, True)])
-                act(R(F("As2")[0], F("As2")[1], F("As2")[2], 1, (0, 8)), A2, AF.Copy)
-            pe([(R("MB", 0, 128, 1, (0, 64)), E, NIDN, True, True), (R("MB", 128, 192), R(wn, W, W + 128), E, True, True)])
-            ET = R("ETs", z * 128, z * 128 + 128, 1, (0, 64))
-            act(ET, R("MB", 0, 128, 1, (0, 64)), AF.Copy)
-            vcopy(J("ui"), R("MB", 128, 192))
-            vts(J("ua"), J("ui"), 2047, OP.bitwise_and)
-            U32, L4 = R("ZB", 128, 192), R("ZB", 192, 320)
-            vts(U32, J("ua"), 32.0, OP.add)
+            E = R("E0", 64 * X, 64 * X + 64) if t == 0 else R("eland", (sl - 2) * 128, (sl - 2) * 128 + 64)
             L = Ln(t, X)
             for h in range(2):
-                vtt(every(F("LU"), h), every(L, h), U32, OP.mult)
-            vts(L4, L, 4096.0, OP.add)
-            vtt(F("LQ"), L4, Qv(t, X), OP.subtract)
+                if kind[h] == "S":
+                    gath_s(tile("s", h), WIN, Lu(t - 1, X, h))
+                    gath_sub(tile("dp", h), WIN, Lu(t - 2, X, h), tile("s", h))
+                    relu2(tile("ra", h), tile("dp", h))
+                    if t == 0:
+                        gath_sub(tile("dq", h), WIN, Lu(-3, X, h), tile("s", h))
+                        relu2(tile("rq", h), tile("dq", h))
             for h in range(2):
-                gath_s(tile("l", y, h), WIN, Lu(t, X, h))
-            for h in range(2):
-                gath_sub(tile("dq", y, h), WIN, Qu(t, X, h), tile("s", z, h))
-            if (t, X) in DABS:
-                for h in range(2):
-                    act(tile("rq", y, h), tile("dq", y, h), AF.Abs)
-            else:
-                vts(tile("rq", y), tile("dq", y), 0.0, OP.max, 2.0, OP.mult)
-            op("V", lambda e, a=tile("sc", y), b=R("maskz", 0, CH), c=tile("l", y): [e.tensor_tensor_scan(
-                out=ap(a), data0=ap(b), data1=ap(c), initial=0.0, op0=OP.mult, op1=OP.max)],
-                [R("maskz", 0, CH), tile("l", y)], [tile("sc", y)], vcost(CH, 0.5))
+                gath_s(tile("l", h), WIN, Lu(t, X, h))
+                if kind[h] != "S":
+                    gath_sub(tile("s", h), WIN, Lu(t - 1, X, h), tile("l", h))
+                    gath_sub(tile("dp", h), WIN, Lu(t - 2, X, h), tile("l", h))
+                if kind[h] == "L":
+                    relu2(tile("vc", h), tile("dp", h))
+                if kind[h] == "A":
+                    act(tile("vc", h), tile("dp", h), AF.Abs)
+            vscan(R("sc%d" % y, 0, CH), R("maskz", 0, CH), R("l%d" % y, 0, CH), OP.mult, OP.max)
             M = R("mmsg", sl * 64, sl * 64 + 64)
             act(M, R("sc%d" % y, 31, CH, 32), AF.Copy)
             MR = R("mland", sl * 64, sl * 64 + 64)
             send(rank + 4, MR, M, "m%d" % sl)
             if X == 1 and t + 2 < NV:
                 send_columns(t + 2)
-            for h in range(2):
-                rb = "R%d" % h
-                mm = []
-                for j in range(2):
-                    o, c0 = R(rb, 512 * j, 512 * j + 512), 1024 * h + 512 * j
-                    mm.append((o, I, R("s%d" % z, c0, c0 + 512), True, False))
-                    mm.append((o, NIDN, R("l%d" % y, c0, c0 + 512), False, True))
-                pe(mm)
-                act(tile("vb", y, h), R(rb, 0, 1024), AF.Abs)
-            for h in range(2):
-                rb = "R%d" % h
-                mm = []
-                for j in range(2):
-                    o, c0 = R(rb, 512 * j, 512 * j + 512), 1024 * h + 512 * j
-                    mm.append((o, I, R("s%d" % z, c0, c0 + 512), True, False))
-                    mm.append((o, I, R("dp%d" % z, c0, c0 + 512), False, False))
-                    mm.append((o, NIDN, R("l%d" % y, c0, c0 + 512), False, True))
-                pe(mm)
-                act(tile("vc", y, h), R(rb, 0, 1024), AF.Abs)
-            for h in range(2):
-                rb = "R%d" % h
-                mm = []
-                for j in range(2):
-                    o, c0 = R(rb, 512 * j, 512 * j + 512), 1024 * h + 512 * j
-                    mm.append((o, I, R("l%d" % y, c0, c0 + 512), True, False))
-                    mm.append((o, ET, R("Ind", c0, c0 + 512, 1, (0, 64)), False, True))
-                pe(mm)
-                act(tile("vo", y, h), R(rb, 0, 1024), AF.Abs)
-            if BSPLIT:
-                for h in range(2):
-                    pe(sums(R("ZB", 320 + 64 * h, 384 + 64 * h), [("Bp", "vb%d" % y, 1024 * h)]))
-                act(F("Bsb"), R("ZB", 320, 448), AF.Copy)
-            for h in range(2):
-                q = [("Bn", "rq%d" % y, 1024 * h)] + ([] if (t, X) in DABS else [("Bp", "dq%d" % y, 1024 * h)])
-                bs = [(R("idf", 0, 128), R(F("Bsb")[0], F("Bsb")[1] + 64 * h, F("Bsb")[1] + 64 * h + 64))]
-                b = [("Bp", "vb%d" % y, 1024 * h)]
-                pe(sums(R("SB", 64 * h, 64 * h + 64), q + ([] if BSPLIT else b), bs if BSPLIT else ()))
-            for h in range(2):
-                bs = [(R("idf", 0, 128), R(F("Bsb")[0], F("Bsb")[1] + 64 * h, F("Bsb")[1] + 64 * h + 64))]
-                b = [("Bp", "vb%d" % y, 1024 * h)]
-                pe(sums(R("CB", 64 * h, 64 * h + 64), ([] if BSPLIT else b) + [("Bn", "vc%d" % y, 1024 * h)], bs if BSPLIT else ()))
-            act(F("Csb"), R("CB", 0, 128), AF.Copy)
-            Z = R("ZB", 0, 64)
-            zc = [(Z, R("blk2", 0, 128), every(F("Csb"), 0), False, False),
-                  (Z, R("blk2", 0, 128), every(F("Csb"), 1), False, True)]
-            if ASTAT:
-                zc[0] = zc[0][:3] + (True, False)
-                zc[1] = zc[1][:3] + (False, False)
-                zc.append((Z, R("grp8", 0, 128, 1, (0, 8)), R(F("As2")[0], F("As2")[1], F("As2")[2], 1, (0, 8)), False, True))
-            else:
-                mm = []
-                for k in range(32):
-                    mm.append((Z, R("blkP", 0, 128), R("ra%d" % z, k, CH, 32), k == 0, False))
-                    mm.append((Z, R("blkN", 0, 128), R("dp%d" % z, k, CH, 32), False, False))
-                pe(mm)
-            pe(zc)
-            for h in range(2):
-                pe(sums(R("SB", 128 + 64 * h, 192 + 64 * h), [("Bp", "vo%d" % y, 1024 * h)],
-                        [(R(wn, W + 128, W + 256), R("one", 0, 64)), (R(wn, W + 256, W + 384), R("one", 0, 64))]))
+            WM = R(wn, W, W + 128)
+            pe(group(R("MB", 0, 128, 1, (0, 64)), [(E, NIDN)]) + group(R("MB", 128, 192), [(WM, E)]))
+            ET = R("ETs", z * 128, z * 128 + 128, 1, (0, 64))
+            JU = R("Js", z * 64, z * 64 + 64)
+            act(ET, R("MB", 0, 128, 1, (0, 64)), AF.Copy)
+            act(JU, R("MB", 128, 192), AF.Identity, 1.0 / 2048.0, 129.0 - 1023.5 / 2048.0)
+            U = R("MB", 192, 320)
+            pe(sum([group(every(U, h), [(WM, E), (R("uidn", 0, 128), JU), (R("cu", 0, 128), ONE64)]) for h in range(2)], []))
+            vtt(F("LU"), L, U, OP.mult)
             if t == 0:
-                colA = "k37"
-                cb = 0
+                colA = R("k37", 0, 2)
             else:
-                colA, cb = "af", t * 16 + 8
+                colA = R("af", t * 16 + 8, t * 16 + 10)
                 if X == 0:
-                    cn = R("MB", 192, 193)
-                    pe([(cn, R("o16", 0, 128), R("eland", (sl - 2) * 80 + 64, (sl - 2) * 80 + 65), True, False),
-                        (cn, R("o16", 0, 128), R("eland", (sl - 1) * 80 + 64, (sl - 1) * 80 + 65), False, True)])
-                    vcopy(R("ai", t * 16, t * 16 + 1), cn)
-                    vts(R("ai", t * 16 + 8, t * 16 + 9), R("ai", t * 16, t * 16 + 1), 31, OP.bitwise_and)
-                    vts(R("af", t * 16, t * 16 + 1), R("ai", t * 16 + 8, t * 16 + 9), 32.0, OP.mult)
-                    vts(R("af", t * 16 + 8, t * 16 + 10), R("k37", 0, 2), R("af", t * 16, t * 16 + 1), OP.add)
+                    cn, xa = R("MB", 448, 512), R("af", t * 16, t * 16 + 1)
+                    pe(group(cn, [(R("o32", 0, 128), R("eland", (sl - 2) * 128 + 64, (sl - 2) * 128 + 128)),
+                                  (R("o32", 0, 128), R("eland", (sl - 1) * 128 + 64, (sl - 1) * 128 + 128)),
+                                  (R("cc", 0, 128), ONE64)]))
+                    act(R("junk", 0, 64), cn, AF.Copy, acc_out=xa)
+                    vts(R("ai", t * 8, t * 8 + 1), xa, 1.0 / 32.0, OP.mult)
+                    vts(R("af", t * 16 + 4, t * 16 + 5), R("ai", t * 8, t * 8 + 1), -32.0, OP.mult, xa, OP.add)
+                    vts(colA, R("k37", 2, 4), R("af", t * 16 + 4, t * 16 + 5), OP.add)
             for h in range(2):
-                vts(every(J("LUi"), h), every(F("LU"), h), R(colA, cb + h, cb + h + 1), OP.add)
-            vts(J("CHi"), J("LUi"), 5, OP.arith_shift_right, 2047, OP.bitwise_and)
-            vts(F("CHp"), J("CHi"), 2048.0, OP.add)
-            pe([(R("MB", 256, 320), I, E, True, False), (R("MB", 256, 320), NIDN, MR, False, True),
-                (R("MB", 320, 384), I, E, True, False), (R("MB", 320, 384), I, MR, False, True)])
-            ABE, WE2 = R("MB", 384, 448), R("CB", 384, 448)
-            act(ABE, R("MB", 256, 320), AF.Abs)
-            vts(J("h"), R("MB", 320, 384), 0.5, OP.mult, -0.25, OP.add)
-            vtt(F("w"), ABE, J("h"), OP.subtract)
-            D, O, C = R("SB", 0, 128), R("SB", 128, 256), R("CB", 0, 128)
-            vtt(D, Qv(t, X), D, OP.min)
-            FAIL = R("ZB", 64, 128)
-            vts(FAIL, Z, 0.0, OP.is_gt)
+                vts(every(J("CH"), h), every(F("LU"), h), 1.0 / 32.0, OP.mult, R(colA[0], colA[1] + h, colA[1] + h + 1), OP.add)
+            pe(group(R("MB", 320, 384), [(I, E), (NIDN, MR)]) + group(R("MB", 384, 448), [(I, E), (I, MR)]))
+            act(F("ABE"), R("MB", 320, 384), AF.Abs)
+            vts(J("nh"), R("MB", 384, 448), -0.5, OP.mult, 0.25, OP.add)
+            Z = R("ZB", 0, 64)
+            B, C, D, O = [R("SB", 128 * j, 128 * j + 128) for j in range(4)]
+
+            def part(r, h):
+                return R(r[0], r[1] + 64 * h, r[1] + 64 * h + 64)
+
+            zopen = [True]
+
+            def page_sums(h, parts):
+                zo = R("ZB", 32 * h, 32 * h + 32)
+                mm = []
+                if zopen[0]:
+                    mm.append((Z, R("cz", 0, 128), ONE64, True, False))
+                    zopen[0] = False
+                for (coef, tl) in parts:
+                    for k in range(16):
+                        for hh in range(2):
+                            mm.append((zo, R(coef, 0, 128), R(tl[0], tl[1] + 16 * hh + k, tl[2], 32), False, False))
+                pe(mm)
+
+            def page_sums2(parts):
+                mm = [(Z, R("cz", 0, 128), ONE64, True, False)]
+                for (coef, nm) in parts:
+                    for k in range(32):
+                        mm.append((Z, R(coef, 0, 128), R(tile(nm, 0)[0], k, CH, 32), False, False))
+                pe(mm)
+
             for h in range(2):
-                vtt(every(F("PF"), h), every(L6(t - 2, X), h), FAIL, OP.mult)
-            vtt(C, F("PF"), C, OP.min)
-            vtt(F("r3"), L, D, OP.max)
-            vtt(F("r2"), F("r3"), C, OP.max)
-            vtt(O, F("CHp"), O, OP.min)
-            vtt(J("r1"), F("r2"), O, OP.max)
+                ind = R("Ind", 1024 * h, 1024 * h + 1024, 1, (0, 64))
+                if kind[h] == "S":
+                    size(tile("vc", h), [(I, tile("s", h)), (I, tile("dp", h)), (NIDN, tile("l", h))])
+                    if t == 0:
+                        size(tile("vo", h), [(I, tile("l", h)), (ET, ind)])
+                        size(tile("vb", h), [(I, tile("s", h)), (NIDN, tile("l", h))])
+                    else:
+                        size(tile("vb", h), [(KI, tile("s", h)), (NKI, tile("l", h)), (I, tile("l", h)), (ET, ind)])
+                else:
+                    size(tile("ra", h), [(I, tile("dp", h)), (NIDN, tile("s", h))])
+                    size(tile("vb", h), [(KI, tile("s", h)), (I, tile("l", h)), (ET, ind)])
+            if kind == "SS":
+                page_sums2([("blkP", "ra"), ("blkN", "dp")])
+            elif "S" not in kind:
+                page_sums2([("blkP", "ra")])
+            else:
+                page_sums2([("blkP", "ra")])
+                hs = kind.index("S")
+                pe([(R("ZB", 32 * hs, 32 * hs + 32), R("blkN", 0, 128), R(tile("dp", 0)[0], 1024 * hs + k, 1024 * hs + 1024, 32), False, False)
+                    for k in range(32)])
+            bc = "Bp" if t == 0 else "Be"
+            if t == 0:
+                for h in range(2):
+                    sums(part(D, h), [("Bp", tile("rq", h)), ("Bn", tile("dq", h))])
+            sums(part(C, 0), [("Bp", tile("vc", 0))] + ([("Bn", tile("dp", 0))] if kind[0] == "L" else []))
+            if t == 0:
+                sums(part(O, 0), [("Bp", tile("vo", 0))])
+            sums(part(B, 0), [(bc, tile("vb", 0))])
+            sums(part(C, 1), [("Bp", tile("vc", 1))] + ([("Bn", tile("dp", 1))] if kind[1] == "L" else []))
+            if t == 0:
+                act(F("CD"), R("SB", 128, 384), AF.Copy)
+                sums(part(O, 1), [("Bp", tile("vo", 1))])
+                act(O, O, AF.Identity, None, TH)
+            else:
+                act(F("CD", 0, 128), C, AF.Copy)
+            sums(part(B, 1), [(bc, tile("vb", 1))])
+            vtt(F("Cb"), B, F("CD", 0, 128), OP.subtract)
+            pe([(Z, R("blk2", 0, 128), every(F("Cb"), 0), False, False), (Z, R("blk2", 0, 128), every(F("Cb"), 1), False, True)])
+            GA, PB, XC = R("VB", 128 * X, 128 * X + 128), R("VB", 256, 384), R("VB", 384, 448)
+            if t == 0:
+                vtt(PB, B, F("CD", 128, 256), OP.subtract)
+                vtt(F("B1"), Vk(-3, X), PB, OP.min)
+            else:
+                vtt(F("B1"), Vk(t - 1, X), B, OP.min)
+                act(O, B, AF.Identity, HUGE, TH)
+            vtt(GA, J("CH"), O, OP.min)
+            vtt(GA, L, GA, OP.max)
+            vtt(GA, F("B1"), GA, OP.max)
+            for h in range(2):
+                vtt(every(PB, h), every(Vk(t - 2, X), h), Z, OP.min)
+            vtt(F("C2"), F("Cb"), PB, OP.min)
+            vtt(J("r"), F("C2"), GA, OP.max)
             NEW = Ln(t + 1, X)
-            vts(NEW, J("r1"), 2047, OP.bitwise_and)
-            last = t == NV - 1
+            vts(NEW, J("r"), 2047, OP.bitwise_and)
             if not last:
-                vcopy(Lu(t + 1, X, None), NEW)
-                if t + 1 <= NV - 3:
-                    vts(L6(t + 1, X), NEW, 6144.0, OP.add)
-            q1, q2 = R("CB", 128, 256), R("CB", 256, 384)
-            vtt(q1, NEW, L, OP.not_equal)
-            vtt(q2, F("LQ"), q1, OP.mult)
+                vcopy(Lu(t + 1, X), NEW)
+            EM = R("emsg", sl * 128, sl * 128 + 64)
+            vtt(XC, F("ABE"), Z, OP.min)
+            vtt(F("y"), J("nh"), XC, OP.max)
             if not last:
-                vtt(Qv(t + 1, X), Qv(t, X), q2, OP.add)
-                vts(Qu(t + 1, X, None), Qv(t + 1, X), -4096.0, OP.add)
-            EM = R("emsg", sl * 80, sl * 80 + 64)
-            vtt(WE2, F("w"), FAIL, OP.mult)
-            vtt(EM, J("h"), WE2, OP.add)
-            c8 = F("cnt")
+                act(R("emsg", sl * 128 + 64, sl * 128 + 128), Z, AF.Sign)
+            act(EM, F("y"), AF.Abs)
+            ne = 64 if last else 128
+            send(rank - HOP if not last else rank - 1, R("eland", sl * 128, sl * 128 + ne), R("emsg", sl * 128, sl * 128 + ne), "e%d" % sl)
+            if t + 1 <= NV - 2:
+                vts(Vk(t + 1, X), NEW, voff(t + 1), OP.add)
             if not last:
-                act(F("junk"), FAIL, AF.Copy, acc_out=R(c8[0], c8[1], c8[1] + 1))
-                act(R("emsg", sl * 80 + 64, sl * 80 + 65), R(c8[0], c8[1], c8[1] + 1), AF.Copy)
-            send(rank - HOP if not last else rank - 1, R("eland", sl * 80, sl * 80 + 72), R("emsg", sl * 80, sl * 80 + 72), "e%d" % sl)
+                vtt(slot("Dn", X, t + 1), L, NEW, OP.subtract)
+            if t == NV - 2:
+                a, b = 768 * X, 768 * X + 768
+                vts(R("eq", a, b), R("Dn", a, b), 0.0, OP.is_equal)
+                vset(slot("eq", X, 0), 0.0)
+                vscan(R("Rq", a, b), R("eq", a, b), R("Dn", a, b), OP.mult, OP.add)
             if last:
-                q3 = R("tf", z * NF + FT["r2"][0], z * NF + FT["r2"][0] + 128)
-                vtt(q3, Qv(t, X), q2, OP.add)
                 vcopy(R("finLQ", 256 * X, 256 * X + 128), NEW)
-                vts(R("finLQ", 256 * X + 128, 256 * X + 256), q3, -4096.0, OP.add)
+                vtt(PB, NEW, L, OP.is_equal)
+                vtt(PB, slot("Rq", X, 5), PB, OP.mult)
+                vtt(R("finLQ", 256 * X + 128, 256 * X + 256), L, PB, OP.add)
                 send(rank - 1, R("fLQ", 256 * X, 256 * X + 256), R("finLQ", 256 * X, 256 * X + 256), "fb" if X == 0 else "fc")
                 if X == 0:
                     vcopy(R("finPS", 0, 256), R("Lnum", 3 * 256, 4 * 256))
@@ -509,7 +527,7 @@ def rank_program(g, core, T, topo):
                     store("Y", "ys", 0, 256, R("fPS", 256, 512), "st1")
                 store("Y", "yl", 128 * X, 128 * X + 128, R("fLQ", 256 * X, 256 * X + 128), "st%d" % (2 + 4 * X))
                 store("S", "yq", 128 * X, 128 * X + 128, R("fLQ", 256 * X + 128, 256 * X + 256), "st%d" % (3 + 4 * X))
-                store("Y", "ye", 64 * X, 64 * X + 64, R("eland", sl * 80, sl * 80 + 64), "st%d" % (4 + 4 * X))
+                store("Y", "ye", 64 * X, 64 * X + 64, R("eland", sl * 128, sl * 128 + 64), "st%d" % (4 + 4 * X))
 
     n = len(ops)
     succ = [[] for _ in range(n)]

@@ -9,7 +9,7 @@ BIG = 2.0 ** 19
 HUGE = 2.0 ** 50
 OFF = 2.0 ** 18
 KIND = {0: "AA", 1: "AA"}
-FIRST = {"Dn": -30.0, "eq": -30.0, "Rq": -30.0}
+FIRST = {}
 
 FT = {}
 IT = {}
@@ -33,8 +33,9 @@ SCRATCH = {
     "Vk": ("sbuf", [128, 8 * 256], "float32"),
     "Dn": ("sbuf", [128, 6 * 256], "float16"), "eq": ("sbuf", [128, 6 * 256], "float16"),
     "Rq": ("sbuf", [128, 6 * 256], "float16"),
-    "finPS": ("sbuf", [128, 512], "float32"), "finLQ": ("sbuf", [128, 512], "float32"),
-    "fPS": ("sbuf", [128, 512], "float32"), "fLQ": ("sbuf", [128, 512], "float32"),
+    "fin": ("sbuf", [128, 1024], "float32"),
+    "LoffB": ("sbuf", [128, 512], "uint16"), "VkB": ("sbuf", [128, 512], "float32"), "L5": ("sbuf", [128, 256], "int32"),
+    "R5": ("sbuf", [128, 256], "float16"), "R5B": ("sbuf", [128, 256], "float16"),
     "tf": ("sbuf", [128, 4 * NF], "float32"), "ti": ("sbuf", [128, 4 * NI], "int32"),
     "E0": ("sbuf", [128, 128], "bfloat16"),
     "mmsg": ("sbuf", [128, 12 * 64], "bfloat16"), "mland": ("sbuf", [128, 12 * 64], "bfloat16"),
@@ -59,7 +60,7 @@ SCRATCH = {
     "SB": ("psum", [128, 512], "float32"), "VB": ("psum", [128, 512], "float32"),
     "ZB": ("psum", [128, 512], "float32"), "MB": ("psum", [128, 512], "float32"),
 }
-for _t in range(NV):
+for _t in range(NV - 1):
     SCRATCH["win%d" % _t] = ("sbuf", [128, WX], "bfloat16")
 for _z in range(4):
     for _n in ("s", "dp", "ra"):
@@ -68,13 +69,18 @@ for _z in range(2):
     for _n in ("l", "dq", "rq", "vb", "vc", "vo", "sc"):
         SCRATCH["%s%d" % (_n, _z)] = ("sbuf", [128, CH], "bfloat16")
 
-SEMAPHORES = (["sV", "sS", "sP", "sG", "lsem", "fa", "fb", "fc"] + ["w%d" % t for t in range(1, NV)]
+SEMAPHORES = (["sV", "sS", "sP", "sG", "lsem"] + ["w%d" % t for t in range(1, NV - 1)]
               + ["m%d" % i for i in range(12)] + ["e%d" % i for i in range(12)]
-              + ["ld%d" % i for i in range(9)] + ["st%d" % i for i in range(10)])
+              + ["ld%d" % i for i in range(12)] + ["mu", "mv", "ml0", "ml1", "mr0", "mr1"] + ["st%d" % i for i in range(10)])
 
 CYC = 0.83e-3 * 1.15
 PEC = 0.417e-3 * 1.15
 GAM = 1.5
+WAKE = 0.08
+SWEEPS = 150
+SEED, SHAKE = 1, 1.5
+CASES = [(0.9, 0.75, 1.0, 0.06), (0.9, 1.0, 1.5, 0.15), (1.0, 1.3, 1.0, 0.08), (1.25, 1.0, 1.2, 0.1)]
+KEPT = {}
 
 
 def rank_program(g, core, T, topo):
@@ -112,18 +118,14 @@ def rank_program(g, core, T, topo):
     def op(eng, emit, rd, wr, occ, lat=None, sem=None, inc=0, deps=()):
         k = len(ops)
         dep = set(deps)
+        banks = set()
         for w, regs in ((False, rd), (True, wr)):
             for r in regs:
                 lst = acc.setdefault(r[0], [])
-                psb = r[0] in PSUM
+                if r[0] in PSUM:
+                    banks.update((r[0], b) for b in range(r[1] // 512, (r[2] - 1) // 512 + 1))
                 for (k2, r2, w2) in lst:
-                    if k2 == k:
-                        continue
-                    if psb and ops[k2]["eng"] != eng:
-                        if r[1] // 512 <= (r2[2] - 1) // 512 and r2[1] // 512 <= (r[2] - 1) // 512:
-                            dep.add(k2)
-                            continue
-                    if (w or w2) and overlap(r, r2):
+                    if k2 != k and (w or w2) and overlap(r, r2):
                         dep.add(k2)
         for w, regs in ((False, rd), (True, wr)):
             for r in regs:
@@ -131,7 +133,7 @@ def rank_program(g, core, T, topo):
                 if w and r[3] == 1 and r[0] not in PSUM:
                     lst[:] = [x for x in lst if x[0] == k or not (x[1][1] >= r[1] and x[1][2] <= r[2])]
                 lst.append((k, r, w))
-        ops.append({"eng": eng, "emit": emit, "dep": dep, "occ": occ, "lat": occ + 0.03 if lat is None else lat,
+        ops.append({"eng": eng, "wr": wr, "banks": sorted(banks), "emit": emit, "dep": dep, "occ": occ, "lat": occ + 0.03 if lat is None else lat,
                     "sem": sem, "inc": inc, "boost": boost[0] + FIRST.get((wr[0][0] if wr else "-").rstrip("0123456789"), 0.0)})
         return k
 
@@ -183,12 +185,14 @@ def rank_program(g, core, T, topo):
                   0.065 + max(64, n_of(out)) * CYC)
 
     def gath_s(out, win, off):
-        return op("S", lambda e: [e.activation(out=ap(out), in_=ap(win).indirect(ap(off)), func=AF.Copy)], [win, off], [out],
-                  0.065 + n_of(out) * GAM * CYC)
+        k = op("S", lambda e: [e.activation(out=ap(out), in_=ap(win).indirect(ap(off)), func=AF.Copy)], [win, off], [out],
+               0.065 + n_of(out) * GAM * CYC)
+        ops[k]["gather"] = True
 
     def gath_sub(out, win, off, b):
-        return op("V", lambda e: [e.tensor_tensor(out=ap(out), in0=ap(win).indirect(ap(off)), in1=ap(b), op=OP.subtract)],
-                  [win, off, b], [out], 0.05 + n_of(out) * GAM * CYC)
+        k = op("V", lambda e: [e.tensor_tensor(out=ap(out), in0=ap(win).indirect(ap(off)), in1=ap(b), op=OP.subtract)],
+               [win, off, b], [out], 0.05 + n_of(out) * GAM * CYC)
+        ops[k]["gather"] = True
 
     def pe(mms):
         rd, wr, cost = [], [], 0.0
@@ -219,9 +223,13 @@ def rank_program(g, core, T, topo):
         return op("G", lambda e: [e.affine_select(out=ap(out), in_=ap(a), pattern=pattern, compare_op=cmp, fill=0.0, base=base,
                                                   channel_multiplier=cm)], [a], [out], 0.2 + 2 * n_of(out) * CYC)
 
-    def load(q, out, name, sem):
-        occ = 0.1
-        return op(q, lambda e: [e.dma_start(out=ap(out), in_=T[name][:])], [], [out], occ, 3.0, sem=sem, inc=16)
+    loads = []
+
+    def load(q, out, name, lat):
+        src = T[name][:] if n_of(out) == T[name].shape[1] else T[name][:, out[1]:out[2]]
+        k = op(q, lambda e: [e.dma_start(out=ap(out), in_=src)], [], [out], 0.05, lat, sem="ld%d" % len(loads), inc=16)
+        ops[k]["first"] = len(loads)
+        loads.append(k)
 
     def store(q, name, lo, hi, src, sem):
         return op(q, lambda e: [e.dma_start(out=T[name][:, lo:hi], in_=ap(src))], [src], [("out_" + name, lo, hi, 1, None)], 0.1, 3.0,
@@ -229,29 +237,31 @@ def rank_program(g, core, T, topo):
 
     nsent = [0]
 
-    def send(dst_rank, out, src, sem, lat=2.5, occ=0.7):
+    def send(dst_rank, out, src, sem, lat=2.5, occ=0.7, bulk=False, deps=()):
         dst = T.cores[dst_rank % NC]
         rid, pid = topo.addr(dst)[0], topo.addr(dst)[1]
-        mask = topo.mask(core, dst)
-        n = len(topo.engines(core, dst))
+        en = topo.engines(core, dst)
+        n = len(en) // 2
+        mask = sum(1 << q for q in (en[:n] if bulk else en[n:2 * n]))
         nsent[0] += n
         k = op("G", lambda e: [e.remote_dma(ap(out), ap(src), T.sem[sem], T.sem.lsem, pid, rid, mask)], [src], [], occ, occ,
-               sem="lsem", inc=0)
+               sem="lsem", inc=0, deps=deps)
         return op("N", None, [], [out], 0.0, lat, sem=sem, inc=n, deps=(k,))
 
-    def send_columns(t):
-        send(rank - HOP * t, R("win%d" % t, 0, WX), R("win0", 0, WX), "w%d" % t, 7.0)
+    def send_columns(t, deps=()):
+        send(rank - HOP * t, R("win%d" % t, 0, WX), R("win0", 0, WX), "w%d" % t, 8.0, bulk=True, deps=deps)
 
     I, NIDN, KI, NKI = R("idn", 0, 128), R("nidn", 0, 128), R("kidn", 0, 128), R("nkidn", 0, 128)
     ONE, BLK, ONE64 = R("one", 0, 128), R("blk", 0, 128), R("one", 0, 64)
-    load("Y", R("win0", 0, W), "xt", "ld0")
-    load("S", R("tsx", 0, 256), "sl", "ld1")
-    load("S", R("tp", 0, 256), "pl", "ld2")
-    load("Y", R("wti", 0, 1), "wt", "ld3")
-    load("Y", R("thi", 0, 1), "th", "ld4")
-    load("S", R("tl", 0, 256), "ll", "ld5")
-    load("S", R("tq", 0, 256), "ql", "ld6")
-    load("Y", R("E0", 0, 128), "ed", "ld7")
+    load("S", R("tsx", 0, 128), "sl", 2.2)
+    load("Y", R("win0", 0, W), "xt", 4.5)
+    for j, (b, nm) in enumerate((("tp", "pl"), ("tl", "ll"), ("tq", "ql"))):
+        load("Y", R(b, 0, 128), nm, 5.0 + 0.4 * j)
+    load("Y", R("wti", 0, 1), "wt", 6.1)
+    load("Y", R("thi", 0, 1), "th", 6.3)
+    load("Y", R("E0", 0, 128), "ed", 6.6)
+    for j, (b, nm) in enumerate((("tsx", "sl"), ("tp", "pl"), ("tl", "ll"), ("tq", "ql"))):
+        load("Y", R(b, 128, 256), nm, 7.0 + 0.4 * j)
     vset(R("one", 0, 128), 1.0)
     vset(R("win0", W + 128, WX), 0.0)
     gsel(R("blk0", 0, 128), ONE, [[-16, 8], [0, 16]], OP.is_ge, 0, 1)
@@ -292,17 +302,20 @@ def rank_program(g, core, T, topo):
         vts(R("k37", h, h + 1), R("kin", 8, 9), 37.0, OP.mult, c, OP.add)
         vts(R("k37", 2 + h, 3 + h), R("kin", 8, 9), 37.0, OP.mult, c + 15.5, OP.add)
 
+    moved = [False]
+
     def Ln(k, X):
         if k <= 0:
             return R(("tq", "tp", "tsx", "tl")[k + 3], 128 * X, 128 * X + 128)
         return R("Lnum", (k - 1) * 256 + 128 * X, (k - 1) * 256 + 128 * X + 128)
 
     def Lu(k, X, h=None):
-        o = (k + 3) * 256 + 128 * X
-        return R("Loff", o, o + 128) if h is None else R("Loff", o + 64 * h, o + 64 * h + 64)
+        b, o = ("LoffB", (k - 3) * 256 + 128 * X) if moved[0] and k < NV - 1 else ("Loff", (k + 3) * 256 + 128 * X)
+        return R(b, o, o + 128) if h is None else R(b, o + 64 * h, o + 64 * h + 64)
 
     def Vk(k, X):
-        return R("Vk", (k + 3) * 256 + 128 * X, (k + 3) * 256 + 128 * X + 128)
+        b, o = ("VkB", (k - 3) * 256 + 128 * X) if moved[0] else ("Vk", (k + 3) * 256 + 128 * X)
+        return R(b, o, o + 128)
 
     def voff(k):
         return OFF + 2048.0 * (8 - (k if k > -3 else -1))
@@ -338,14 +351,16 @@ def rank_program(g, core, T, topo):
         vts(out, a, 0.0, OP.max, 2.0, OP.mult)
 
     for t in range(NV):
-        wn = "win%d" % t
-        WIN = R(wn, 0, W)
         last = t == NV - 1
-        TH = R("af", t * 16 + 12, t * 16 + 13)
-        vts(TH, R(wn, W + 128, W + 129), R(wn, W + 129, W + 130), OP.add)
+        moved[0] = last
+        wn = "win%d" % (0 if last else t)
+        WIN = R(wn, 0, W)
+        TH = R("af", 12, 13) if last else R("af", t * 16 + 12, t * 16 + 13)
+        if not last:
+            vts(TH, R(wn, W + 128, W + 129), R(wn, W + 129, W + 130), OP.add)
         for X in range(2):
             z, y, sl = (t % 2) * 2 + X, X, 2 * t + X
-            kind = "SS" if t == 0 else KIND[X]
+            kind = "SS" if t == 0 else KIND.get((t, X), KIND[X])
 
             def F(nm, lo=0, hi=None):
                 o, n = FT[nm]
@@ -380,11 +395,11 @@ def rank_program(g, core, T, topo):
                     act(tile("vc", h), tile("dp", h), AF.Abs)
             vscan(R("sc%d" % y, 0, CH), R("maskz", 0, CH), R("l%d" % y, 0, CH), OP.mult, OP.max)
             M = R("mmsg", sl * 64, sl * 64 + 64)
-            act(M, R("sc%d" % y, 31, CH, 32), AF.Copy)
+            gsel(M, R("sc%d" % y, 31, CH, 32), [[0, 64]], OP.is_ge, 0, 0)
             MR = R("mland", sl * 64, sl * 64 + 64)
-            send(rank + 4, MR, M, "m%d" % sl)
-            if X == 1 and t + 2 < NV:
-                send_columns(t + 2)
+            km = send(rank + 4, MR, M, "m%d" % sl)
+            if X == 0 and t + 2 < NV - 1:
+                send_columns(t + 2, (km - 1,))
             WM = R(wn, W, W + 128)
             pe(group(R("MB", 0, 128, 1, (0, 64)), [(E, NIDN)]) + group(R("MB", 128, 192), [(WM, E)]))
             ET = R("ETs", z * 128, z * 128 + 128, 1, (0, 64))
@@ -492,42 +507,50 @@ def rank_program(g, core, T, topo):
                 vtt(every(PB, h), every(Vk(t - 2, X), h), Z, OP.min)
             vtt(F("C2"), F("Cb"), PB, OP.min)
             vtt(J("r"), F("C2"), GA, OP.max)
-            NEW = Ln(t + 1, X)
+            move = t == NV - 2
+            home = rank + HOP * (NV - 1)
+            NEW = R("L5", 128 * X, 128 * X + 128) if move else Ln(t + 1, X)
             vts(NEW, J("r"), 2047, OP.bitwise_and)
+            if move:
+                send(home, Ln(t + 1, X), NEW, "ml%d" % X)
             if not last:
-                vcopy(Lu(t + 1, X), NEW)
+                vcopy(Lu(t + 1, X), Ln(t + 1, X))
             EM = R("emsg", sl * 128, sl * 128 + 64)
             vtt(XC, F("ABE"), Z, OP.min)
             vtt(F("y"), J("nh"), XC, OP.max)
             if not last:
                 act(R("emsg", sl * 128 + 64, sl * 128 + 128), Z, AF.Sign)
             act(EM, F("y"), AF.Abs)
-            ne = 64 if last else 128
-            send(rank - HOP if not last else rank - 1, R("eland", sl * 128, sl * 128 + ne), R("emsg", sl * 128, sl * 128 + ne), "e%d" % sl)
+            if not last:
+                send(rank + HOP * t if move else rank - HOP, R("eland", sl * 128, sl * 128 + 128), R("emsg", sl * 128, sl * 128 + 128),
+                     "e%d" % sl)
             if t + 1 <= NV - 2:
                 vts(Vk(t + 1, X), NEW, voff(t + 1), OP.add)
+            if t == NV - 3 and X == 1:
+                send(home, R("LoffB", 0, 512), R("Loff", (t + 3) * 256, (t + 5) * 256), "mu", 3.5, bulk=True)
+                send(home, R("VkB", 0, 512), R("Vk", (t + 3) * 256, (t + 5) * 256), "mv", 4.5, bulk=True)
+                act(R("fin", 0, 256), R("VkB", 256, 512), AF.Identity, None, -voff(t + 1))
+                store("Y", "yp", 0, 256, R("fin", 0, 256), "st0")
             if not last:
                 vtt(slot("Dn", X, t + 1), L, NEW, OP.subtract)
-            if t == NV - 2:
+            if move:
                 a, b = 768 * X, 768 * X + 768
                 vts(R("eq", a, b), R("Dn", a, b), 0.0, OP.is_equal)
                 vset(slot("eq", X, 0), 0.0)
                 vscan(R("Rq", a, b), R("eq", a, b), R("Dn", a, b), OP.mult, OP.add)
+                vcopy(R("R5", 128 * X, 128 * X + 128), slot("Rq", X, 5))
+                send(home, R("R5B", 128 * X, 128 * X + 128), R("R5", 128 * X, 128 * X + 128), "mr%d" % X)
+                vcopy(R("fin", 256 + 128 * X, 384 + 128 * X), Ln(t + 1, X))
+                store("Y", "ys", 128 * X, 128 * X + 128, R("fin", 256 + 128 * X, 384 + 128 * X), "st%d" % (1 + 4 * X))
             if last:
-                vcopy(R("finLQ", 256 * X, 256 * X + 128), NEW)
+                FL, FQ = R("fin", 512 + 128 * X, 640 + 128 * X), R("fin", 768 + 128 * X, 896 + 128 * X)
+                vcopy(FL, NEW)
                 vtt(PB, NEW, L, OP.is_equal)
-                vtt(PB, slot("Rq", X, 5), PB, OP.mult)
-                vtt(R("finLQ", 256 * X + 128, 256 * X + 256), L, PB, OP.add)
-                send(rank - 1, R("fLQ", 256 * X, 256 * X + 256), R("finLQ", 256 * X, 256 * X + 256), "fb" if X == 0 else "fc")
-                if X == 0:
-                    vcopy(R("finPS", 0, 256), R("Lnum", 3 * 256, 4 * 256))
-                    vcopy(R("finPS", 256, 512), R("Lnum", 4 * 256, 5 * 256))
-                    send(rank - 1, R("fPS", 0, 512), R("finPS", 0, 512), "fa")
-                    store("Y", "yp", 0, 256, R("fPS", 0, 256), "st0")
-                    store("Y", "ys", 0, 256, R("fPS", 256, 512), "st1")
-                store("Y", "yl", 128 * X, 128 * X + 128, R("fLQ", 256 * X, 256 * X + 128), "st%d" % (2 + 4 * X))
-                store("S", "yq", 128 * X, 128 * X + 128, R("fLQ", 256 * X + 128, 256 * X + 256), "st%d" % (3 + 4 * X))
-                store("Y", "ye", 64 * X, 64 * X + 64, R("eland", sl * 128, sl * 128 + 64), "st%d" % (4 + 4 * X))
+                vtt(PB, R("R5B", 128 * X, 128 * X + 128), PB, OP.mult)
+                vtt(FQ, L, PB, OP.add)
+                store("Y", "yl", 128 * X, 128 * X + 128, FL, "st%d" % (2 + 4 * X))
+                store("S", "yq", 128 * X, 128 * X + 128, FQ, "st%d" % (3 + 4 * X))
+                store("Y", "ye", 64 * X, 64 * X + 64, EM, "st%d" % (4 + 4 * X))
 
     n = len(ops)
     succ = [[] for _ in range(n)]
@@ -537,34 +560,89 @@ def rank_program(g, core, T, topo):
     prio = [0.0] * n
     for k in range(n - 1, -1, -1):
         prio[k] = ops[k]["lat"] + max([prio[s] + 0.08 for s in succ[k]] + [0.0])
-    left = [len(ops[k]["dep"]) for k in range(n)]
-    rdy = [0.0] * n
-    free = {"V": 0.0, "S": 0.0, "P": 0.0, "G": 0.0, "Y": 0.0}
-    pool = {"V": [], "S": [], "P": [], "G": [], "Y": [], "N": []}
-    for k in range(n):
-        if left[k] == 0:
-            pool[ops[k]["eng"]].append(k)
-    order = []
-    while len(order) < n:
+
+    def place(key, back):
+        before = succ if back else [list(o["dep"]) for o in ops]
+        at = [0.0] * n
+        used = {e: [] for e in ENG}
+        held = {}
+        after = [list(o["dep"]) for o in ops] if back else succ
+        left = [len(x) for x in before]
+        ready = [k for k in range(n) if not left[k]]
+        while ready:
+            k = min(ready, key=lambda q: key[q] if back or "first" not in ops[q] else (-1e9, q))
+            ready.remove(k)
+            for q in after[k]:
+                left[q] -= 1
+                if not left[q]:
+                    ready.append(q)
+            o = ops[k]
+            if back:
+                s = max([at[q] + ops[q]["occ"] + WAKE for q in before[k]] + [-0.0]) + o["lat"] - o["occ"]
+            else:
+                s = max([at[q] + ops[q]["lat"] + WAKE for q in before[k]] + [0.0])
+            if o["eng"] != "N":
+                u = used[o["eng"]]
+                lo, hi = (o["occ"] - o["lat"] - WAKE, o["occ"]) if back else (0.0, o["lat"] + WAKE)
+                while True:
+                    j = len(u)
+                    while j > 0 and u[j - 1][1] > s:
+                        j -= 1
+                    while j < len(u) and u[j][0] < s + o["occ"] - 1e-9:
+                        s = max(s, u[j][1])
+                        j += 1
+                    clash = [x[1] for b in o["banks"] for x in held.setdefault(b, [])
+                             if x[2] != o["eng"] and x[1] > s + lo + 1e-9 and x[0] < s + hi - 1e-9]
+                    if not clash:
+                        break
+                    s = max(clash) - lo
+                u.insert(j, (s, s + o["occ"]))
+                for b in o["banks"]:
+                    held[b].append((s + lo, s + hi, o["eng"]))
+            at[k] = s
+        return at
+
+    def replay(order, f, gam, dma, wake):
+        fin = [0.0] * n
+        free = {e: 0.0 for e in ENG}
+        lastuse = {}
+        for k in order:
+            o = ops[k]
+            e = o["eng"]
+            s = max([fin[q] + wake for q in o["dep"]] + [free.get(e, 0.0)])
+            for b in o["banks"]:
+                lu = lastuse.setdefault(b, {})
+                s = max([s] + [fin[q] + wake for x, q in lu.items() if x != e])
+                lu[e] = k
+            c = dma if o["sem"] else f * (gam if o.get("gather") else 1.0)
+            if e != "N":
+                free[e] = s + o["occ"] * c
+            fin[k] = s + o["lat"] * c
+        return max(fin)
+
+    if "order" not in KEPT:
+        key = [(-prio[k] - ops[k]["boost"], k) for k in range(n)]
         best = None
-        for e in pool:
-            if pool[e]:
-                m = min(rdy[k] for k in pool[e])
-                s = m if e == "N" else max(free[e], m)
-                if best is None or s < best[0]:
-                    best = (s, e)
-        s, e = best
-        k = max([k for k in pool[e] if rdy[k] <= s + 1e-9], key=lambda q: (prio[q] + ops[q]["boost"], -q))
-        pool[e].remove(k)
-        order.append(k)
-        if e != "N":
-            free[e] = s + ops[k]["occ"]
-        fin = s + ops[k]["lat"]
-        for q in succ[k]:
-            left[q] -= 1
-            rdy[q] = max(rdy[q], fin + 0.08)
-            if left[q] == 0:
-                pool[ops[q]["eng"]].append(q)
+        rng = np.random.default_rng(SEED)
+        for sweep in range(SWEEPS):
+            at = place(key, False)
+            order = sorted(range(n), key=lambda q: (at[q], q))
+            end = sum(replay(order, *c) / c[0] for c in CASES) / len(CASES)
+            if best is None or end < best[0]:
+                best = (end, at)
+            shake = rng.random(n) * SHAKE
+            bk = place([(-best[1][k] + float(shake[k]), -k) for k in range(n)], True)
+            key = [(-(bk[k] + ops[k]["occ"]) - ops[k]["boost"], k) for k in range(n)]
+        KEPT["order"] = sorted(range(n), key=lambda q: (best[1][q], q))
+        KEPT["end"] = best[0]
+        KEPT["dbg"] = (ops, prio, succ, best[1])
+    order = KEPT["order"]
+    lastuse = {}
+    for k in order:
+        for b in ops[k]["banks"]:
+            lu = lastuse.setdefault(b, {})
+            ops[k]["dep"].update(q for e, q in lu.items() if e != ops[k]["eng"])
+            lu[ops[k]["eng"]] = k
 
     known = {e: {} for e in ENG}
     count = {"sV": 0, "sS": 0, "sP": 0, "sG": 0}

@@ -1,4 +1,6 @@
+import math
 import numpy as np
+from concourse.bass import DstId, RemoteDMATransfer
 from concourse.mybir import AluOpType as OP, ActivationFunctionType as AF, AxisListType
 
 NV, HOP, NC = 6, 3, 8
@@ -9,7 +11,17 @@ BIG = 2.0 ** 19
 HUGE = 2.0 ** 50
 OFF = 2.0 ** 18
 KIND = {0: "AA", 1: "AA"}
+DABS = (0, 1)
+AST = [(0, 0), (0, 1)]
 FIRST = {}
+WHOLE = ()
+GCONV = True
+GCOPY = 3
+CHS = []
+NR = 2
+VG = [(0, 0, 0), (0, 1, 0)]
+FLAT = 7.0
+FOLD = []
 
 FT = {}
 IT = {}
@@ -23,29 +35,32 @@ def _fields(d, items):
     return o
 
 
-NF = _fields(FT, [("LU", 128), ("CD", 256), ("Cb", 128), ("B1", 128), ("C2", 128), ("ABE", 64), ("y", 64)])
-NI = _fields(IT, [("CH", 128), ("r", 128), ("nh", 64)])
+NF = _fields(FT, [("LU", 128), ("CD", 256), ("O", 128), ("As1", 8), ("As2", 64), ("Cb", 128), ("B1", 128), ("C2", 128), ("ABE", 64), ("y", 64)])
+NI = _fields(IT, [("r", 128), ("nh", 64)])
 
 SCRATCH = {
     "tp": ("sbuf", [128, 256], "int32"), "tsx": ("sbuf", [128, 256], "int32"),
     "tl": ("sbuf", [128, 256], "int32"), "tq": ("sbuf", [128, 256], "int32"),
     "Lnum": ("sbuf", [128, 6 * 256], "int32"), "Loff": ("sbuf", [128, 9 * 256], "uint16"),
-    "Vk": ("sbuf", [128, 8 * 256], "float32"),
+    "Vk": ("sbuf", [128, 8 * 256], "int32"),
     "Dn": ("sbuf", [128, 6 * 256], "float16"), "eq": ("sbuf", [128, 6 * 256], "float16"),
     "Rq": ("sbuf", [128, 6 * 256], "float16"),
     "fin": ("sbuf", [128, 1024], "float32"),
-    "LoffB": ("sbuf", [128, 512], "uint16"), "VkB": ("sbuf", [128, 512], "float32"), "L5": ("sbuf", [128, 256], "int32"),
+    "LoffB": ("sbuf", [128, 512], "uint16"), "VkB": ("sbuf", [128, 512], "int32"), "L5": ("sbuf", [128, 256], "int32"),
     "R5": ("sbuf", [128, 256], "float16"), "R5B": ("sbuf", [128, 256], "float16"),
     "tf": ("sbuf", [128, 4 * NF], "float32"), "ti": ("sbuf", [128, 4 * NI], "int32"),
-    "E0": ("sbuf", [128, 128], "bfloat16"),
-    "mmsg": ("sbuf", [128, 12 * 64], "bfloat16"), "mland": ("sbuf", [128, 12 * 64], "bfloat16"),
+    "E0": ("sbuf", [128, 192], "bfloat16"),
+    "mmsg": ("sbuf", [128, 12 * 128], "bfloat16"), "mland": ("sbuf", [128, 12 * 64], "bfloat16"),
     "emsg": ("sbuf", [128, 12 * 128], "bfloat16"), "eland": ("sbuf", [128, 12 * 128], "bfloat16"),
-    "ETs": ("sbuf", [128, 4 * 128], "bfloat16"), "Js": ("sbuf", [128, 4 * 64], "bfloat16"),
-    "Ind": ("sbuf", [128, 2048], "bfloat16"), "maskz": ("sbuf", [128, 2048], "bfloat16"),
-    "one": ("sbuf", [128, 2048], "bfloat16"), "idn": ("sbuf", [128, 128], "bfloat16"),
+    "ETs": ("sbuf", [128, 4 * 192], "bfloat16"), "cj": ("sbuf", [128, 256], "bfloat16"),
+    "cz1": ("sbuf", [128, 128], "bfloat16"), "ch": ("sbuf", [128, 128], "bfloat16"), "blkH": ("sbuf", [128, 128], "bfloat16"),
+    "Bh": ("sbuf", [128, 144], "bfloat16"), "Bhn": ("sbuf", [128, 144], "bfloat16"),
+    "Ind": ("sbuf", [128, 2048], "bfloat16"), "maskz": ("sbuf", [128, 1024], "bfloat16"),
+    "pr0": ("sbuf", [128, 64], "bfloat16"), "pair": ("sbuf", [128, 64], "float32"), "grp8": ("sbuf", [128, 128], "float32"),
+    "one": ("sbuf", [128, 1024], "bfloat16"), "idn": ("sbuf", [128, 128], "bfloat16"),
     "nidn": ("sbuf", [128, 128], "bfloat16"), "kidn": ("sbuf", [128, 128], "bfloat16"),
     "nkidn": ("sbuf", [128, 128], "bfloat16"), "uidn": ("sbuf", [128, 128], "bfloat16"),
-    "blk0": ("sbuf", [128, 128], "bfloat16"),
+    "blk0": ("sbuf", [128, 128], "bfloat16"), "blkE": ("sbuf", [128, 128], "bfloat16"),
     "blk": ("sbuf", [128, 128], "bfloat16"), "blkP": ("sbuf", [128, 128], "bfloat16"),
     "blkN": ("sbuf", [128, 128], "bfloat16"), "blk2": ("sbuf", [128, 128], "float32"),
     "Bp": ("sbuf", [128, 144], "bfloat16"), "Bn": ("sbuf", [128, 144], "bfloat16"), "Be": ("sbuf", [128, 144], "bfloat16"),
@@ -63,23 +78,26 @@ SCRATCH = {
 for _t in range(NV - 1):
     SCRATCH["win%d" % _t] = ("sbuf", [128, WX], "bfloat16")
 for _z in range(4):
-    for _n in ("s", "dp", "ra"):
+    for _n in ("s", "dp", "ra", "l")[:4 if _z < 3 else 3]:
         SCRATCH["%s%d" % (_n, _z)] = ("sbuf", [128, CH], "bfloat16")
 for _z in range(2):
-    for _n in ("l", "dq", "rq", "vb", "vc", "vo", "sc"):
+    for _n in ("dq", "rq", "vb", "vc", "vo", "sc"):
         SCRATCH["%s%d" % (_n, _z)] = ("sbuf", [128, CH], "bfloat16")
 
-SEMAPHORES = (["sV", "sS", "sP", "sG", "lsem"] + ["w%d" % t for t in range(1, NV - 1)]
+SEMAPHORES = (["sV", "sS", "sP", "sG", "lsem"] + ["w%d" % t for t in range(2, 2 * NV - 2)]
               + ["m%d" % i for i in range(12)] + ["e%d" % i for i in range(12)]
-              + ["ld%d" % i for i in range(12)] + ["mu", "mv", "ml0", "ml1", "mr0", "mr1"] + ["st%d" % i for i in range(10)])
+              + ["ld%d" % i for i in range(12)] + ["mu", "mv", "ml0", "ml1", "mr0", "mr1"] + ["st%d" % i for i in range(10)]
+              + ["ad%d" % i for i in range(12)] + ["fl%d" % i for i in range(12)])
+ENGINES = {"fold": lambda en: en[0::2], "small": lambda en: en[len(en) // 2:], "bulk": lambda en: en[:len(en) // 2]}
 
 CYC = 0.83e-3 * 1.15
 PEC = 0.417e-3 * 1.15
 GAM = 1.5
 WAKE = 0.08
-SWEEPS = 150
-SEED, SHAKE = 1, 1.5
-CASES = [(0.9, 0.75, 1.0, 0.06), (0.9, 1.0, 1.5, 0.15), (1.0, 1.3, 1.0, 0.08), (1.25, 1.0, 1.2, 0.1)]
+STARTS, SWEEPS, STEPS = 5, 100, (1000, 6000, 6000)
+SEED, SHAKE, SPAN, SOME, HEAT = 2, 6.0, 12.0, 0.2, 0.04
+CASES = [(0.9, 0.8, 1.0, 0.06, 1.0), (0.95, 1.0, 1.5, 0.1, 1.0), (1.1, 1.2, 1.2, 0.08, 1.0), (1.15, 1.0, 1.5, 0.1, 1.55),
+         (0.95, 0.9, 1.0, 0.06, 1.6)]
 KEPT = {}
 
 
@@ -89,7 +107,7 @@ def rank_program(g, core, T, topo):
         return
     ENG = {"V": g.vector, "S": g.scalar, "P": g.tensor, "G": g, "Y": g.sync}
     ESEM = {"V": "sV", "S": "sS", "P": "sP", "G": "sG"}
-    PSUM = ("R0", "R1", "SB", "VB", "ZB", "MB")
+    PSUM = [k for k in SCRATCH if SCRATCH[k][0] == "psum"]
     ops = []
     acc = {}
     boost = [1000.0]
@@ -130,7 +148,7 @@ def rank_program(g, core, T, topo):
         for w, regs in ((False, rd), (True, wr)):
             for r in regs:
                 lst = acc[r[0]]
-                if w and r[3] == 1 and r[0] not in PSUM:
+                if w and r[3] == 1 and r[4] is None:
                     lst[:] = [x for x in lst if x[0] == k or not (x[1][1] >= r[1] and x[1][2] <= r[2])]
                 lst.append((k, r, w))
         ops.append({"eng": eng, "wr": wr, "banks": sorted(banks), "emit": emit, "dep": dep, "occ": occ, "lat": occ + 0.03 if lat is None else lat,
@@ -189,6 +207,10 @@ def rank_program(g, core, T, topo):
                0.065 + n_of(out) * GAM * CYC)
         ops[k]["gather"] = True
 
+    def gath_v(out, win, off):
+        k = op("V", lambda e: [e.tensor_copy(out=ap(out), in_=ap(win).indirect(ap(off)))], [win, off], [out], 0.05 + n_of(out) * GAM * CYC)
+        ops[k]["gather"] = True
+
     def gath_sub(out, win, off, b):
         k = op("V", lambda e: [e.tensor_tensor(out=ap(out), in0=ap(win).indirect(ap(off)), in1=ap(b), op=OP.subtract)],
                [win, off, b], [out], 0.05 + n_of(out) * GAM * CYC)
@@ -237,31 +259,46 @@ def rank_program(g, core, T, topo):
 
     nsent = [0]
 
-    def send(dst_rank, out, src, sem, lat=2.5, occ=0.7, bulk=False, deps=()):
+    def send(dst_rank, out, src, sem, lat=2.5, occ=0.8, use="small", deps=(), gone=None):
         dst = T.cores[dst_rank % NC]
         rid, pid = topo.addr(dst)[0], topo.addr(dst)[1]
         en = topo.engines(core, dst)
-        n = len(en) // 2
-        mask = sum(1 << q for q in (en[:n] if bulk else en[n:2 * n]))
-        nsent[0] += n
-        k = op("G", lambda e: [e.remote_dma(ap(out), ap(src), T.sem[sem], T.sem.lsem, pid, rid, mask)], [src], [], occ, occ,
-               sem="lsem", inc=0, deps=deps)
-        return op("N", None, [], [out], 0.0, lat, sem=sem, inc=n, deps=(k,))
+        en = ENGINES[use](en)
+        n = len(en)
+        mask = sum(1 << q for q in en)
+        if gone is None:
+            nsent[0] += n
+        left = T.sem[gone or "lsem"]
+        if isinstance(src, list):
+            def em(e):
+                return [e.remote_dma_fused([RemoteDMATransfer(dst_ids=[DstId(rid=rid, pnc=pid)], dma_engine_mask=mask, remote_sem=T.sem[sem],
+                                                              srcs=[ap(x) for x in src], dsts=[ap(out)], alu_op=2)], local_sem=left)]
+        else:
+            def em(e):
+                return [e.remote_dma(ap(out), ap(src), T.sem[sem], left, pid, rid, mask)]
+        srcs = src if isinstance(src, list) else [src]
+        k = op("G", em, srcs, [], occ, occ, sem="lsem", inc=0, deps=deps)
+        if gone:
+            op("N", None, srcs, [], 0.0, lat, sem=gone, inc=n, deps=(k,))
+        op("N", None, [], [out], 0.0, lat, sem=sem, inc=n, deps=(k,))
+        return k
 
-    def send_columns(t, deps=()):
-        send(rank - HOP * t, R("win%d" % t, 0, WX), R("win0", 0, WX), "w%d" % t, 8.0, bulk=True, deps=deps)
+    def send_columns(t, X, deps=()):
+        a, b = X * WX // 2, (X + 1) * WX // 2
+        send(rank - HOP * t, R("win%d" % t, a, b), R("win0", a, b), "w%d" % (2 * t + X), 9.0, use="bulk", deps=deps)
 
     I, NIDN, KI, NKI = R("idn", 0, 128), R("nidn", 0, 128), R("kidn", 0, 128), R("nkidn", 0, 128)
     ONE, BLK, ONE64 = R("one", 0, 128), R("blk", 0, 128), R("one", 0, 64)
-    load("S", R("tsx", 0, 128), "sl", 2.2)
+    load("S", R("tsx", 0, 128), "sl", 2.4)
+    load("S", R("tl", 0, 128), "ll", 2.7)
     load("Y", R("win0", 0, W), "xt", 4.5)
-    for j, (b, nm) in enumerate((("tp", "pl"), ("tl", "ll"), ("tq", "ql"))):
-        load("Y", R(b, 0, 128), nm, 5.0 + 0.4 * j)
-    load("Y", R("wti", 0, 1), "wt", 6.1)
-    load("Y", R("thi", 0, 1), "th", 6.3)
-    load("Y", R("E0", 0, 128), "ed", 6.6)
+    load("Y", R("E0", 0, 128), "ed", 4.7)
+    for j, (b, nm) in enumerate((("tp", "pl"), ("tq", "ql"))):
+        load("Y", R(b, 0, 128), nm, 5.0 + 0.3 * j)
+    load("Y", R("wti", 0, 1), "wt", 5.5)
+    load("Y", R("thi", 0, 1), "th", 5.7)
     for j, (b, nm) in enumerate((("tsx", "sl"), ("tp", "pl"), ("tl", "ll"), ("tq", "ql"))):
-        load("Y", R(b, 128, 256), nm, 7.0 + 0.4 * j)
+        load("Y", R(b, 128, 256), nm, 6.0 + 0.3 * j)
     vset(R("one", 0, 128), 1.0)
     vset(R("win0", W + 128, WX), 0.0)
     gsel(R("blk0", 0, 128), ONE, [[-16, 8], [0, 16]], OP.is_ge, 0, 1)
@@ -273,29 +310,41 @@ def rank_program(g, core, T, topo):
     vts(R("tci", 8, 9), R("tci", 0, 1), 15, OP.bitwise_and)
     vts(R("win0", W + 128, W + 129), R("tci", 4, 5), -16.0 * BIG, OP.mult)
     vts(R("win0", W + 129, W + 130), R("tci", 8, 9), -BIG, OP.mult)
-    vts(R("win0", W, W + 128), BLK, R("tcf", 0, 1), OP.mult)
-    send_columns(1)
+    vts(R("win0", W, W + 128), BLK, R("tcf", 0, 1), OP.mult, 1.0 / 2048.0, OP.mult)
+    send_columns(1, 0)
+    send_columns(1, 1)
     boost[0] = 0.0
-    vset(R("one", 128, 2048), 1.0)
+    vset(R("one", 128, 1024), 1.0)
     op("G", lambda e: [e.iota(ap(R("kin", 0, 1)), [[0, 1]], 0, 1)], [], [R("kin", 0, 1)], 0.2)
-    gsel(R("Ind", 0, 2048, 1, (0, 64)), R("one", 0, 2048, 1, (0, 64)), [[-1, 64], [0, 32]], OP.is_equal, 0, 1)
-    vts(NIDN, I, -1.0, OP.mult)
-    vts(KI, I, HUGE, OP.mult)
-    vts(NKI, I, -HUGE, OP.mult)
-    vts(R("uidn", 0, 128), I, -2048.0, OP.mult)
-    for nm, c in (("Bp", BIG), ("Bn", -BIG), ("Be", BIG / HUGE)):
-        vset(R(nm, 0, 144), 0.0)
-        vts(R(nm, 15, 128, 16), R("blk", 0, 128, 16), c, OP.mult)
-    vts(R("blkP", 0, 128), BLK, BIG, OP.mult)
-    vts(R("blkN", 0, 128), BLK, -BIG, OP.mult)
-    vts(R("blk2", 0, 128), BLK, 2.0, OP.mult)
-    vset(R("cz", 0, 128), -BIG / 512.0)
-    vset(R("cu", 0, 128, 1, (0, 64)), 129.0 * 32.0)
-    vset(R("cu", 0, 128, 1, (64, 128)), 0.5)
-    vset(R("o32", 0, 128), 1.0 / 32.0)
-    vset(R("cc", 0, 128), -15.5 / 8192.0)
-    vset(R("maskz", 0, CH), 1.0)
-    vset(R("maskz", 0, CH, 32), 0.0)
+    for h in range(2):
+        gsel(R("Ind", 1024 * h, 1024 * h + 1024, 1, (0, 64)), R("one", 0, 1024, 1, (0, 64)), [[-1, 32], [0, 32]], OP.is_equal, -32 * h, 1)
+    for out, src, c in ((NIDN, I, -1.0), (KI, I, HUGE), (NKI, I, -HUGE),
+                        (R("blkE", 0, 128), BLK, BIG / HUGE), (R("blkP", 0, 128), BLK, BIG), (R("blkH", 0, 128), BLK, -BIG * HUGE),
+                        (R("cz1", 0, 128), ONE, BIG * HUGE * 31.75 / 128.0), (R("ch", 0, 128), ONE, BIG * HUGE / 256.0),
+                        (R("blkN", 0, 128), BLK, -BIG), (R("blk2", 0, 128), BLK, 2.0),
+                        (R("cz", 0, 128), ONE, -BIG / 512.0),
+                        (R("o32", 0, 128), ONE, 1.0 / 32.0),
+                        (R("cc", 0, 128), ONE, -15.5 / 8192.0)):
+        act(out, src, AF.Copy, c)
+    vset(R("Bp", 0, 144), 0.0)
+    vts(R("Bp", 15, 128, 16), R("blk", 0, 128, 16), BIG, OP.mult)
+    act(R("Bn", 0, 144), R("Bp", 0, 144), AF.Copy, -1.0)
+    act(R("Be", 0, 144), R("Bp", 0, 144), AF.Copy, 1.0 / HUGE)
+    act(R("Bh", 0, 144), R("Bp", 0, 144), AF.Copy, HUGE)
+    act(R("Bhn", 0, 144), R("Bp", 0, 144), AF.Copy, -HUGE)
+    vset(R("cu", 0, 128, 1, (0, 64)), 129.0 / 64.0)
+    vset(R("cu", 0, 128, 1, (64, 128)), 2.0 ** -12)
+    vset(R("cj", 0, 128, 1, (0, 64)), 2.0)
+    vset(R("cj", 0, 128, 1, (64, 128)), 1.0 / 128.0)
+    vset(R("cj", 128, 256), 2.0 ** -19)
+    vset(R("E0", 128, 192), 0.0)
+    op("G", lambda e: [e.iota(ap(R("maskz", 0, 1024)), [[0, 32], [256, 32]], 0, 0, allow_small_or_imprecise_dtypes=True)],
+       [], [R("maskz", 0, 1024)], 0.15 + 2 * 1024 * CYC)
+    P8 = (0, 8)
+    gsel(R("pr0", 0, 64), ONE64, [[-2, 64]], OP.is_ge, 0, 1)
+    gsel(R("pair", 0, 64), R("pr0", 0, 64), [[2, 64]], OP.is_ge, 1, -1)
+    gsel(R("blk0", 0, 128, 1, P8), R("one", 0, 128, 1, P8), [[1, 128]], OP.is_ge, 0, -16)
+    gsel(R("grp8", 0, 128, 1, P8), R("blk0", 0, 128, 1, P8), [[-1, 128]], OP.is_ge, 15, 16)
     vts(R("kin", 8, 9), R("kin", 0, 1), 15, OP.bitwise_and)
     for h in range(2):
         c = 37.0 * 16 * h + 2048.0 - 31.0 / 64.0
@@ -320,6 +369,29 @@ def rank_program(g, core, T, topo):
     def voff(k):
         return OFF + 2048.0 * (8 - (k if k > -3 else -1))
 
+    def gcopy(out, a):
+        gsel(out, a, [[0, n_of(out)]], OP.is_ge, 0, 0)
+
+    nadd = [0]
+
+    def add_into(out, src, rd):
+        op("G", lambda e: [e.dma_start(out=ap(out), in_=src, accum_op=OP.add)], rd + [out], [out], 1.6, 4.5, sem="ad%d" % nadd[0], inc=16)
+        nadd[0] += 1
+
+    def make_v(k, X, src):
+        if not GCONV:
+            vts(Vk(k, X), src, voff(k), OP.add)
+        elif k > 0:
+            add_into(Vk(k, X), ap(src), [src])
+        elif X == 0:
+            add_into(R("Vk", (k + 3) * 256, (k + 4) * 256), T[("ql", "pl", "sl", "ll")[k + 3]][:], [])
+
+    if GCONV:
+        for lo, hi in ((-3, -2), (-2, 1), (1, 5)):
+            v = R("Vk", (lo + 3) * 256, (hi + 3) * 256)
+            op("G", lambda e, v=v, lo=lo, hi=hi: [e.iota(ap(v), [[-2048, hi - lo], [0, 256]], int(voff(lo)), 0)], [], [v],
+               0.15 + 2 * n_of(v) * CYC)
+
     def slot(b, X, j):
         return R(b, 768 * X + j, 768 * X + 768, 6)
 
@@ -328,18 +400,19 @@ def rank_program(g, core, T, topo):
 
     for X in range(2):
         for k in (-1, -2, 0, -3):
-            vcopy(Lu(k, X), Ln(k, X))
+            (gcopy if GCOPY and (X == 1 or k < -1) else vcopy)(Lu(k, X), Ln(k, X))
         for k in (-2, -3, -1, 0):
-            vts(Vk(k, X), Ln(k, X), voff(k), OP.add)
+            make_v(k, X, Ln(k, X))
         vtt(slot("Dn", X, 0), Ln(-3, X), Ln(0, X), OP.subtract)
 
-    def sums(out, parts):
-        pe(group(out, [(R(coef, 15 - i, 143 - i), R(tile[0], tile[1] + i, tile[2], 16)) for (coef, tile) in parts for i in range(16)]))
+    def sums(out, parts, more=()):
+        pe(group(out, [(R(coef, 15 - i, 143 - i), R(tile[0], tile[1] + i, tile[2], 16)) for (coef, tile) in parts for i in range(16)]
+                 + list(more)))
 
     nreg = [0]
 
     def size(out, terms):
-        rb = "R%d" % (nreg[0] % 2)
+        rb = "R%d" % (nreg[0] % NR)
         nreg[0] += 1
         mm = []
         for j in range(2):
@@ -347,8 +420,8 @@ def rank_program(g, core, T, topo):
         pe(mm)
         act(out, R(rb, 0, 1024), AF.Abs)
 
-    def relu2(out, a):
-        vts(out, a, 0.0, OP.max, 2.0, OP.mult)
+    def relu2(out, a, c=1.0):
+        vts(out, a, 0.0, OP.max, 2.0 * c, OP.mult)
 
     for t in range(NV):
         last = t == NV - 1
@@ -357,7 +430,7 @@ def rank_program(g, core, T, topo):
         WIN = R(wn, 0, W)
         TH = R("af", 12, 13) if last else R("af", t * 16 + 12, t * 16 + 13)
         if not last:
-            vts(TH, R(wn, W + 128, W + 129), R(wn, W + 129, W + 130), OP.add)
+            act(TH, R(wn, W + 128, W + 129), AF.Identity, None, R(wn, W + 129, W + 130))
         for X in range(2):
             z, y, sl = (t % 2) * 2 + X, X, 2 * t + X
             kind = "SS" if t == 0 else KIND.get((t, X), KIND[X])
@@ -371,8 +444,8 @@ def rank_program(g, core, T, topo):
                 return R("ti", z * NI + o, z * NI + o + n)
 
             def tile(nm, h):
-                q = z if nm in ("s", "dp", "ra") else y
-                return R("%s%d" % (nm, q), 1024 * h, 1024 * h + 1024)
+                q = z if nm in ("s", "dp", "ra") else sl % 3 if nm == "l" else y
+                return R("%s%d" % (nm, q), 0, CH) if h is None else R("%s%d" % (nm, q), 1024 * h, 1024 * h + 1024)
 
             E = R("E0", 64 * X, 64 * X + 64) if t == 0 else R("eland", (sl - 2) * 128, (sl - 2) * 128 + 64)
             L = Ln(t, X)
@@ -380,35 +453,43 @@ def rank_program(g, core, T, topo):
                 if kind[h] == "S":
                     gath_s(tile("s", h), WIN, Lu(t - 1, X, h))
                     gath_sub(tile("dp", h), WIN, Lu(t - 2, X, h), tile("s", h))
-                    relu2(tile("ra", h), tile("dp", h))
+                    relu2(tile("ra", h), tile("dp", h), HUGE)
                     if t == 0:
                         gath_sub(tile("dq", h), WIN, Lu(-3, X, h), tile("s", h))
-                        relu2(tile("rq", h), tile("dq", h))
-            for h in range(2):
-                gath_s(tile("l", h), WIN, Lu(t, X, h))
-                if kind[h] != "S":
-                    gath_sub(tile("s", h), WIN, Lu(t - 1, X, h), tile("l", h))
-                    gath_sub(tile("dp", h), WIN, Lu(t - 2, X, h), tile("l", h))
-                if kind[h] == "L":
+                        if X in DABS:
+                            act(tile("rq", h), tile("dq", h), AF.Abs)
+                        else:
+                            relu2(tile("rq", h), tile("dq", h))
+            def parts(what):
+                return [None] if what in WHOLE and (kind[0] == kind[1] or what == "sc") else [0, 1]
+
+            for h in parts("l"):
+                (gath_v if (t, X, h) in VG else gath_s)(tile("l", h), WIN, Lu(t, X, h))
+            for nm, k in (("s", t - 1), ("dp", t - 2)):
+                for h in parts(nm):
+                    if kind[h or 0] != "S":
+                        gath_sub(tile(nm, h), WIN, Lu(k, X, h), tile("l", h))
+            for h in parts("vc"):
+                if kind[h or 0] == "L":
                     relu2(tile("vc", h), tile("dp", h))
-                if kind[h] == "A":
+                if kind[h or 0] == "A":
                     act(tile("vc", h), tile("dp", h), AF.Abs)
-            vscan(R("sc%d" % y, 0, CH), R("maskz", 0, CH), R("l%d" % y, 0, CH), OP.mult, OP.max)
-            M = R("mmsg", sl * 64, sl * 64 + 64)
-            gsel(M, R("sc%d" % y, 31, CH, 32), [[0, 64]], OP.is_ge, 0, 0)
-            MR = R("mland", sl * 64, sl * 64 + 64)
+            for h in range(2):
+                vscan(tile("sc", h), R("maskz", 0, 1024), tile("l", h), OP.min, OP.max)
+            M, MR = R("mmsg", sl * 64, sl * 64 + 64), R("mland", sl * 64, sl * 64 + 64)
+            gcopy(M, R("sc%d" % y, 31, CH, 32))
             km = send(rank + 4, MR, M, "m%d" % sl)
-            if X == 0 and t + 2 < NV - 1:
-                send_columns(t + 2, (km - 1,))
+            if t + 2 < NV - 1:
+                send_columns(t + 2, X, (km,))
             WM = R(wn, W, W + 128)
-            pe(group(R("MB", 0, 128, 1, (0, 64)), [(E, NIDN)]) + group(R("MB", 128, 192), [(WM, E)]))
-            ET = R("ETs", z * 128, z * 128 + 128, 1, (0, 64))
-            JU = R("Js", z * 64, z * 64 + 64)
-            act(ET, R("MB", 0, 128, 1, (0, 64)), AF.Copy)
-            act(JU, R("MB", 128, 192), AF.Identity, 1.0 / 2048.0, 129.0 - 1023.5 / 2048.0)
-            U = R("MB", 192, 320)
-            pe(sum([group(every(U, h), [(WM, E), (R("uidn", 0, 128), JU), (R("cu", 0, 128), ONE64)]) for h in range(2)], []))
-            vtt(F("LU"), L, U, OP.mult)
+            pe(group(R("MB", 0, 128), [(R(E[0], E[1], E[1] + 128), NIDN)]) + group(R("MB", 128, 192), [(WM, E), (R("cj", 0, 128), ONE64), (R("cj", 128, 256), ONE64)]))
+            ET = R("ETs", z * 192, z * 192 + 128, 1, (0, 64))
+            JU = R("ETs", z * 192 + 128, z * 192 + 192)
+            act(R("ETs", z * 192, z * 192 + 192), R("MB", 0, 192), AF.Copy)
+            U = R("MB", 192, 256)
+            pe(group(U, [(WM, E), (NIDN, JU), (R("cu", 0, 128), ONE64)]))
+            for h in range(2):
+                vtt(every(F("LU"), h), every(L, h), U, OP.mult)
             if t == 0:
                 colA = R("k37", 0, 2)
             else:
@@ -419,88 +500,76 @@ def rank_program(g, core, T, topo):
                                   (R("o32", 0, 128), R("eland", (sl - 1) * 128 + 64, (sl - 1) * 128 + 128)),
                                   (R("cc", 0, 128), ONE64)]))
                     act(R("junk", 0, 64), cn, AF.Copy, acc_out=xa)
-                    vts(R("ai", t * 8, t * 8 + 1), xa, 1.0 / 32.0, OP.mult)
-                    vts(R("af", t * 16 + 4, t * 16 + 5), R("ai", t * 8, t * 8 + 1), -32.0, OP.mult, xa, OP.add)
-                    vts(colA, R("k37", 2, 4), R("af", t * 16 + 4, t * 16 + 5), OP.add)
+                    x32 = R("af", t * 16 + 4, t * 16 + 5)
+                    vts(x32, xa, 1.5 * 2.0 ** 28, OP.add, -1.5 * 2.0 ** 28, OP.add)
+                    vts(colA, R("k37", 2, 4), xa, OP.add, x32, OP.subtract)
+            GA = R("VB", 128 * X, 128 * X + 128)
             for h in range(2):
-                vts(every(J("CH"), h), every(F("LU"), h), 1.0 / 32.0, OP.mult, R(colA[0], colA[1] + h, colA[1] + h + 1), OP.add)
+                col = R(colA[0], colA[1] + h, colA[1] + h + 1)
+                if (t, X) in CHS:
+                    act(every(GA, h), every(F("LU"), h), AF.Identity, 64.0, col)
+                else:
+                    vts(every(GA, h), every(F("LU"), h), 64.0, OP.mult, col, OP.add)
             pe(group(R("MB", 320, 384), [(I, E), (NIDN, MR)]) + group(R("MB", 384, 448), [(I, E), (I, MR)]))
             act(F("ABE"), R("MB", 320, 384), AF.Abs)
             vts(J("nh"), R("MB", 384, 448), -0.5, OP.mult, 0.25, OP.add)
             Z = R("ZB", 0, 64)
             B, C, D, O = [R("SB", 128 * j, 128 * j + 128) for j in range(4)]
 
+            for h in range(2):
+                ind = R("Ind", 1024 * h, 1024 * h + 1024, 1, (0, 64))
+                if t == 0:
+                    size(tile("vc", h), [(I, tile("s", h)), (I, tile("dp", h)), (NIDN, tile("l", h))])
+                    size(tile("vo", h), [(I, tile("l", h)), (ET, ind)])
+                    size(tile("vb", h), [(I, tile("s", h)), (NIDN, tile("l", h))])
+                elif kind[h] == "S":
+                    size(tile("vc", h), [(KI, tile("s", h)), (KI, tile("dp", h)), (NKI, tile("l", h))])
+                    size(tile("vb", h), [(KI, tile("s", h)), (NKI, tile("l", h)), (I, tile("l", h)), (ET, ind)])
+                else:
+                    size(tile("ra", h), [(KI, tile("dp", h)), (NKI, tile("s", h))])
+                    size(tile("vb", h), [(KI, tile("s", h)), (I, tile("l", h)), (ET, ind)])
+            A1, A2 = R("ZB", 64, 72), R("ZB", 128, 192, 1, P8)
+            AS2 = F("As2")[:4] + (P8,)
+            zs = [(R("cz1" if t else "cz", 0, 128), ONE64)]
+            if (t, X) in AST:
+                pe(group(A1, [(R(tile(nm, None)[0], i, CH, 16), R(coef, 0, 128, 16))
+                              for (coef, nm) in ((("blkP", "ra"),) if t else (("blkE", "ra"), ("blkN", "dp"))) for i in range(16)]))
+                act(F("As1"), A1, AF.Copy)
+                pe(group(A2, [(F("As1"), R("pair", 0, 64))]))
+                act(AS2, A2, AF.Copy)
+                zs.append((R("grp8", 0, 128, 1, P8), AS2))
+            else:
+                zs += [(R("blkP", 0, 128), R(tile("ra", None)[0], k, CH, 32)) for k in range(32)]
+                pe([m[:4] + (False,) for m in group(Z, zs)])
+
             def part(r, h):
                 return R(r[0], r[1] + 64 * h, r[1] + 64 * h + 64)
 
-            zopen = [True]
-
-            def page_sums(h, parts):
-                zo = R("ZB", 32 * h, 32 * h + 32)
-                mm = []
-                if zopen[0]:
-                    mm.append((Z, R("cz", 0, 128), ONE64, True, False))
-                    zopen[0] = False
-                for (coef, tl) in parts:
-                    for k in range(16):
-                        for hh in range(2):
-                            mm.append((zo, R(coef, 0, 128), R(tl[0], tl[1] + 16 * hh + k, tl[2], 32), False, False))
-                pe(mm)
-
-            def page_sums2(parts):
-                mm = [(Z, R("cz", 0, 128), ONE64, True, False)]
-                for (coef, nm) in parts:
-                    for k in range(32):
-                        mm.append((Z, R(coef, 0, 128), R(tile(nm, 0)[0], k, CH, 32), False, False))
-                pe(mm)
-
-            for h in range(2):
-                ind = R("Ind", 1024 * h, 1024 * h + 1024, 1, (0, 64))
-                if kind[h] == "S":
-                    size(tile("vc", h), [(I, tile("s", h)), (I, tile("dp", h)), (NIDN, tile("l", h))])
-                    if t == 0:
-                        size(tile("vo", h), [(I, tile("l", h)), (ET, ind)])
-                        size(tile("vb", h), [(I, tile("s", h)), (NIDN, tile("l", h))])
-                    else:
-                        size(tile("vb", h), [(KI, tile("s", h)), (NKI, tile("l", h)), (I, tile("l", h)), (ET, ind)])
-                else:
-                    size(tile("ra", h), [(I, tile("dp", h)), (NIDN, tile("s", h))])
-                    size(tile("vb", h), [(KI, tile("s", h)), (I, tile("l", h)), (ET, ind)])
-            if kind == "SS":
-                page_sums2([("blkP", "ra"), ("blkN", "dp")])
-            elif "S" not in kind:
-                page_sums2([("blkP", "ra")])
-            else:
-                page_sums2([("blkP", "ra")])
-                hs = kind.index("S")
-                pe([(R("ZB", 32 * hs, 32 * hs + 32), R("blkN", 0, 128), R(tile("dp", 0)[0], 1024 * hs + k, 1024 * hs + 1024, 32), False, False)
-                    for k in range(32)])
-            bc = "Bp" if t == 0 else "Be"
             if t == 0:
-                for h in range(2):
-                    sums(part(D, h), [("Bp", tile("rq", h)), ("Bn", tile("dq", h))])
-            sums(part(C, 0), [("Bp", tile("vc", 0))] + ([("Bn", tile("dp", 0))] if kind[0] == "L" else []))
-            if t == 0:
-                sums(part(O, 0), [("Bp", tile("vo", 0))])
-            sums(part(B, 0), [(bc, tile("vb", 0))])
-            sums(part(C, 1), [("Bp", tile("vc", 1))] + ([("Bn", tile("dp", 1))] if kind[1] == "L" else []))
-            if t == 0:
+                sums(D, [("Bp", tile("rq", None))] + ([] if X in DABS else [("Bn", tile("dq", None))]))
+                sums(C, [("Bp", tile("vc", None))])
                 act(F("CD"), R("SB", 128, 384), AF.Copy)
-                sums(part(O, 1), [("Bp", tile("vo", 1))])
-                act(O, O, AF.Identity, None, TH)
+                sums(O, [("Bp", tile("vo", None))])
+                for h in range(2):
+                    sums(part(B, h), [("Bp", tile("vb", h))])
+                act(F("O"), O, AF.Identity, None, TH)
+                vtt(F("Cb"), B, F("CD", 0, 128), OP.subtract)
             else:
-                act(F("CD", 0, 128), C, AF.Copy)
-            sums(part(B, 1), [(bc, tile("vb", 1))])
-            vtt(F("Cb"), B, F("CD", 0, 128), OP.subtract)
-            pe([(Z, R("blk2", 0, 128), every(F("Cb"), 0), False, False), (Z, R("blk2", 0, 128), every(F("Cb"), 1), False, True)])
-            GA, PB, XC = R("VB", 128 * X, 128 * X + 128), R("VB", 256, 384), R("VB", 384, 448)
+                sums(C, [("Bh", tile("vc", None))], [(R("ch", 0, 128), ONE)])
+                for h in range(2):
+                    sums(part(B, h), [("Be", tile("vb", h))])
+                act(F("O"), B, AF.Identity, HUGE, TH)
+                vtt(F("Cb"), F("O"), C, OP.subtract)
+            zc = group(Z, [(R("blk2", 0, 128), every(F("Cb"), 0)), (R("blk2", 0, 128), every(F("Cb"), 1))])
+            zc[0] = zc[0][:3] + (False, False)
+            pe(([m[:4] + (False,) for m in group(Z, zs)] if (t, X) in AST else []) + zc)
+            PB, XC = R("VB", 256, 384), R("VB", 384, 448)
             if t == 0:
                 vtt(PB, B, F("CD", 128, 256), OP.subtract)
                 vtt(F("B1"), Vk(-3, X), PB, OP.min)
             else:
                 vtt(F("B1"), Vk(t - 1, X), B, OP.min)
-                act(O, B, AF.Identity, HUGE, TH)
-            vtt(GA, J("CH"), O, OP.min)
+            vtt(GA, F("O"), GA, OP.min)
             vtt(GA, L, GA, OP.max)
             vtt(GA, F("B1"), GA, OP.max)
             for h in range(2):
@@ -514,7 +583,7 @@ def rank_program(g, core, T, topo):
             if move:
                 send(home, Ln(t + 1, X), NEW, "ml%d" % X)
             if not last:
-                vcopy(Lu(t + 1, X), Ln(t + 1, X))
+                (gcopy if GCOPY > 1 else vcopy)(Lu(t + 1, X), Ln(t + 1, X))
             EM = R("emsg", sl * 128, sl * 128 + 64)
             vtt(XC, F("ABE"), Z, OP.min)
             vtt(F("y"), J("nh"), XC, OP.max)
@@ -525,11 +594,11 @@ def rank_program(g, core, T, topo):
                 send(rank + HOP * t if move else rank - HOP, R("eland", sl * 128, sl * 128 + 128), R("emsg", sl * 128, sl * 128 + 128),
                      "e%d" % sl)
             if t + 1 <= NV - 2:
-                vts(Vk(t + 1, X), NEW, voff(t + 1), OP.add)
+                make_v(t + 1, X, NEW)
             if t == NV - 3 and X == 1:
-                send(home, R("LoffB", 0, 512), R("Loff", (t + 3) * 256, (t + 5) * 256), "mu", 3.5, bulk=True)
-                send(home, R("VkB", 0, 512), R("Vk", (t + 3) * 256, (t + 5) * 256), "mv", 4.5, bulk=True)
-                act(R("fin", 0, 256), R("VkB", 256, 512), AF.Identity, None, -voff(t + 1))
+                send(home, R("LoffB", 0, 512), R("Loff", (t + 3) * 256, (t + 5) * 256), "mu", 4.5, use="bulk")
+                send(home, R("VkB", 0, 512), R("Vk", (t + 3) * 256, (t + 5) * 256), "mv", 7.0, use="bulk")
+                vts(R("fin", 0, 256), R("VkB", 256, 512), -voff(t + 1), OP.add)
                 store("Y", "yp", 0, 256, R("fin", 0, 256), "st0")
             if not last:
                 vtt(slot("Dn", X, t + 1), L, NEW, OP.subtract)
@@ -538,9 +607,9 @@ def rank_program(g, core, T, topo):
                 vts(R("eq", a, b), R("Dn", a, b), 0.0, OP.is_equal)
                 vset(slot("eq", X, 0), 0.0)
                 vscan(R("Rq", a, b), R("eq", a, b), R("Dn", a, b), OP.mult, OP.add)
-                vcopy(R("R5", 128 * X, 128 * X + 128), slot("Rq", X, 5))
+                gcopy(R("R5", 128 * X, 128 * X + 128), slot("Rq", X, 5))
                 send(home, R("R5B", 128 * X, 128 * X + 128), R("R5", 128 * X, 128 * X + 128), "mr%d" % X)
-                vcopy(R("fin", 256 + 128 * X, 384 + 128 * X), Ln(t + 1, X))
+                (gcopy if GCOPY else vcopy)(R("fin", 256 + 128 * X, 384 + 128 * X), Ln(t + 1, X))
                 store("Y", "ys", 128 * X, 128 * X + 128, R("fin", 256 + 128 * X, 384 + 128 * X), "st%d" % (1 + 4 * X))
             if last:
                 FL, FQ = R("fin", 512 + 128 * X, 640 + 128 * X), R("fin", 768 + 128 * X, 896 + 128 * X)
@@ -562,80 +631,158 @@ def rank_program(g, core, T, topo):
         prio[k] = ops[k]["lat"] + max([prio[s] + 0.08 for s in succ[k]] + [0.0])
 
     def place(key, back):
-        before = succ if back else [list(o["dep"]) for o in ops]
+        before, after = (succ, pred) if back else (pred, succ)
         at = [0.0] * n
+        done = [0.0] * n
         used = {e: [] for e in ENG}
-        held = {}
-        after = [list(o["dep"]) for o in ops] if back else succ
+        held = {b: [] for x in bank for b in x}
         left = [len(x) for x in before]
         ready = [k for k in range(n) if not left[k]]
         while ready:
-            k = min(ready, key=lambda q: key[q] if back or "first" not in ops[q] else (-1e9, q))
+            k = min(ready, key=key.get)
             ready.remove(k)
             for q in after[k]:
                 left[q] -= 1
                 if not left[q]:
                     ready.append(q)
-            o = ops[k]
+            s, e, c = 0.0, eng[k], occ[k]
+            for q in before[k]:
+                if done[q] > s:
+                    s = done[q]
             if back:
-                s = max([at[q] + ops[q]["occ"] + WAKE for q in before[k]] + [-0.0]) + o["lat"] - o["occ"]
-            else:
-                s = max([at[q] + ops[q]["lat"] + WAKE for q in before[k]] + [0.0])
-            if o["eng"] != "N":
-                u = used[o["eng"]]
-                lo, hi = (o["occ"] - o["lat"] - WAKE, o["occ"]) if back else (0.0, o["lat"] + WAKE)
+                s += lat[k] - c
+            if e != "N":
+                u = used[e]
+                lo, hi = (c - lat[k] - WAKE, c) if back else (0.0, lat[k] + WAKE)
                 while True:
                     j = len(u)
                     while j > 0 and u[j - 1][1] > s:
                         j -= 1
-                    while j < len(u) and u[j][0] < s + o["occ"] - 1e-9:
+                    while j < len(u) and u[j][0] < s + c - 1e-9:
                         s = max(s, u[j][1])
                         j += 1
-                    clash = [x[1] for b in o["banks"] for x in held.setdefault(b, [])
-                             if x[2] != o["eng"] and x[1] > s + lo + 1e-9 and x[0] < s + hi - 1e-9]
-                    if not clash:
+                    s2 = s
+                    for b in bank[k]:
+                        h = held[b]
+                        i = len(h) - 1
+                        while i >= 0 and h[i][0] > s + lo - 4.0:
+                            if h[i][2] != e and h[i][1] > s + lo + 1e-9 and h[i][0] < s + hi - 1e-9:
+                                s2 = max(s2, h[i][1] - lo)
+                            i -= 1
+                    if s2 == s:
                         break
-                    s = max(clash) - lo
-                u.insert(j, (s, s + o["occ"]))
-                for b in o["banks"]:
-                    held[b].append((s + lo, s + hi, o["eng"]))
+                    s = s2
+                u.insert(j, (s, s + c))
+                for b in bank[k]:
+                    h = held[b]
+                    i = len(h)
+                    while i > 0 and h[i - 1][0] > s + lo:
+                        i -= 1
+                    h.insert(i, (s + lo, s + hi, e))
             at[k] = s
+            done[k] = s + (c if back else lat[k]) + WAKE
         return at
 
-    def replay(order, f, gam, dma, wake):
-        fin = [0.0] * n
-        free = {e: 0.0 for e in ENG}
-        lastuse = {}
+    def replay(order, ties=None):
+        waits, lastuse = [], {}
         for k in order:
-            o = ops[k]
-            e = o["eng"]
-            s = max([fin[q] + wake for q in o["dep"]] + [free.get(e, 0.0)])
-            for b in o["banks"]:
+            w = pred[k]
+            for b in bank[k]:
                 lu = lastuse.setdefault(b, {})
-                s = max([s] + [fin[q] + wake for x, q in lu.items() if x != e])
-                lu[e] = k
-            c = dma if o["sem"] else f * (gam if o.get("gather") else 1.0)
-            if e != "N":
-                free[e] = s + o["occ"] * c
-            fin[k] = s + o["lat"] * c
-        return max(fin)
+                w = w + [q for x, q in lu.items() if x != eng[k]]
+                lu[eng[k]] = k
+            waits.append(w)
+        total = 0.0
+        for (f, gam, dma, wake, ten), (oc, la) in zip(CASES, scaled):
+            fin = [0.0] * n
+            why = [None] * n
+            free = {e: 0.0 for e in "VSPGYN"}
+            prev = {}
+            for k, w in zip(order, waits):
+                e = eng[k]
+                s, y = free[e], prev.get(e)
+                for q in w:
+                    if fin[q] > s:
+                        s, y = fin[q], q
+                if e != "N":
+                    free[e] = s + oc[k]
+                    prev[e] = k
+                fin[k] = s + la[k]
+                why[k] = y
+            end = max(fin)
+            total += end / (f * (0.6 + 0.4 * gam))
+            if ties is not None:
+                k = fin.index(end)
+                while why[k] is not None:
+                    if why[k] not in ops[k]["dep"] and "first" not in ops[k]:
+                        ties.append((why[k], k))
+                    k = why[k]
+        return total / len(CASES)
 
     if "order" not in KEPT:
-        key = [(-prio[k] - ops[k]["boost"], k) for k in range(n)]
-        best = None
+        pred = [sorted(o["dep"]) for o in ops]
+        eng, occ, lat, bank = [[o[x] for o in ops] for x in ("eng", "occ", "lat", "banks")]
+        early = [o["boost"] + (1e6 if "first" in o else 0.0) for o in ops]
+        scaled = []
+        for (f, gam, dma, wake, ten) in CASES:
+            c = [dma if o["sem"] else f * (gam if o.get("gather") else ten if o["eng"] == "P" else 1.0) for o in ops]
+            scaled.append(([occ[k] * c[k] for k in range(n)], [lat[k] * c[k] + wake for k in range(n)]))
         rng = np.random.default_rng(SEED)
-        for sweep in range(SWEEPS):
-            at = place(key, False)
-            order = sorted(range(n), key=lambda q: (at[q], q))
-            end = sum(replay(order, *c) / c[0] for c in CASES) / len(CASES)
-            if best is None or end < best[0]:
-                best = (end, at)
-            shake = rng.random(n) * SHAKE
-            bk = place([(-best[1][k] + float(shake[k]), -k) for k in range(n)], True)
-            key = [(-(bk[k] + ops[k]["occ"]) - ops[k]["boost"], k) for k in range(n)]
-        KEPT["order"] = sorted(range(n), key=lambda q: (best[1][q], q))
+
+        def packed():
+            key = {k: (-prio[k] * ("first" not in ops[k]) - early[k], k) for k in range(n)}
+            best = None
+            for sweep in range(SWEEPS):
+                at = place(key, False)
+                end = replay(sorted(range(n), key=lambda q: (at[q], q)))
+                if best is None or end < best[0]:
+                    best = (end, at)
+                a = rng.random() * max(best[1]) - SPAN / 2
+                shake = (rng.random(n) - 0.5) * SHAKE * (0.3 + rng.random()) * (rng.random(n) < SOME)
+                was = [best[1][k] + (float(shake[k]) if sweep < 20 or a < best[1][k] < a + SPAN else 0.0) for k in range(n)]
+                if sweep < 20 or sweep % 2 == 0:
+                    bk = place({k: (-was[k], -k) for k in range(n)}, True)
+                    was = [-(bk[k] + occ[k]) for k in range(n)]
+                key = {k: (was[k] * ("first" not in ops[k]) - early[k], k) for k in range(n)}
+            return sorted(range(n), key=lambda q: (best[1][q], q))
+
+        def moved_on(order, steps):
+            ties = []
+            now = replay(order, ties)
+            best = (now, order)
+            for step in range(steps):
+                j, k = ties[int(rng.integers(len(ties)))]
+                a, b = order.index(j), order.index(k)
+                mid = order[a:b + 1]
+                if rng.random() < 0.5:
+                    take = {k}
+                    for q in reversed(mid):
+                        if q in take:
+                            take.update(pred[q])
+                    if j in take:
+                        continue
+                    mid = [q for q in mid if q in take] + [q for q in mid if q not in take]
+                else:
+                    take = {j}
+                    for q in mid:
+                        if q in take:
+                            take.update(succ[q])
+                    if k in take:
+                        continue
+                    mid = [q for q in mid if q not in take] + [q for q in mid if q in take]
+                new, t2 = order[:a] + mid + order[b + 1:], []
+                end = replay(new, t2)
+                if end < now + HEAT * (1.0 - step / steps) * -math.log(1.0 - rng.random()):
+                    order, now, ties = new, end, t2
+                    if end < best[0]:
+                        best = (end, order)
+            return best
+
+        best = min(moved_on(packed(), STEPS[0]) for j in range(STARTS))
+        for steps in STEPS[1:]:
+            best = moved_on(best[1], steps)
+        KEPT["order"] = best[1]
         KEPT["end"] = best[0]
-        KEPT["dbg"] = (ops, prio, succ, best[1])
     order = KEPT["order"]
     lastuse = {}
     for k in order:

@@ -5,23 +5,22 @@ from concourse.mybir import AluOpType as OP, ActivationFunctionType as AF, AxisL
 
 NV, HOP, NC = 6, 3, 8
 W = 2048
-WX = W + 128 + 16
+WX = 128
+WT = W + 8
 CH = 2048
-BIG = 2.0 ** 19
-HUGE = 2.0 ** 50
-OFF = 2.0 ** 18
-KIND = {0: "AA", 1: "AA"}
+BIG = 2.0 ** 21
+HUGE = 2.0 ** 16
+TOP = 2.0 ** 18
+WHOLE23 = 1.5 * 2.0 ** 23
+KIND = {0: "AL", 1: "AA", (4, 0): "AA", (5, 0): "AA"}
 DABS = (0, 1)
 AST = [(0, 0), (0, 1)]
 FIRST = {}
 WHOLE = ()
-GCONV = True
-GCOPY = 3
-CHS = []
+ONV = {"O": [(t, 0) for t in range(4)], "ET": [(0, 0), (0, 1)], "W": [1]}
+UDUP = True
 NR = 2
 VG = [(0, 0, 0), (0, 1, 0)]
-FLAT = 7.0
-FOLD = []
 
 FT = {}
 IT = {}
@@ -35,27 +34,30 @@ def _fields(d, items):
     return o
 
 
-NF = _fields(FT, [("LU", 128), ("CD", 256), ("O", 128), ("As1", 8), ("As2", 64), ("Cb", 128), ("B1", 128), ("C2", 128), ("ABE", 64), ("y", 64)])
-NI = _fields(IT, [("r", 128), ("nh", 64)])
+NF = _fields(FT, [("LU", 128), ("Bs", 128), ("As1", 8), ("As2", 64), ("Cb", 128), ("ABE", 64)])
 
 SCRATCH = {
     "tp": ("sbuf", [128, 256], "int32"), "tsx": ("sbuf", [128, 256], "int32"),
     "tl": ("sbuf", [128, 256], "int32"), "tq": ("sbuf", [128, 256], "int32"),
     "Lnum": ("sbuf", [128, 6 * 256], "int32"), "Loff": ("sbuf", [128, 9 * 256], "uint16"),
-    "Vk": ("sbuf", [128, 8 * 256], "int32"),
-    "Dn": ("sbuf", [128, 6 * 256], "float16"), "eq": ("sbuf", [128, 6 * 256], "float16"),
+    "Vk": ("sbuf", [128, 9 * 256], "int32"),
+    "H0": ("sbuf", [128, 520], "float32"), "H1": ("sbuf", [128, 520], "float32"),
+    "H2": ("sbuf", [128, 512], "float32"), "H3": ("sbuf", [128, 512], "float32"),
+    "res": ("sbuf", [128, 1024], "int32"), "cst": ("sbuf", [128, 12 * 128], "bfloat16"),
+    "xb": ("sbuf", [128, W], "bfloat16"),
+    "i16": ("sbuf", [128, 256], "float16"), "Lh": ("sbuf", [128, 7 * 256], "float16"), "eq": ("sbuf", [128, 6 * 256], "float16"),
     "Rq": ("sbuf", [128, 6 * 256], "float16"),
     "fin": ("sbuf", [128, 1024], "float32"),
     "LoffB": ("sbuf", [128, 512], "uint16"), "VkB": ("sbuf", [128, 512], "int32"), "L5": ("sbuf", [128, 256], "int32"),
-    "R5": ("sbuf", [128, 256], "float16"), "R5B": ("sbuf", [128, 256], "float16"),
-    "tf": ("sbuf", [128, 4 * NF], "float32"), "ti": ("sbuf", [128, 4 * NI], "int32"),
+    "R5": ("sbuf", [128, 256], "int32"), "R5B": ("sbuf", [128, 256], "int32"),
+    "tf": ("sbuf", [128, 4 * NF], "float32"),
     "E0": ("sbuf", [128, 192], "bfloat16"),
     "mmsg": ("sbuf", [128, 12 * 128], "bfloat16"), "mland": ("sbuf", [128, 12 * 64], "bfloat16"),
     "emsg": ("sbuf", [128, 12 * 128], "bfloat16"), "eland": ("sbuf", [128, 12 * 128], "bfloat16"),
     "ETs": ("sbuf", [128, 4 * 192], "bfloat16"), "cj": ("sbuf", [128, 256], "bfloat16"),
     "cz1": ("sbuf", [128, 128], "bfloat16"), "ch": ("sbuf", [128, 128], "bfloat16"), "blkH": ("sbuf", [128, 128], "bfloat16"),
     "Bh": ("sbuf", [128, 144], "bfloat16"), "Bhn": ("sbuf", [128, 144], "bfloat16"),
-    "Ind": ("sbuf", [128, 2048], "bfloat16"), "maskz": ("sbuf", [128, 1024], "bfloat16"),
+    "Ind": ("sbuf", [128, 1024], "bfloat16"), "maskz": ("sbuf", [128, 1024], "bfloat16"),
     "pr0": ("sbuf", [128, 64], "bfloat16"), "pair": ("sbuf", [128, 64], "float32"), "grp8": ("sbuf", [128, 128], "float32"),
     "one": ("sbuf", [128, 1024], "bfloat16"), "idn": ("sbuf", [128, 128], "bfloat16"),
     "nidn": ("sbuf", [128, 128], "bfloat16"), "kidn": ("sbuf", [128, 128], "bfloat16"),
@@ -72,32 +74,33 @@ SCRATCH = {
     "ai": ("sbuf", [128, 6 * 8], "int32"), "af": ("sbuf", [128, 6 * 16], "float32"),
     "junk": ("sbuf", [128, 64], "bfloat16"),
     "R0": ("psum", [128, 1024], "float32"), "R1": ("psum", [128, 1024], "float32"),
-    "SB": ("psum", [128, 512], "float32"), "VB": ("psum", [128, 512], "float32"),
+    "SB": ("psum", [128, 512], "float32"), "DB": ("psum", [128, 512], "float32"),
     "ZB": ("psum", [128, 512], "float32"), "MB": ("psum", [128, 512], "float32"),
 }
 for _t in range(NV - 1):
-    SCRATCH["win%d" % _t] = ("sbuf", [128, WX], "bfloat16")
+    SCRATCH["win%d" % _t] = ("sbuf", [128, WT], "float32")
+    SCRATCH["ext%d" % _t] = ("sbuf", [128, WX], "bfloat16")
 for _z in range(4):
     for _n in ("s", "dp", "ra", "l")[:4 if _z < 3 else 3]:
         SCRATCH["%s%d" % (_n, _z)] = ("sbuf", [128, CH], "bfloat16")
 for _z in range(2):
-    for _n in ("dq", "rq", "vb", "vc", "vo", "sc"):
+    for _n in ("vb", "vc", "sc"):
         SCRATCH["%s%d" % (_n, _z)] = ("sbuf", [128, CH], "bfloat16")
 
-SEMAPHORES = (["sV", "sS", "sP", "sG", "lsem"] + ["w%d" % t for t in range(2, 2 * NV - 2)]
+SEMAPHORES = (["sV", "sS", "sP", "sG", "lsem", "in"] + ["w%d" % t for t in range(2, 2 * NV - 2)]
               + ["m%d" % i for i in range(12)] + ["e%d" % i for i in range(12)]
               + ["ld%d" % i for i in range(12)] + ["mu", "mv", "ml0", "ml1", "mr0", "mr1"] + ["st%d" % i for i in range(10)]
-              + ["ad%d" % i for i in range(12)] + ["fl%d" % i for i in range(12)])
+              + ["ad%d" % i for i in range(14)] + ["x%d" % t for t in range(1, NV - 1)])
 ENGINES = {"fold": lambda en: en[0::2], "small": lambda en: en[len(en) // 2:], "bulk": lambda en: en[:len(en) // 2]}
 
 CYC = 0.83e-3 * 1.15
 PEC = 0.417e-3 * 1.15
 GAM = 1.5
 WAKE = 0.08
-STARTS, SWEEPS, STEPS = 5, 100, (1000, 6000, 6000)
-SEED, SHAKE, SPAN, SOME, HEAT = 2, 6.0, 12.0, 0.2, 0.04
-CASES = [(0.9, 0.8, 1.0, 0.06, 1.0), (0.95, 1.0, 1.5, 0.1, 1.0), (1.1, 1.2, 1.2, 0.08, 1.0), (1.15, 1.0, 1.5, 0.1, 1.55),
-         (0.95, 0.9, 1.0, 0.06, 1.6)]
+LEAD, PACE, OPEN, LEAD0, STRETCH, STRETCH0 = 10.0, 20.0, 20.0, 8.0, 1.0, 1.0
+STARTS, SWEEPS, STEPS = 3, 30, (6000, 45000)
+SEED, SHAKE, SPAN, SOME, HEAT = 2, 6.0, 12.0, 0.2, 0.1
+CASES = [(0.9, 0.85, 1.0, 0.07, 1.0), (1.05, 1.2, 1.4, 0.1, 1.0), (1.0, 1.0, 1.2, 0.08, 1.5)]
 KEPT = {}
 
 
@@ -110,6 +113,7 @@ def rank_program(g, core, T, topo):
     PSUM = [k for k in SCRATCH if SCRATCH[k][0] == "psum"]
     ops = []
     acc = {}
+    lead = [(-1, 0)]
     boost = [1000.0]
 
     def R(b, lo, hi, st=1, p=None):
@@ -127,9 +131,9 @@ def rank_program(g, core, T, topo):
         return r[0] in PSUM
 
     def overlap(a, b):
-        if a[1] >= b[2] or b[1] >= a[2]:
+        if a[1] >= b[2] or b[1] >= a[2] or (a[4] and b[4] and (a[4][0] >= b[4][1] or b[4][0] >= a[4][1]) and a[0] == "Ind"):
             return False
-        if a[3] == b[3] and a[3] > 1 and (a[1] - b[1]) % a[3] != 0:
+        if a[0][0] != "H" and (a[1] - b[1]) % math.gcd(a[3], b[3]) != 0:
             return False
         return True
 
@@ -152,7 +156,7 @@ def rank_program(g, core, T, topo):
                     lst[:] = [x for x in lst if x[0] == k or not (x[1][1] >= r[1] and x[1][2] <= r[2])]
                 lst.append((k, r, w))
         ops.append({"eng": eng, "wr": wr, "banks": sorted(banks), "emit": emit, "dep": dep, "occ": occ, "lat": occ + 0.03 if lat is None else lat,
-                    "sem": sem, "inc": inc, "boost": boost[0] + FIRST.get((wr[0][0] if wr else "-").rstrip("0123456789"), 0.0)})
+                    "sem": sem, "inc": inc, "lead": lead[0], "boost": boost[0] + FIRST.get((wr[0][0] if wr else "-").rstrip("0123456789"), 0.0)})
         return k
 
     def vcost(n, f=1.0):
@@ -233,7 +237,7 @@ def rank_program(g, core, T, topo):
         for x in rd:
             key = x[0]
             if key in rd2:
-                rd2[key] = (key, min(rd2[key][1], x[1]), max(rd2[key][2], x[2]), 1, None)
+                rd2[key] = (key, min(rd2[key][1], x[1]), max(rd2[key][2], x[2]), 1, x[4] if x[4] == rd2[key][4] else None)
             else:
                 rd2[key] = x
         return op("P", em, list(rd2.values()), wr, cost + 0.01, cost + 0.1)
@@ -284,62 +288,70 @@ def rank_program(g, core, T, topo):
         return k
 
     def send_columns(t, X, deps=()):
-        a, b = X * WX // 2, (X + 1) * WX // 2
-        send(rank - HOP * t, R("win%d" % t, a, b), R("win0", a, b), "w%d" % (2 * t + X), 9.0, use="bulk", deps=deps)
+        a, b = (0, W // 2, WT)[X:X + 2]
+        send(rank - HOP * t, R("win%d" % t, a, b), R("win0", a, b), "w%d" % (2 * t + X), 12.0, use="bulk", deps=deps)
+        if X == 1:
+            send(rank - HOP * t, R("ext%d" % t, 0, WX), R("ext0", 0, WX), "x%d" % t, deps=deps)
 
     I, NIDN, KI, NKI = R("idn", 0, 128), R("nidn", 0, 128), R("kidn", 0, 128), R("nkidn", 0, 128)
     ONE, BLK, ONE64 = R("one", 0, 128), R("blk", 0, 128), R("one", 0, 64)
-    load("S", R("tsx", 0, 128), "sl", 2.4)
-    load("S", R("tl", 0, 128), "ll", 2.7)
-    load("Y", R("win0", 0, W), "xt", 4.5)
-    load("Y", R("E0", 0, 128), "ed", 4.7)
-    for j, (b, nm) in enumerate((("tp", "pl"), ("tq", "ql"))):
-        load("Y", R(b, 0, 128), nm, 5.0 + 0.3 * j)
-    load("Y", R("wti", 0, 1), "wt", 5.5)
-    load("Y", R("thi", 0, 1), "th", 5.7)
-    for j, (b, nm) in enumerate((("tsx", "sl"), ("tp", "pl"), ("tl", "ll"), ("tq", "ql"))):
-        load("Y", R(b, 128, 256), nm, 6.0 + 0.3 * j)
+    HALF, K5, NK5, CK, CQ, CM, CN, CX, CK1, CN1, NM1, HM1 = [R("cst", 128 * j, 128 * j + 128) for j in range(12)]
+    load("Y", R("xb", 0, W), "xt", 3.9)
+    for j, (b, nm) in enumerate((("tsx", "sl"), ("tl", "ll"), ("tp", "pl"), ("tq", "ql"))):
+        load("Y", R(b, 0, 256), nm, 4.5 + 0.6 * j)
+    load("Y", R("wti", 0, 1), "wt", 6.6)
+    load("Y", R("E0", 0, 128), "ed", 6.9)
+    load("Y", R("thi", 0, 1), "th", 7.1)
     vset(R("one", 0, 128), 1.0)
-    vset(R("win0", W + 128, WX), 0.0)
+    vset(R("win0", W, WT), 0.0)
     gsel(R("blk0", 0, 128), ONE, [[-16, 8], [0, 16]], OP.is_ge, 0, 1)
     gsel(BLK, R("blk0", 0, 128), [[16, 8], [0, 16]], OP.is_ge, 15, -1)
     gsel(I, ONE, [[-1, 128]], OP.is_equal, 0, 1)
-    vcopy(R("tcf", 0, 1), R("wti", 0, 1))
-    vts(R("tci", 0, 1), R("thi", 0, 1), -1, OP.add)
-    vts(R("tci", 4, 5), R("tci", 0, 1), 4, OP.arith_shift_right)
-    vts(R("tci", 8, 9), R("tci", 0, 1), 15, OP.bitwise_and)
-    vts(R("win0", W + 128, W + 129), R("tci", 4, 5), -16.0 * BIG, OP.mult)
-    vts(R("win0", W + 129, W + 130), R("tci", 8, 9), -BIG, OP.mult)
-    vts(R("win0", W, W + 128), BLK, R("tcf", 0, 1), OP.mult, 1.0 / 2048.0, OP.mult)
-    send_columns(1, 0)
-    send_columns(1, 1)
     boost[0] = 0.0
+    vcopy(R("tcf", 0, 1), R("wti", 0, 1))
+    vts(R("af", 12, 13), R("thi", 0, 1), -1.0, OP.add, -BIG, OP.mult)
+    vts(R("win0", W, W + 1), R("thi", 0, 1), -1.0 - TOP / 4.0, OP.add, -BIG, OP.mult)
+    vts(R("ext0", 0, 128), BLK, R("tcf", 0, 1), OP.mult, 1.0 / 2048.0, OP.mult)
+    for h in range(2):
+        a, b = R("win0", 1024 * h, 1024 * h + 1024), R("xb", 1024 * h, 1024 * h + 1024)
+        if h in ONV["W"]:
+            vts(a, b, -128.0, OP.add, HUGE + 1.0, OP.mult)
+        else:
+            act(a, b, AF.Identity, HUGE + 1.0, -128.0 * (HUGE + 1.0))
+        send_columns(1, h)
     vset(R("one", 128, 1024), 1.0)
     op("G", lambda e: [e.iota(ap(R("kin", 0, 1)), [[0, 1]], 0, 1)], [], [R("kin", 0, 1)], 0.2)
-    for h in range(2):
-        gsel(R("Ind", 1024 * h, 1024 * h + 1024, 1, (0, 64)), R("one", 0, 1024, 1, (0, 64)), [[-1, 32], [0, 32]], OP.is_equal, -32 * h, 1)
-    for out, src, c in ((NIDN, I, -1.0), (KI, I, HUGE), (NKI, I, -HUGE),
-                        (R("blkE", 0, 128), BLK, BIG / HUGE), (R("blkP", 0, 128), BLK, BIG), (R("blkH", 0, 128), BLK, -BIG * HUGE),
-                        (R("cz1", 0, 128), ONE, BIG * HUGE * 31.75 / 128.0), (R("ch", 0, 128), ONE, BIG * HUGE / 256.0),
+    IND = [R("Ind", 0, 1024, 1, (32 * h, 32 * h + 32)) for h in range(2)]
+    gsel(IND[0], R("one", 0, 1024, 1, (0, 32)), [[-1, 32], [0, 32]], OP.is_equal, 0, 1)
+    op("Y", lambda e: [e.dma_start(out=ap(IND[1]), in_=ap(IND[0]))], [IND[0]], [IND[1]], 0.05, 3.0, sem="in", inc=16)
+    for out, src, c in ((NIDN, I, -1.0), (NM1, I, -1.0 / HUGE), (HM1, I, 0.5 / HUGE),
+                        (R("blkP", 0, 128), BLK, BIG),
+                        (R("cz1", 0, 128), ONE, -BIG * HUGE * 31.75 / 128.0),
                         (R("blkN", 0, 128), BLK, -BIG), (R("blk2", 0, 128), BLK, 2.0),
-                        (R("cz", 0, 128), ONE, -BIG / 512.0),
-                        (R("o32", 0, 128), ONE, 1.0 / 32.0),
-                        (R("cc", 0, 128), ONE, -15.5 / 8192.0)):
+                        (R("cz", 0, 128), ONE, -BIG * 31.75 / 128.0),
+                        (R("o32", 0, 128), ONE, -1.0 / 32.0),
+                        (R("cc", 0, 128), ONE, -15.5 / 8192.0),
+                        (HALF, I, 0.5), (K5, I, 512.0), (NK5, I, -512.0), (CQ, ONE, -1.0 / 512.0),
+                        (CM, ONE, WHOLE23 / 128.0), (CX, ONE, TOP / 128.0)):
         act(out, src, AF.Copy, c)
+    for out, c in ((CN, 8.0), (CN1, 9.0)):
+        vset(out[:4] + ((0, 64),), -WHOLE23 / 64.0)
+        vset(out[:4] + ((64, 128),), c)
+    I16, N16 = R("i16", 0, 128), R("i16", 128, 256)
+    vcopy(I16, I)
+    vts(N16, I, -1.0, OP.mult)
+    vset(R("DB", 0, 512, 4), 0.0)
     vset(R("Bp", 0, 144), 0.0)
     vts(R("Bp", 15, 128, 16), R("blk", 0, 128, 16), BIG, OP.mult)
     act(R("Bn", 0, 144), R("Bp", 0, 144), AF.Copy, -1.0)
-    act(R("Be", 0, 144), R("Bp", 0, 144), AF.Copy, 1.0 / HUGE)
-    act(R("Bh", 0, 144), R("Bp", 0, 144), AF.Copy, HUGE)
-    act(R("Bhn", 0, 144), R("Bp", 0, 144), AF.Copy, -HUGE)
+    act(R("Be", 0, 144), R("Bp", 0, 144), AF.Copy, -4.0 / BIG)
     vset(R("cu", 0, 128, 1, (0, 64)), 129.0 / 64.0)
     vset(R("cu", 0, 128, 1, (64, 128)), 2.0 ** -12)
-    vset(R("cj", 0, 128, 1, (0, 64)), 2.0)
+    vset(R("cj", 0, 128, 1, (0, 64)), 2.0 ** -18)
     vset(R("cj", 0, 128, 1, (64, 128)), 1.0 / 128.0)
-    vset(R("cj", 128, 256), 2.0 ** -19)
     vset(R("E0", 128, 192), 0.0)
-    op("G", lambda e: [e.iota(ap(R("maskz", 0, 1024)), [[0, 32], [256, 32]], 0, 0, allow_small_or_imprecise_dtypes=True)],
-       [], [R("maskz", 0, 1024)], 0.15 + 2 * 1024 * CYC)
+    vset(R("maskz", 0, 1024), 256.0 * HUGE)
+    vset(R("maskz", 0, 1024, 32), -256.0 * HUGE)
     P8 = (0, 8)
     gsel(R("pr0", 0, 64), ONE64, [[-2, 64]], OP.is_ge, 0, 1)
     gsel(R("pair", 0, 64), R("pr0", 0, 64), [[2, 64]], OP.is_ge, 1, -1)
@@ -347,7 +359,7 @@ def rank_program(g, core, T, topo):
     gsel(R("grp8", 0, 128, 1, P8), R("blk0", 0, 128, 1, P8), [[-1, 128]], OP.is_ge, 15, 16)
     vts(R("kin", 8, 9), R("kin", 0, 1), 15, OP.bitwise_and)
     for h in range(2):
-        c = 37.0 * 16 * h + 2048.0 - 31.0 / 64.0
+        c = 37.0 * 16 * h + 8 * 2048.0 - 31.0 / 64.0
         vts(R("k37", h, h + 1), R("kin", 8, 9), 37.0, OP.mult, c, OP.add)
         vts(R("k37", 2 + h, 3 + h), R("kin", 8, 9), 37.0, OP.mult, c + 15.5, OP.add)
 
@@ -363,11 +375,18 @@ def rank_program(g, core, T, topo):
         return R(b, o, o + 128) if h is None else R(b, o + 64 * h, o + 64 * h + 64)
 
     def Vk(k, X):
-        b, o = ("VkB", (k - 3) * 256 + 128 * X) if moved[0] else ("Vk", (k + 3) * 256 + 128 * X)
+        b, o = ("VkB", (k - 3) * 256 + 128 * X) if moved[0] and k < NV - 1 else ("Vk", (k + 3) * 256 + 128 * X)
         return R(b, o, o + 128)
 
+    def Lh(k, X):
+        return R("Lh", (k + 1) * 256 + 128 * X, (k + 1) * 256 + 128 * X + 128)
+
     def voff(k):
-        return OFF + 2048.0 * (8 - (k if k > -3 else -1))
+        return 2048.0 * (2 + (k if k > -3 else -1))
+
+    def steps(t, X, j=None):
+        b, o = ("H%d" % (2 + X), 0) if t == NV - 1 else ("H%d" % X, NV - t)
+        return R(b, o, o + 512) if j is None else R(b, o + j, o + 512, 4)
 
     def gcopy(out, a):
         gsel(out, a, [[0, n_of(out)]], OP.is_ge, 0, 0)
@@ -379,18 +398,12 @@ def rank_program(g, core, T, topo):
         nadd[0] += 1
 
     def make_v(k, X, src):
-        if not GCONV:
-            vts(Vk(k, X), src, voff(k), OP.add)
-        elif k > 0:
-            add_into(Vk(k, X), ap(src), [src])
-        elif X == 0:
-            add_into(R("Vk", (k + 3) * 256, (k + 4) * 256), T[("ql", "pl", "sl", "ll")[k + 3]][:], [])
+        add_into(Vk(k, X), ap(src), [src])
 
-    if GCONV:
-        for lo, hi in ((-3, -2), (-2, 1), (1, 5)):
-            v = R("Vk", (lo + 3) * 256, (hi + 3) * 256)
-            op("G", lambda e, v=v, lo=lo, hi=hi: [e.iota(ap(v), [[-2048, hi - lo], [0, 256]], int(voff(lo)), 0)], [], [v],
-               0.15 + 2 * n_of(v) * CYC)
+    for lo, hi in ((k, k + 1) for k in range(1, NV)):
+        v = R("Vk", (lo + 3) * 256, (hi + 3) * 256)
+        op("G", lambda e, v=v, lo=lo, hi=hi: [e.iota(ap(v), [[2048, hi - lo], [0, 256]], int(voff(lo)), 0)], [], [v],
+           0.15 + 2 * n_of(v) * CYC)
 
     def slot(b, X, j):
         return R(b, 768 * X + j, 768 * X + 768, 6)
@@ -400,14 +413,16 @@ def rank_program(g, core, T, topo):
 
     for X in range(2):
         for k in (-1, -2, 0, -3):
-            (gcopy if GCOPY and (X == 1 or k < -1) else vcopy)(Lu(k, X), Ln(k, X))
-        for k in (-2, -3, -1, 0):
-            make_v(k, X, Ln(k, X))
-        vtt(slot("Dn", X, 0), Ln(-3, X), Ln(0, X), OP.subtract)
+            (gcopy if X == 1 or k < -1 else vcopy)(Lu(k, X), Ln(k, X))
+        for j, k in ((1, 0), (2, -3)):
+            vts(steps(0, X, j), Ln(k, X), voff(k), OP.add)
+        gcopy(steps(0, X, 3), Ln(-2, X))
+        gcopy(Lh(-1, X), Ln(-3, X))
+        gcopy(Lh(0, X), Ln(0, X))
 
     def sums(out, parts, more=()):
-        pe(group(out, [(R(coef, 15 - i, 143 - i), R(tile[0], tile[1] + i, tile[2], 16)) for (coef, tile) in parts for i in range(16)]
-                 + list(more)))
+        pe(group(out, list(more)
+                 + [(R(coef, 15 - i, 143 - i), R(tile[0], tile[1] + i, tile[2], 16)) for (coef, tile) in parts for i in range(16)]))
 
     nreg = [0]
 
@@ -426,25 +441,22 @@ def rank_program(g, core, T, topo):
     for t in range(NV):
         last = t == NV - 1
         moved[0] = last
-        wn = "win%d" % (0 if last else t)
-        WIN = R(wn, 0, W)
-        TH = R("af", 12, 13) if last else R("af", t * 16 + 12, t * 16 + 13)
-        if not last:
-            act(TH, R(wn, W + 128, W + 129), AF.Identity, None, R(wn, W + 129, W + 130))
+        wn = "ext%d" % (0 if last else t)
+        WIN = R("win%d" % (0 if last else t) if t else "xb", 0, W)
+        TH = R(WIN[0], W, W + 1) if t else R("af", 12, 13)
         for X in range(2):
             z, y, sl = (t % 2) * 2 + X, X, 2 * t + X
+            lead[0] = (t, X)
             kind = "SS" if t == 0 else KIND.get((t, X), KIND[X])
 
             def F(nm, lo=0, hi=None):
                 o, n = FT[nm]
                 return R("tf", z * NF + o + lo, z * NF + o + (n if hi is None else hi))
 
-            def J(nm):
-                o, n = IT[nm]
-                return R("ti", z * NI + o, z * NI + o + n)
-
             def tile(nm, h):
                 q = z if nm in ("s", "dp", "ra") else sl % 3 if nm == "l" else y
+                if nm in ("dq", "rq", "vo"):
+                    nm, q = {"dq": "s", "rq": "dp", "vo": "ra"}[nm], 2 + y
                 return R("%s%d" % (nm, q), 0, CH) if h is None else R("%s%d" % (nm, q), 1024 * h, 1024 * h + 1024)
 
             E = R("E0", 64 * X, 64 * X + 64) if t == 0 else R("eland", (sl - 2) * 128, (sl - 2) * 128 + 64)
@@ -453,7 +465,7 @@ def rank_program(g, core, T, topo):
                 if kind[h] == "S":
                     gath_s(tile("s", h), WIN, Lu(t - 1, X, h))
                     gath_sub(tile("dp", h), WIN, Lu(t - 2, X, h), tile("s", h))
-                    relu2(tile("ra", h), tile("dp", h), HUGE)
+                    relu2(tile("ra", h), tile("dp", h))
                     if t == 0:
                         gath_sub(tile("dq", h), WIN, Lu(-3, X, h), tile("s", h))
                         if X in DABS:
@@ -481,15 +493,24 @@ def rank_program(g, core, T, topo):
             km = send(rank + 4, MR, M, "m%d" % sl)
             if t + 2 < NV - 1:
                 send_columns(t + 2, X, (km,))
-            WM = R(wn, W, W + 128)
-            pe(group(R("MB", 0, 128), [(R(E[0], E[1], E[1] + 128), NIDN)]) + group(R("MB", 128, 192), [(WM, E), (R("cj", 0, 128), ONE64), (R("cj", 128, 256), ONE64)]))
-            ET = R("ETs", z * 192, z * 192 + 128, 1, (0, 64))
+            WM = R(wn, 0, 128)
+            pe(group(R("MB", 0, 128), [(R(E[0], E[1], E[1] + 128), NIDN)])
+               + group(R("MB", 128, 192), [(WM, E), (R("cj", 0, 128), ONE64)] + ([] if t else [(ONE, ONE64)])))
             JU = R("ETs", z * 192 + 128, z * 192 + 192)
-            act(R("ETs", z * 192, z * 192 + 192), R("MB", 0, 192), AF.Copy)
-            U = R("MB", 192, 256)
-            pe(group(U, [(WM, E), (NIDN, JU), (R("cu", 0, 128), ONE64)]))
-            for h in range(2):
-                vtt(every(F("LU"), h), every(L, h), U, OP.mult)
+            if (t, X) in ONV["ET"]:
+                vts(R("ETs", z * 192, z * 192 + 192), R("MB", 0, 192), 128.0 if t else 0.0, OP.add)
+            else:
+                act(R("ETs", z * 192, z * 192 + 192), R("MB", 0, 192), AF.Identity, None, 128.0 if t else 0.0)
+            us = [(WM, E), (NIDN, JU), (R("cu", 0, 128), ONE64)]
+            if UDUP:
+                U = R("MB", 192, 320)
+                pe([m for h in range(2) for m in group(every(U, h), us)])
+                vtt(F("LU"), L, U, OP.mult)
+            else:
+                U = R("MB", 192, 256)
+                pe(group(U, us))
+                for h in range(2):
+                    vtt(every(F("LU"), h), every(L, h), U, OP.mult)
             if t == 0:
                 colA = R("k37", 0, 2)
             else:
@@ -503,43 +524,35 @@ def rank_program(g, core, T, topo):
                     x32 = R("af", t * 16 + 4, t * 16 + 5)
                     vts(x32, xa, 1.5 * 2.0 ** 28, OP.add, -1.5 * 2.0 ** 28, OP.add)
                     vts(colA, R("k37", 2, 4), xa, OP.add, x32, OP.subtract)
-            GA = R("VB", 128 * X, 128 * X + 128)
-            for h in range(2):
-                col = R(colA[0], colA[1] + h, colA[1] + h + 1)
-                if (t, X) in CHS:
-                    act(every(GA, h), every(F("LU"), h), AF.Identity, 64.0, col)
-                else:
-                    vts(every(GA, h), every(F("LU"), h), 64.0, OP.mult, col, OP.add)
-            pe(group(R("MB", 320, 384), [(I, E), (NIDN, MR)]) + group(R("MB", 384, 448), [(I, E), (I, MR)]))
-            act(F("ABE"), R("MB", 320, 384), AF.Abs)
-            vts(J("nh"), R("MB", 384, 448), -0.5, OP.mult, 0.25, OP.add)
-            Z = R("ZB", 0, 64)
-            B, C, D, O = [R("SB", 128 * j, 128 * j + 128) for j in range(4)]
+            def half_of(j, h):
+                return R("DB", j + 4 * h, 512, 8)
 
             for h in range(2):
-                ind = R("Ind", 1024 * h, 1024 * h + 1024, 1, (0, 64))
+                vts(half_of(1, h), every(F("LU"), h), 64.0, OP.mult, R(colA[0], colA[1] + h, colA[1] + h + 1), OP.add)
+            Z = R("ZB", 0, 64)
+            C, B, D, O = [R("SB", 128 * j, 128 * j + 128) for j in range(4)]
+
+            for h in range(2):
+                ind, ET = IND[h], R("ETs", z * 192, z * 192 + 128, 1, (32 * h, 32 * h + 32))
                 if t == 0:
                     size(tile("vc", h), [(I, tile("s", h)), (I, tile("dp", h)), (NIDN, tile("l", h))])
                     size(tile("vo", h), [(I, tile("l", h)), (ET, ind)])
                     size(tile("vb", h), [(I, tile("s", h)), (NIDN, tile("l", h))])
-                elif kind[h] == "S":
-                    size(tile("vc", h), [(KI, tile("s", h)), (KI, tile("dp", h)), (NKI, tile("l", h))])
-                    size(tile("vb", h), [(KI, tile("s", h)), (NKI, tile("l", h)), (I, tile("l", h)), (ET, ind)])
                 else:
-                    size(tile("ra", h), [(KI, tile("dp", h)), (NKI, tile("s", h))])
-                    size(tile("vb", h), [(KI, tile("s", h)), (I, tile("l", h)), (ET, ind)])
+                    size(tile("vb", h), [(I, tile("s", h)), (ET, ind)])
+                    size(tile("ra", h), [(I, tile("dp", h)), (NIDN, tile("s", h))])
             A1, A2 = R("ZB", 64, 72), R("ZB", 128, 192, 1, P8)
             AS2 = F("As2")[:4] + (P8,)
             zs = [(R("cz1" if t else "cz", 0, 128), ONE64)]
             if (t, X) in AST:
                 pe(group(A1, [(R(tile(nm, None)[0], i, CH, 16), R(coef, 0, 128, 16))
-                              for (coef, nm) in ((("blkP", "ra"),) if t else (("blkE", "ra"), ("blkN", "dp"))) for i in range(16)]))
+                              for (coef, nm) in ((("blkP", "ra"),) if t else (("blkP", "ra"), ("blkN", "dp"))) for i in range(16)]))
                 act(F("As1"), A1, AF.Copy)
                 pe(group(A2, [(F("As1"), R("pair", 0, 64))]))
-                act(AS2, A2, AF.Copy)
+                act(AS2, A2, AF.Copy, -1.0)
                 zs.append((R("grp8", 0, 128, 1, P8), AS2))
             else:
-                zs += [(R("blkP", 0, 128), R(tile("ra", None)[0], k, CH, 32)) for k in range(32)]
+                zs += [(R("blkN", 0, 128), R(tile("ra", None)[0], k, CH, 32)) for k in range(32)]
                 pe([m[:4] + (False,) for m in group(Z, zs)])
 
             def part(r, h):
@@ -547,73 +560,76 @@ def rank_program(g, core, T, topo):
 
             if t == 0:
                 sums(D, [("Bp", tile("rq", None))] + ([] if X in DABS else [("Bn", tile("dq", None))]))
-                sums(C, [("Bp", tile("vc", None))])
-                act(F("CD"), R("SB", 128, 384), AF.Copy)
+                sums(B, [("Bp", tile("vb", None))])
+                act(F("Bs"), B, AF.Identity, None, -BIG / 2.0)
                 sums(O, [("Bp", tile("vo", None))])
-                for h in range(2):
-                    sums(part(B, h), [("Bp", tile("vb", h))])
-                act(F("O"), O, AF.Identity, None, TH)
-                vtt(F("Cb"), B, F("CD", 0, 128), OP.subtract)
+                act(steps(t, X, 0), O, AF.Identity, None, TH)
+                vtt(R("DB", 2, 512, 4), D, F("Bs"), OP.subtract)
+                sums(C, [("Bp", tile("vc", None))])
+                vtt(F("Cb"), C, F("Bs"), OP.subtract)
             else:
-                sums(C, [("Bh", tile("vc", None))], [(R("ch", 0, 128), ONE)])
+                for h in parts("vc"):
+                    sums(C if h is None else part(C, h), [("Bp", tile("vc", h))] + ([("Bn", tile("dp", h))] if kind[h or 0] == "L" else []))
                 for h in range(2):
-                    sums(part(B, h), [("Be", tile("vb", h))])
-                act(F("O"), B, AF.Identity, HUGE, TH)
-                vtt(F("Cb"), F("O"), C, OP.subtract)
+                    sums(R("DB", 2 + 256 * h, 256 + 256 * h, 4), [("Be", tile("vb", h))], [(CX, ONE64)])
+                if (t, X) in ONV["O"]:
+                    vts(steps(t, X, 0), R("DB", 2, 512, 4), -BIG / 4.0, OP.mult, TH, OP.add)
+                else:
+                    act(steps(t, X, 0), R("DB", 2, 512, 4), AF.Identity, -BIG / 4.0, TH)
+                vtt(F("Bs"), C, steps(t, X, 0), OP.subtract)
+                vts(F("Cb"), F("Bs"), WHOLE23 * BIG * HUGE / 4.0, OP.add, (2.0 - WHOLE23) * BIG * HUGE / 4.0, OP.add)
             zc = group(Z, [(R("blk2", 0, 128), every(F("Cb"), 0)), (R("blk2", 0, 128), every(F("Cb"), 1))])
             zc[0] = zc[0][:3] + (False, False)
             pe(([m[:4] + (False,) for m in group(Z, zs)] if (t, X) in AST else []) + zc)
-            PB, XC = R("VB", 256, 384), R("VB", 384, 448)
-            if t == 0:
-                vtt(PB, B, F("CD", 128, 256), OP.subtract)
-                vtt(F("B1"), Vk(-3, X), PB, OP.min)
-            else:
-                vtt(F("B1"), Vk(t - 1, X), B, OP.min)
-            vtt(GA, F("O"), GA, OP.min)
-            vtt(GA, L, GA, OP.max)
-            vtt(GA, F("B1"), GA, OP.max)
             for h in range(2):
-                vtt(every(PB, h), every(Vk(t - 2, X), h), Z, OP.min)
-            vtt(F("C2"), F("Cb"), PB, OP.min)
-            vtt(J("r"), F("C2"), GA, OP.max)
+                vtt(half_of(3, h), every(F("Cb"), h), Z, OP.max)
+            vscan(R("res", 512 * X, 512 * X + 512), R("DB", 0, 512), steps(t, X), OP.min, OP.max)
             move = t == NV - 2
             home = rank + HOP * (NV - 1)
             NEW = R("L5", 128 * X, 128 * X + 128) if move else Ln(t + 1, X)
-            vts(NEW, J("r"), 2047, OP.bitwise_and)
+            vts(NEW, R("res", 512 * X + 3, 512 * X + 512, 4), 2047, OP.bitwise_and)
             if move:
                 send(home, Ln(t + 1, X), NEW, "ml%d" % X)
             if not last:
-                (gcopy if GCOPY > 1 else vcopy)(Lu(t + 1, X), Ln(t + 1, X))
-            EM = R("emsg", sl * 128, sl * 128 + 64)
-            vtt(XC, F("ABE"), Z, OP.min)
-            vtt(F("y"), J("nh"), XC, OP.max)
-            if not last:
-                act(R("emsg", sl * 128 + 64, sl * 128 + 128), Z, AF.Sign)
-            act(EM, F("y"), AF.Abs)
+                gcopy(Lu(t + 1, X), Ln(t + 1, X))
+            EM, SG = R("emsg", sl * 128, sl * 128 + 64), R("emsg", sl * 128 + 64, sl * 128 + 128)
+            act(SG, Z, AF.Sign)
+            X1, X2 = R("MB", 320, 384), R("MB", 384, 448)
+            pe(group(X1, [(I, E), (NM1 if t else NIDN, MR), (K5, SG)])
+               + group(X2, [(HALF, E), (HM1 if t else HALF, MR), (CQ, ONE64), (CM, ONE64), (NK5, SG), (CN1 if t else CN, ONE64)]))
+            act(F("ABE"), X1, AF.Abs, None, 384.0 if t else 512.0)
+            vtt(EM, F("ABE"), X2, OP.min)
             if not last:
                 send(rank + HOP * t if move else rank - HOP, R("eland", sl * 128, sl * 128 + 128), R("emsg", sl * 128, sl * 128 + 128),
                      "e%d" % sl)
-            if t + 1 <= NV - 2:
-                make_v(t + 1, X, NEW)
+                make_v(t + 1, X, Ln(t + 1, X))
+                gcopy(steps(t + 1, X, 1), Vk(t + 1, X))
+            if t == 0:
+                vts(steps(1, X, 3), Ln(-1, X), voff(-1), OP.add)
             if t == NV - 3 and X == 1:
                 send(home, R("LoffB", 0, 512), R("Loff", (t + 3) * 256, (t + 5) * 256), "mu", 4.5, use="bulk")
                 send(home, R("VkB", 0, 512), R("Vk", (t + 3) * 256, (t + 5) * 256), "mv", 7.0, use="bulk")
                 vts(R("fin", 0, 256), R("VkB", 256, 512), -voff(t + 1), OP.add)
                 store("Y", "yp", 0, 256, R("fin", 0, 256), "st0")
+                for j in range(4):
+                    gcopy(steps(NV - 1, j % 2, 3 - j // 2), R("VkB", 128 * j, 128 * j + 128))
             if not last:
-                vtt(slot("Dn", X, t + 1), L, NEW, OP.subtract)
+                gcopy(Lh(t + 1, X), NEW)
             if move:
-                a, b = 768 * X, 768 * X + 768
-                vts(R("eq", a, b), R("Dn", a, b), 0.0, OP.is_equal)
-                vset(slot("eq", X, 0), 0.0)
-                vscan(R("Rq", a, b), R("eq", a, b), R("Dn", a, b), OP.mult, OP.add)
+                for h in range(2):
+                    a, b = 768 * X + 384 * h, 768 * X + 384 * h + 384
+                    pe([m for j in range(NV) for m in group(R("SB", 128 + j, 512, 6), [(I16, part(Lh(j - 1, X), h)), (N16, part(Lh(j, X), h))]
+                                                            + ([] if j else [(CQ, ONE64)]))])
+                    vts(R("eq", a, b), R("SB", 128, 512), 0.0, OP.is_equal)
+                    vscan(R("Rq", a, b), R("eq", a, b), R("SB", 128, 512), OP.mult, OP.add)
                 gcopy(R("R5", 128 * X, 128 * X + 128), slot("Rq", X, 5))
                 send(home, R("R5B", 128 * X, 128 * X + 128), R("R5", 128 * X, 128 * X + 128), "mr%d" % X)
-                (gcopy if GCOPY else vcopy)(R("fin", 256 + 128 * X, 384 + 128 * X), Ln(t + 1, X))
+                gcopy(R("fin", 256 + 128 * X, 384 + 128 * X), Ln(t + 1, X))
                 store("Y", "ys", 128 * X, 128 * X + 128, R("fin", 256 + 128 * X, 384 + 128 * X), "st%d" % (1 + 4 * X))
             if last:
                 FL, FQ = R("fin", 512 + 128 * X, 640 + 128 * X), R("fin", 768 + 128 * X, 896 + 128 * X)
                 vcopy(FL, NEW)
+                PB = R("SB", 256, 384)
                 vtt(PB, NEW, L, OP.is_equal)
                 vtt(PB, R("R5B", 128 * X, 128 * X + 128), PB, OP.mult)
                 vtt(FQ, L, PB, OP.add)
@@ -629,6 +645,8 @@ def rank_program(g, core, T, topo):
     prio = [0.0] * n
     for k in range(n - 1, -1, -1):
         prio[k] = ops[k]["lat"] + max([prio[s] + 0.08 for s in succ[k]] + [0.0])
+
+    KEPT["ops"], KEPT["prio"], KEPT["succ"] = ops, prio, succ
 
     def place(key, back):
         before, after = (succ, pred) if back else (pred, succ)
@@ -728,9 +746,22 @@ def rank_program(g, core, T, topo):
             c = [dma if o["sem"] else f * (gam if o.get("gather") else ten if o["eng"] == "P" else 1.0) for o in ops]
             scaled.append(([occ[k] * c[k] for k in range(n)], [lat[k] * c[k] + wake for k in range(n)]))
         rng = np.random.default_rng(SEED)
+        alone = [0.0] * n
+        for tag in sorted({o["lead"] for o in ops}):
+            mine = [k for k in range(n) if ops[k]["lead"] == tag]
+            free, fin = {}, {}
+            for k in sorted(mine, key=lambda q: (-prio[q], q)):
+                s = max([free.get(eng[k], 0.0)] + [fin[q] for q in pred[k] if q in fin])
+                if eng[k] != "N":
+                    free[eng[k]] = s + occ[k]
+                fin[k] = s + lat[k] + WAKE
+                alone[k] = s
+            t, X = tag
+            for k in mine:
+                alone[k] = alone[k] * (STRETCH if t else STRETCH0) + (OPEN + PACE * (t - 1) + LEAD * X if t > 0 else LEAD0 * X if t == 0 else -20.0)
 
         def packed():
-            key = {k: (-prio[k] * ("first" not in ops[k]) - early[k], k) for k in range(n)}
+            key = {k: (alone[k] * ("first" not in ops[k]) - early[k], k) for k in range(n)}
             best = None
             for sweep in range(SWEEPS):
                 at = place(key, False)
@@ -746,9 +777,62 @@ def rank_program(g, core, T, topo):
                 key = {k: (was[k] * ("first" not in ops[k]) - early[k], k) for k in range(n)}
             return sorted(range(n), key=lambda q: (best[1][q], q))
 
-        def moved_on(order, steps):
+        (oc0, la0), (oc1, la1), (oc2, la2) = scaled
+        wt = [1.0 / (3.0 * f * (0.6 + 0.4 * gam)) for (f, gam, dma, wake, ten) in CASES]
+        seat = [[(b, eng[k]) for b in bank[k]] for k in range(n)]
+        rival = [[(b, e) for b in bank[k] for e in "VSP" if e != eng[k]] for k in range(n)]
+
+        def onward(order, a, was):
+            f0, f1, f2, waits, ahead = [x[:] for x in was]
+            last, lu = {}, {}
+            for k in order[max(0, a - 120):a]:
+                last[eng[k]] = k
+                for x in seat[k]:
+                    lu[x] = k
+            for k in order[a:]:
+                e, w = eng[k], pred[k]
+                if seat[k]:
+                    w = w + [lu[x] for x in rival[k] if x in lu]
+                    for x in seat[k]:
+                        lu[x] = k
+                q = last.get(e) if e != "N" else None
+                last[e] = k
+                waits[k], ahead[k] = w, q
+                if q is None:
+                    s0 = s1 = s2 = 0.0
+                else:
+                    s0, s1, s2 = f0[q] - la0[q] + oc0[q], f1[q] - la1[q] + oc1[q], f2[q] - la2[q] + oc2[q]
+                for q in w:
+                    if f0[q] > s0:
+                        s0 = f0[q]
+                    if f1[q] > s1:
+                        s1 = f1[q]
+                    if f2[q] > s2:
+                        s2 = f2[q]
+                f0[k], f1[k], f2[k] = s0 + la0[k], s1 + la1[k], s2 + la2[k]
+            return wt[0] * max(f0) + wt[1] * max(f1) + wt[2] * max(f2), (f0, f1, f2, waits, ahead)
+
+        def tied(state):
             ties = []
-            now = replay(order, ties)
+            for fin, (oc, la) in zip(state, scaled):
+                k = fin.index(max(fin))
+                while True:
+                    s, y = fin[k] - la[k] - 1e-9, None
+                    for q in state[3][k]:
+                        if fin[q] >= s:
+                            y = q
+                    if y is None:
+                        y = state[4][k]
+                        if y is None or fin[y] - la[y] + oc[y] < s:
+                            break
+                    if y not in ops[k]["dep"] and "first" not in ops[k]:
+                        ties.append((y, k))
+                    k = y
+            return ties
+
+        def moved_on(order, steps, heat):
+            now, state = onward(order, 0, [[0.0] * n] * 5)
+            ties = tied(state)
             best = (now, order)
             for step in range(steps):
                 j, k = ties[int(rng.integers(len(ties)))]
@@ -770,17 +854,18 @@ def rank_program(g, core, T, topo):
                     if k in take:
                         continue
                     mid = [q for q in mid if q not in take] + [q for q in mid if q in take]
-                new, t2 = order[:a] + mid + order[b + 1:], []
-                end = replay(new, t2)
-                if end < now + HEAT * (1.0 - step / steps) * -math.log(1.0 - rng.random()):
-                    order, now, ties = new, end, t2
+                new = order[:a] + mid + order[b + 1:]
+                end, st = onward(new, a, state)
+                if end < now + heat * (1.0 - step / steps) * -math.log(1.0 - rng.random()):
+                    order, now, state = new, end, st
+                    ties = tied(state)
                     if end < best[0]:
                         best = (end, order)
             return best
 
-        best = min(moved_on(packed(), STEPS[0]) for j in range(STARTS))
+        best = min(moved_on(packed(), STEPS[0], HEAT) for j in range(STARTS))
         for steps in STEPS[1:]:
-            best = moved_on(best[1], steps)
+            best = moved_on(best[1], steps, HEAT)
         KEPT["order"] = best[1]
         KEPT["end"] = best[0]
     order = KEPT["order"]

import math
import numpy as np
from concourse.bass import DstId, RemoteDMATransfer
from concourse.mybir import AluOpType as OP, ActivationFunctionType as AF, AxisListType

NV, HOP, NC = 6, 3, 8
W = 2048
WX = 128
WT = W + 8
CH = 2048
BIG = 2.0 ** 21
HUGE = 2.0 ** 16
TOP = 2.0 ** 18
WHOLE23 = 1.5 * 2.0 ** 23
KIND = {0: "AL", 1: "AA", (4, 0): "AA", (5, 0): "AA"}
DABS = (0, 1)
AST = [(0, 0), (0, 1)]
FIRST = {}
WHOLE = ()
ONV = {"O": [(t, 0) for t in range(4)], "ET": [(0, 0), (0, 1)], "W": [1]}
UDUP = True
NR = 2
VG = [(0, 0, 0), (0, 1, 0)]

FT = {}
IT = {}


def _fields(d, items):
    o = 0
    for k, n in items:
        d[k] = (o, n)
        o += n
    return o


NF = _fields(FT, [("LU", 128), ("Bs", 128), ("As1", 8), ("As2", 64), ("Cb", 128), ("ABE", 64)])

SCRATCH = {
    "tp": ("sbuf", [128, 256], "int32"), "tsx": ("sbuf", [128, 256], "int32"),
    "tl": ("sbuf", [128, 256], "int32"), "tq": ("sbuf", [128, 256], "int32"),
    "Lnum": ("sbuf", [128, 6 * 256], "int32"), "Loff": ("sbuf", [128, 9 * 256], "uint16"),
    "Vk": ("sbuf", [128, 9 * 256], "int32"),
    "H0": ("sbuf", [128, 520], "float32"), "H1": ("sbuf", [128, 520], "float32"),
    "H2": ("sbuf", [128, 512], "float32"), "H3": ("sbuf", [128, 512], "float32"),
    "res": ("sbuf", [128, 1024], "int32"), "cst": ("sbuf", [128, 12 * 128], "bfloat16"),
    "xb": ("sbuf", [128, W], "bfloat16"),
    "i16": ("sbuf", [128, 256], "float16"), "Lh": ("sbuf", [128, 7 * 256], "float16"), "eq": ("sbuf", [128, 6 * 256], "float16"),
    "Rq": ("sbuf", [128, 6 * 256], "float16"),
    "fin": ("sbuf", [128, 1024], "float32"),
    "LoffB": ("sbuf", [128, 512], "uint16"), "VkB": ("sbuf", [128, 512], "int32"), "L5": ("sbuf", [128, 256], "int32"),
    "R5": ("sbuf", [128, 256], "int32"), "R5B": ("sbuf", [128, 256], "int32"),
    "tf": ("sbuf", [128, 4 * NF], "float32"),
    "E0": ("sbuf", [128, 192], "bfloat16"),
    "mmsg": ("sbuf", [128, 12 * 128], "bfloat16"), "mland": ("sbuf", [128, 12 * 64], "bfloat16"),
    "emsg": ("sbuf", [128, 12 * 128], "bfloat16"), "eland": ("sbuf", [128, 12 * 128], "bfloat16"),
    "ETs": ("sbuf", [128, 4 * 192], "bfloat16"), "cj": ("sbuf", [128, 256], "bfloat16"),
    "cz1": ("sbuf", [128, 128], "bfloat16"), "ch": ("sbuf", [128, 128], "bfloat16"), "blkH": ("sbuf", [128, 128], "bfloat16"),
    "Bh": ("sbuf", [128, 144], "bfloat16"), "Bhn": ("sbuf", [128, 144], "bfloat16"),
    "Ind": ("sbuf", [128, 1024], "bfloat16"), "maskz": ("sbuf", [128, 1024], "bfloat16"),
    "pr0": ("sbuf", [128, 64], "bfloat16"), "pair": ("sbuf", [128, 64], "float32"), "grp8": ("sbuf", [128, 128], "float32"),
    "one": ("sbuf", [128, 1024], "bfloat16"), "idn": ("sbuf", [128, 128], "bfloat16"),
    "nidn": ("sbuf", [128, 128], "bfloat16"), "kidn": ("sbuf", [128, 128], "bfloat16"),
    "nkidn": ("sbuf", [128, 128], "bfloat16"), "uidn": ("sbuf", [128, 128], "bfloat16"),
    "blk0": ("sbuf", [128, 128], "bfloat16"), "blkE": ("sbuf", [128, 128], "bfloat16"),
    "blk": ("sbuf", [128, 128], "bfloat16"), "blkP": ("sbuf", [128, 128], "bfloat16"),
    "blkN": ("sbuf", [128, 128], "bfloat16"), "blk2": ("sbuf", [128, 128], "float32"),
    "Bp": ("sbuf", [128, 144], "bfloat16"), "Bn": ("sbuf", [128, 144], "bfloat16"), "Be": ("sbuf", [128, 144], "bfloat16"),
    "cz": ("sbuf", [128, 128], "bfloat16"), "cu": ("sbuf", [128, 128], "bfloat16"),
    "cc": ("sbuf", [128, 128], "bfloat16"), "o32": ("sbuf", [128, 128], "bfloat16"),
    "kin": ("sbuf", [128, 16], "int32"), "k37": ("sbuf", [128, 8], "float32"),
    "wti": ("sbuf", [128, 8], "int32"), "thi": ("sbuf", [128, 8], "int32"),
    "tci": ("sbuf", [128, 16], "int32"), "tcf": ("sbuf", [128, 16], "float32"),
    "ai": ("sbuf", [128, 6 * 8], "int32"), "af": ("sbuf", [128, 6 * 16], "float32"),
    "junk": ("sbuf", [128, 64], "bfloat16"),
    "R0": ("psum", [128, 1024], "float32"), "R1": ("psum", [128, 1024], "float32"),
    "SB": ("psum", [128, 512], "float32"), "DB": ("psum", [128, 512], "float32"),
    "ZB": ("psum", [128, 512], "float32"), "MB": ("psum", [128, 512], "float32"),
}
for _t in range(NV - 1):
    SCRATCH["win%d" % _t] = ("sbuf", [128, WT], "float32")
    SCRATCH["ext%d" % _t] = ("sbuf", [128, WX], "bfloat16")
for _z in range(4):
    for _n in ("s", "dp", "ra", "l")[:4 if _z < 3 else 3]:
        SCRATCH["%s%d" % (_n, _z)] = ("sbuf", [128, CH], "bfloat16")
for _z in range(2):
    for _n in ("vb", "vc", "sc"):
        SCRATCH["%s%d" % (_n, _z)] = ("sbuf", [128, CH], "bfloat16")

SEMAPHORES = (["sV", "sS", "sP", "sG", "lsem", "in"] + ["w%d" % t for t in range(2, 2 * NV - 2)]
              + ["m%d" % i for i in range(12)] + ["e%d" % i for i in range(12)]
              + ["ld%d" % i for i in range(12)] + ["mu", "mv", "ml0", "ml1", "mr0", "mr1"] + ["st%d" % i for i in range(10)]
              + ["ad%d" % i for i in range(14)] + ["x%d" % t for t in range(1, NV - 1)])
ENGINES = {"fold": lambda en: en[0::2], "small": lambda en: en[len(en) // 2:], "bulk": lambda en: en[:len(en) // 2]}

CYC = 0.83e-3 * 1.15
PEC = 0.417e-3 * 1.15
GAM = 1.5
WAKE = 0.08
LEAD, PACE, OPEN, LEAD0, STRETCH, STRETCH0 = 10.0, 20.0, 20.0, 8.0, 1.0, 1.0
STARTS, SWEEPS, STEPS = 3, 30, (6000, 45000)
SEED, SHAKE, SPAN, SOME, HEAT = 2, 6.0, 12.0, 0.2, 0.1
CASES = [(0.9, 0.85, 1.0, 0.07, 1.0), (1.05, 1.2, 1.4, 0.1, 1.0), (1.0, 1.0, 1.2, 0.08, 1.5)]
KEPT = {}


def rank_program(g, core, T, topo):
    rank = T.rank_of(core)
    if rank is None:
        return
    ENG = {"V": g.vector, "S": g.scalar, "P": g.tensor, "G": g, "Y": g.sync}
    ESEM = {"V": "sV", "S": "sS", "P": "sP", "G": "sG"}
    PSUM = [k for k in SCRATCH if SCRATCH[k][0] == "psum"]
    ops = []
    acc = {}
    lead = [(-1, 0)]
    boost = [1000.0]

    def R(b, lo, hi, st=1, p=None):
        return (b, lo, hi, st, p)

    def ap(r):
        b, lo, hi, st, p = r
        sl = slice(lo, hi, st) if st != 1 else slice(lo, hi)
        return T[b][p[0]:p[1], sl] if p else T[b][:, sl]

    def n_of(r):
        return (r[2] - r[1] + r[3] - 1) // r[3]

    def ps(r):
        return r[0] in PSUM

    def overlap(a, b):
        if a[1] >= b[2] or b[1] >= a[2] or (a[4] and b[4] and (a[4][0] >= b[4][1] or b[4][0] >= a[4][1]) and a[0] == "Ind"):
            return False
        if a[0][0] != "H" and (a[1] - b[1]) % math.gcd(a[3], b[3]) != 0:
            return False
        return True

    def op(eng, emit, rd, wr, occ, lat=None, sem=None, inc=0, deps=()):
        k = len(ops)
        dep = set(deps)
        banks = set()
        for w, regs in ((False, rd), (True, wr)):
            for r in regs:
                lst = acc.setdefault(r[0], [])
                if r[0] in PSUM:
                    banks.update((r[0], b) for b in range(r[1] // 512, (r[2] - 1) // 512 + 1))
                for (k2, r2, w2) in lst:
                    if k2 != k and (w or w2) and overlap(r, r2):
                        dep.add(k2)
        for w, regs in ((False, rd), (True, wr)):
            for r in regs:
                lst = acc[r[0]]
                if w and r[3] == 1 and r[4] is None:
                    lst[:] = [x for x in lst if x[0] == k or not (x[1][1] >= r[1] and x[1][2] <= r[2])]
                lst.append((k, r, w))
        ops.append({"eng": eng, "wr": wr, "banks": sorted(banks), "emit": emit, "dep": dep, "occ": occ, "lat": occ + 0.03 if lat is None else lat,
                    "sem": sem, "inc": inc, "lead": lead[0], "boost": boost[0] + FIRST.get((wr[0][0] if wr else "-").rstrip("0123456789"), 0.0)})
        return k

    def vcost(n, f=1.0):
        return 0.05 + max(64, n * f) * CYC

    def two(*rs):
        for r in rs:
            if not (r[0] in SCRATCH and SCRATCH[r[0]][2] in ("bfloat16", "uint16", "float16")) or ps(r):
                return 1.0
        return 0.5

    def vtt(out, a, b, alu):
        f = 1.0 if (ps(a) or ps(b)) else 2.0
        return op("V", lambda e: [e.tensor_tensor(out=ap(out), in0=ap(a), in1=ap(b), op=alu)], [a, b], [out], vcost(n_of(out), f))

    def vts(out, a, s1, op0, s2=None, op1=None):
        cols = [x for x in (s1, s2) if isinstance(x, tuple)]

        def em(e):
            x1 = ap(s1) if isinstance(s1, tuple) else s1
            x2 = ap(s2) if isinstance(s2, tuple) else s2
            if op1 is None:
                return [e.tensor_scalar(out=ap(out), in0=ap(a), scalar1=x1, scalar2=None, op0=op0)]
            return [e.tensor_scalar(out=ap(out), in0=ap(a), scalar1=x1, scalar2=x2, op0=op0, op1=op1)]
        return op("V", em, [a] + cols, [out], vcost(n_of(out), two(out, a)))

    def vcopy(out, a):
        return op("V", lambda e: [e.tensor_copy(out=ap(out), in_=ap(a))], [a], [out], vcost(n_of(out), two(out, a)))

    def vset(out, c):
        return op("V", lambda e: [e.memset(ap(out), c)], [], [out], vcost(n_of(out), two(out)))

    def vscan(out, a, b, op0, op1):
        return op("V", lambda e: [e.tensor_tensor_scan(out=ap(out), data0=ap(a), data1=ap(b), initial=0.0, op0=op0, op1=op1)],
                  [a, b], [out], vcost(n_of(out), two(out, a, b)))

    def act(out, a, func, scale=None, bias=None, acc_out=None):
        def em(e):
            kw = {}
            if scale is not None:
                kw["scale"] = scale
            if bias is not None:
                kw["bias"] = ap(bias) if isinstance(bias, tuple) else bias
            if acc_out is not None:
                kw["accum_out"] = ap(acc_out)
            return [e.activation(out=ap(out), in_=ap(a), func=func, **kw)]
        return op("S", em, [a] + ([bias] if isinstance(bias, tuple) else []), [out] + ([acc_out] if acc_out else []),
                  0.065 + max(64, n_of(out)) * CYC)

    def gath_s(out, win, off):
        k = op("S", lambda e: [e.activation(out=ap(out), in_=ap(win).indirect(ap(off)), func=AF.Copy)], [win, off], [out],
               0.065 + n_of(out) * GAM * CYC)
        ops[k]["gather"] = True

    def gath_v(out, win, off):
        k = op("V", lambda e: [e.tensor_copy(out=ap(out), in_=ap(win).indirect(ap(off)))], [win, off], [out], 0.05 + n_of(out) * GAM * CYC)
        ops[k]["gather"] = True

    def gath_sub(out, win, off, b):
        k = op("V", lambda e: [e.tensor_tensor(out=ap(out), in0=ap(win).indirect(ap(off)), in1=ap(b), op=OP.subtract)],
               [win, off, b], [out], 0.05 + n_of(out) * GAM * CYC)
        ops[k]["gather"] = True

    def pe(mms):
        rd, wr, cost = [], [], 0.0
        for (o, l, r, a, z) in mms:
            for x in (l, r):
                if x not in rd:
                    rd.append(x)
            if o not in wr:
                wr.append(o)
            f = 4.0 if SCRATCH[r[0]][2] == "float32" else 1.0
            cost += f * max(min(64, n_of(l)), n_of(r)) * PEC

        def em(e):
            return [e.matmul(out=ap(o), lhsT=ap(l), rhs=ap(r), start=a, stop=z) for (o, l, r, a, z) in mms]
        rd2 = {}
        for x in rd:
            key = x[0]
            if key in rd2:
                rd2[key] = (key, min(rd2[key][1], x[1]), max(rd2[key][2], x[2]), 1, x[4] if x[4] == rd2[key][4] else None)
            else:
                rd2[key] = x
        return op("P", em, list(rd2.values()), wr, cost + 0.01, cost + 0.1)

    def group(out, terms):
        return [(out, l, r, j == 0, j == len(terms) - 1) for j, (l, r) in enumerate(terms)]

    def gsel(out, a, pattern, cmp, base, cm):
        return op("G", lambda e: [e.affine_select(out=ap(out), in_=ap(a), pattern=pattern, compare_op=cmp, fill=0.0, base=base,
                                                  channel_multiplier=cm)], [a], [out], 0.2 + 2 * n_of(out) * CYC)

    loads = []

    def load(q, out, name, lat):
        src = T[name][:] if n_of(out) == T[name].shape[1] else T[name][:, out[1]:out[2]]
        k = op(q, lambda e: [e.dma_start(out=ap(out), in_=src)], [], [out], 0.05, lat, sem="ld%d" % len(loads), inc=16)
        ops[k]["first"] = len(loads)
        loads.append(k)

    def store(q, name, lo, hi, src, sem):
        return op(q, lambda e: [e.dma_start(out=T[name][:, lo:hi], in_=ap(src))], [src], [("out_" + name, lo, hi, 1, None)], 0.1, 3.0,
                  sem=sem, inc=16)

    nsent = [0]

    def send(dst_rank, out, src, sem, lat=2.5, occ=0.8, use="small", deps=(), gone=None):
        dst = T.cores[dst_rank % NC]
        rid, pid = topo.addr(dst)[0], topo.addr(dst)[1]
        en = topo.engines(core, dst)
        en = ENGINES[use](en)
        n = len(en)
        mask = sum(1 << q for q in en)
        if gone is None:
            nsent[0] += n
        left = T.sem[gone or "lsem"]
        if isinstance(src, list):
            def em(e):
                return [e.remote_dma_fused([RemoteDMATransfer(dst_ids=[DstId(rid=rid, pnc=pid)], dma_engine_mask=mask, remote_sem=T.sem[sem],
                                                              srcs=[ap(x) for x in src], dsts=[ap(out)], alu_op=2)], local_sem=left)]
        else:
            def em(e):
                return [e.remote_dma(ap(out), ap(src), T.sem[sem], left, pid, rid, mask)]
        srcs = src if isinstance(src, list) else [src]
        k = op("G", em, srcs, [], occ, occ, sem="lsem", inc=0, deps=deps)
        if gone:
            op("N", None, srcs, [], 0.0, lat, sem=gone, inc=n, deps=(k,))
        op("N", None, [], [out], 0.0, lat, sem=sem, inc=n, deps=(k,))
        return k

    def send_columns(t, X, deps=()):
        a, b = (0, W // 2, WT)[X:X + 2]
        send(rank - HOP * t, R("win%d" % t, a, b), R("win0", a, b), "w%d" % (2 * t + X), 12.0, use="bulk", deps=deps)
        if X == 1:
            send(rank - HOP * t, R("ext%d" % t, 0, WX), R("ext0", 0, WX), "x%d" % t, deps=deps)

    I, NIDN, KI, NKI = R("idn", 0, 128), R("nidn", 0, 128), R("kidn", 0, 128), R("nkidn", 0, 128)
    ONE, BLK, ONE64 = R("one", 0, 128), R("blk", 0, 128), R("one", 0, 64)
    HALF, K5, NK5, CK, CQ, CM, CN, CX, CK1, CN1, NM1, HM1 = [R("cst", 128 * j, 128 * j + 128) for j in range(12)]
    load("Y", R("xb", 0, W), "xt", 3.9)
    for j, (b, nm) in enumerate((("tsx", "sl"), ("tl", "ll"), ("tp", "pl"), ("tq", "ql"))):
        load("Y", R(b, 0, 256), nm, 4.5 + 0.6 * j)
    load("Y", R("wti", 0, 1), "wt", 6.6)
    load("Y", R("E0", 0, 128), "ed", 6.9)
    load("Y", R("thi", 0, 1), "th", 7.1)
    vset(R("one", 0, 128), 1.0)
    vset(R("win0", W, WT), 0.0)
    gsel(R("blk0", 0, 128), ONE, [[-16, 8], [0, 16]], OP.is_ge, 0, 1)
    gsel(BLK, R("blk0", 0, 128), [[16, 8], [0, 16]], OP.is_ge, 15, -1)
    gsel(I, ONE, [[-1, 128]], OP.is_equal, 0, 1)
    boost[0] = 0.0
    vcopy(R("tcf", 0, 1), R("wti", 0, 1))
    vts(R("af", 12, 13), R("thi", 0, 1), -1.0, OP.add, -BIG, OP.mult)
    vts(R("win0", W, W + 1), R("thi", 0, 1), -1.0 - TOP / 4.0, OP.add, -BIG, OP.mult)
    vts(R("ext0", 0, 128), BLK, R("tcf", 0, 1), OP.mult, 1.0 / 2048.0, OP.mult)
    for h in range(2):
        a, b = R("win0", 1024 * h, 1024 * h + 1024), R("xb", 1024 * h, 1024 * h + 1024)
        if h in ONV["W"]:
            vts(a, b, -128.0, OP.add, HUGE + 1.0, OP.mult)
        else:
            act(a, b, AF.Identity, HUGE + 1.0, -128.0 * (HUGE + 1.0))
        send_columns(1, h)
    vset(R("one", 128, 1024), 1.0)
    op("G", lambda e: [e.iota(ap(R("kin", 0, 1)), [[0, 1]], 0, 1)], [], [R("kin", 0, 1)], 0.2)
    IND = [R("Ind", 0, 1024, 1, (32 * h, 32 * h + 32)) for h in range(2)]
    gsel(IND[0], R("one", 0, 1024, 1, (0, 32)), [[-1, 32], [0, 32]], OP.is_equal, 0, 1)
    op("Y", lambda e: [e.dma_start(out=ap(IND[1]), in_=ap(IND[0]))], [IND[0]], [IND[1]], 0.05, 3.0, sem="in", inc=16)
    for out, src, c in ((NIDN, I, -1.0), (NM1, I, -1.0 / HUGE), (HM1, I, 0.5 / HUGE),
                        (R("blkP", 0, 128), BLK, BIG),
                        (R("cz1", 0, 128), ONE, -BIG * HUGE * 31.75 / 128.0),
                        (R("blkN", 0, 128), BLK, -BIG), (R("blk2", 0, 128), BLK, 2.0),
                        (R("cz", 0, 128), ONE, -BIG * 31.75 / 128.0),
                        (R("o32", 0, 128), ONE, -1.0 / 32.0),
                        (R("cc", 0, 128), ONE, -15.5 / 8192.0),
                        (HALF, I, 0.5), (K5, I, 512.0), (NK5, I, -512.0), (CQ, ONE, -1.0 / 512.0),
                        (CM, ONE, WHOLE23 / 128.0), (CX, ONE, TOP / 128.0)):
        act(out, src, AF.Copy, c)
    for out, c in ((CN, 8.0), (CN1, 9.0)):
        vset(out[:4] + ((0, 64),), -WHOLE23 / 64.0)
        vset(out[:4] + ((64, 128),), c)
    I16, N16 = R("i16", 0, 128), R("i16", 128, 256)
    vcopy(I16, I)
    vts(N16, I, -1.0, OP.mult)
    vset(R("DB", 0, 512, 4), 0.0)
    vset(R("Bp", 0, 144), 0.0)
    vts(R("Bp", 15, 128, 16), R("blk", 0, 128, 16), BIG, OP.mult)
    act(R("Bn", 0, 144), R("Bp", 0, 144), AF.Copy, -1.0)
    act(R("Be", 0, 144), R("Bp", 0, 144), AF.Copy, -4.0 / BIG)
    vset(R("cu", 0, 128, 1, (0, 64)), 129.0 / 64.0)
    vset(R("cu", 0, 128, 1, (64, 128)), 2.0 ** -12)
    vset(R("cj", 0, 128, 1, (0, 64)), 2.0 ** -18)
    vset(R("cj", 0, 128, 1, (64, 128)), 1.0 / 128.0)
    vset(R("E0", 128, 192), 0.0)
    vset(R("maskz", 0, 1024), 256.0 * HUGE)
    vset(R("maskz", 0, 1024, 32), -256.0 * HUGE)
    P8 = (0, 8)
    gsel(R("pr0", 0, 64), ONE64, [[-2, 64]], OP.is_ge, 0, 1)
    gsel(R("pair", 0, 64), R("pr0", 0, 64), [[2, 64]], OP.is_ge, 1, -1)
    gsel(R("blk0", 0, 128, 1, P8), R("one", 0, 128, 1, P8), [[1, 128]], OP.is_ge, 0, -16)
    gsel(R("grp8", 0, 128, 1, P8), R("blk0", 0, 128, 1, P8), [[-1, 128]], OP.is_ge, 15, 16)
    vts(R("kin", 8, 9), R("kin", 0, 1), 15, OP.bitwise_and)
    for h in range(2):
        c = 37.0 * 16 * h + 8 * 2048.0 - 31.0 / 64.0
        vts(R("k37", h, h + 1), R("kin", 8, 9), 37.0, OP.mult, c, OP.add)
        vts(R("k37", 2 + h, 3 + h), R("kin", 8, 9), 37.0, OP.mult, c + 15.5, OP.add)

    moved = [False]

    def Ln(k, X):
        if k <= 0:
            return R(("tq", "tp", "tsx", "tl")[k + 3], 128 * X, 128 * X + 128)
        return R("Lnum", (k - 1) * 256 + 128 * X, (k - 1) * 256 + 128 * X + 128)

    def Lu(k, X, h=None):
        b, o = ("LoffB", (k - 3) * 256 + 128 * X) if moved[0] and k < NV - 1 else ("Loff", (k + 3) * 256 + 128 * X)
        return R(b, o, o + 128) if h is None else R(b, o + 64 * h, o + 64 * h + 64)

    def Vk(k, X):
        b, o = ("VkB", (k - 3) * 256 + 128 * X) if moved[0] and k < NV - 1 else ("Vk", (k + 3) * 256 + 128 * X)
        return R(b, o, o + 128)

    def Lh(k, X):
        return R("Lh", (k + 1) * 256 + 128 * X, (k + 1) * 256 + 128 * X + 128)

    def voff(k):
        return 2048.0 * (2 + (k if k > -3 else -1))

    def steps(t, X, j=None):
        b, o = ("H%d" % (2 + X), 0) if t == NV - 1 else ("H%d" % X, NV - t)
        return R(b, o, o + 512) if j is None else R(b, o + j, o + 512, 4)

    def gcopy(out, a):
        gsel(out, a, [[0, n_of(out)]], OP.is_ge, 0, 0)

    nadd = [0]

    def add_into(out, src, rd):
        op("G", lambda e: [e.dma_start(out=ap(out), in_=src, accum_op=OP.add)], rd + [out], [out], 1.6, 4.5, sem="ad%d" % nadd[0], inc=16)
        nadd[0] += 1

    def make_v(k, X, src):
        add_into(Vk(k, X), ap(src), [src])

    for lo, hi in ((k, k + 1) for k in range(1, NV)):
        v = R("Vk", (lo + 3) * 256, (hi + 3) * 256)
        op("G", lambda e, v=v, lo=lo, hi=hi: [e.iota(ap(v), [[2048, hi - lo], [0, 256]], int(voff(lo)), 0)], [], [v],
           0.15 + 2 * n_of(v) * CYC)

    def slot(b, X, j):
        return R(b, 768 * X + j, 768 * X + 768, 6)

    def every(r, h):
        return R(r[0], r[1] + h, r[2], 2)

    for X in range(2):
        for k in (-1, -2, 0, -3):
            (gcopy if X == 1 or k < -1 else vcopy)(Lu(k, X), Ln(k, X))
        for j, k in ((1, 0), (2, -3)):
            vts(steps(0, X, j), Ln(k, X), voff(k), OP.add)
        gcopy(steps(0, X, 3), Ln(-2, X))
        gcopy(Lh(-1, X), Ln(-3, X))
        gcopy(Lh(0, X), Ln(0, X))

    def sums(out, parts, more=()):
        pe(group(out, list(more)
                 + [(R(coef, 15 - i, 143 - i), R(tile[0], tile[1] + i, tile[2], 16)) for (coef, tile) in parts for i in range(16)]))

    nreg = [0]

    def size(out, terms):
        rb = "R%d" % (nreg[0] % NR)
        nreg[0] += 1
        mm = []
        for j in range(2):
            mm += group(R(rb, 512 * j, 512 * j + 512), [(l, R(r[0], r[1] + 512 * j, r[1] + 512 * j + 512, 1, r[4])) for (l, r) in terms])
        pe(mm)
        act(out, R(rb, 0, 1024), AF.Abs)

    def relu2(out, a, c=1.0):
        vts(out, a, 0.0, OP.max, 2.0 * c, OP.mult)

    for t in range(NV):
        last = t == NV - 1
        moved[0] = last
        wn = "ext%d" % (0 if last else t)
        WIN = R("win%d" % (0 if last else t) if t else "xb", 0, W)
        TH = R(WIN[0], W, W + 1) if t else R("af", 12, 13)
        for X in range(2):
            z, y, sl = (t % 2) * 2 + X, X, 2 * t + X
            lead[0] = (t, X)
            kind = "SS" if t == 0 else KIND.get((t, X), KIND[X])

            def F(nm, lo=0, hi=None):
                o, n = FT[nm]
                return R("tf", z * NF + o + lo, z * NF + o + (n if hi is None else hi))

            def tile(nm, h):
                q = z if nm in ("s", "dp", "ra") else sl % 3 if nm == "l" else y
                if nm in ("dq", "rq", "vo"):
                    nm, q = {"dq": "s", "rq": "dp", "vo": "ra"}[nm], 2 + y
                return R("%s%d" % (nm, q), 0, CH) if h is None else R("%s%d" % (nm, q), 1024 * h, 1024 * h + 1024)

            E = R("E0", 64 * X, 64 * X + 64) if t == 0 else R("eland", (sl - 2) * 128, (sl - 2) * 128 + 64)
            L = Ln(t, X)
            for h in range(2):
                if kind[h] == "S":
                    gath_s(tile("s", h), WIN, Lu(t - 1, X, h))
                    gath_sub(tile("dp", h), WIN, Lu(t - 2, X, h), tile("s", h))
                    relu2(tile("ra", h), tile("dp", h))
                    if t == 0:
                        gath_sub(tile("dq", h), WIN, Lu(-3, X, h), tile("s", h))
                        if X in DABS:
                            act(tile("rq", h), tile("dq", h), AF.Abs)
                        else:
                            relu2(tile("rq", h), tile("dq", h))
            def parts(what):
                return [None] if what in WHOLE and (kind[0] == kind[1] or what == "sc") else [0, 1]

            for h in parts("l"):
                (gath_v if (t, X, h) in VG else gath_s)(tile("l", h), WIN, Lu(t, X, h))
            for nm, k in (("s", t - 1), ("dp", t - 2)):
                for h in parts(nm):
                    if kind[h or 0] != "S":
                        gath_sub(tile(nm, h), WIN, Lu(k, X, h), tile("l", h))
            for h in parts("vc"):
                if kind[h or 0] == "L":
                    relu2(tile("vc", h), tile("dp", h))
                if kind[h or 0] == "A":
                    act(tile("vc", h), tile("dp", h), AF.Abs)
            for h in range(2):
                vscan(tile("sc", h), R("maskz", 0, 1024), tile("l", h), OP.min, OP.max)
            M, MR = R("mmsg", sl * 64, sl * 64 + 64), R("mland", sl * 64, sl * 64 + 64)
            gcopy(M, R("sc%d" % y, 31, CH, 32))
            km = send(rank + 4, MR, M, "m%d" % sl)
            if t + 2 < NV - 1:
                send_columns(t + 2, X, (km,))
            WM = R(wn, 0, 128)
            pe(group(R("MB", 0, 128), [(R(E[0], E[1], E[1] + 128), NIDN)])
               + group(R("MB", 128, 192), [(WM, E), (R("cj", 0, 128), ONE64)] + ([] if t else [(ONE, ONE64)])))
            JU = R("ETs", z * 192 + 128, z * 192 + 192)
            if (t, X) in ONV["ET"]:
                vts(R("ETs", z * 192, z * 192 + 192), R("MB", 0, 192), 128.0 if t else 0.0, OP.add)
            else:
                act(R("ETs", z * 192, z * 192 + 192), R("MB", 0, 192), AF.Identity, None, 128.0 if t else 0.0)
            us = [(WM, E), (NIDN, JU), (R("cu", 0, 128), ONE64)]
            if UDUP:
                U = R("MB", 192, 320)
                pe([m for h in range(2) for m in group(every(U, h), us)])
                vtt(F("LU"), L, U, OP.mult)
            else:
                U = R("MB", 192, 256)
                pe(group(U, us))
                for h in range(2):
                    vtt(every(F("LU"), h), every(L, h), U, OP.mult)
            if t == 0:
                colA = R("k37", 0, 2)
            else:
                colA = R("af", t * 16 + 8, t * 16 + 10)
                if X == 0:
                    cn, xa = R("MB", 448, 512), R("af", t * 16, t * 16 + 1)
                    pe(group(cn, [(R("o32", 0, 128), R("eland", (sl - 2) * 128 + 64, (sl - 2) * 128 + 128)),
                                  (R("o32", 0, 128), R("eland", (sl - 1) * 128 + 64, (sl - 1) * 128 + 128)),
                                  (R("cc", 0, 128), ONE64)]))
                    act(R("junk", 0, 64), cn, AF.Copy, acc_out=xa)
                    x32 = R("af", t * 16 + 4, t * 16 + 5)
                    vts(x32, xa, 1.5 * 2.0 ** 28, OP.add, -1.5 * 2.0 ** 28, OP.add)
                    vts(colA, R("k37", 2, 4), xa, OP.add, x32, OP.subtract)
            def half_of(j, h):
                return R("DB", j + 4 * h, 512, 8)

            for h in range(2):
                vts(half_of(1, h), every(F("LU"), h), 64.0, OP.mult, R(colA[0], colA[1] + h, colA[1] + h + 1), OP.add)
            Z = R("ZB", 0, 64)
            C, B, D, O = [R("SB", 128 * j, 128 * j + 128) for j in range(4)]

            for h in range(2):
                ind, ET = IND[h], R("ETs", z * 192, z * 192 + 128, 1, (32 * h, 32 * h + 32))
                if t == 0:
                    size(tile("vc", h), [(I, tile("s", h)), (I, tile("dp", h)), (NIDN, tile("l", h))])
                    size(tile("vo", h), [(I, tile("l", h)), (ET, ind)])
                    size(tile("vb", h), [(I, tile("s", h)), (NIDN, tile("l", h))])
                else:
                    size(tile("vb", h), [(I, tile("s", h)), (ET, ind)])
                    size(tile("ra", h), [(I, tile("dp", h)), (NIDN, tile("s", h))])
            A1, A2 = R("ZB", 64, 72), R("ZB", 128, 192, 1, P8)
            AS2 = F("As2")[:4] + (P8,)
            zs = [(R("cz1" if t else "cz", 0, 128), ONE64)]
            if (t, X) in AST:
                pe(group(A1, [(R(tile(nm, None)[0], i, CH, 16), R(coef, 0, 128, 16))
                              for (coef, nm) in ((("blkP", "ra"),) if t else (("blkP", "ra"), ("blkN", "dp"))) for i in range(16)]))
                act(F("As1"), A1, AF.Copy)
                pe(group(A2, [(F("As1"), R("pair", 0, 64))]))
                act(AS2, A2, AF.Copy, -1.0)
                zs.append((R("grp8", 0, 128, 1, P8), AS2))
            else:
                zs += [(R("blkN", 0, 128), R(tile("ra", None)[0], k, CH, 32)) for k in range(32)]
                pe([m[:4] + (False,) for m in group(Z, zs)])

            def part(r, h):
                return R(r[0], r[1] + 64 * h, r[1] + 64 * h + 64)

            if t == 0:
                sums(D, [("Bp", tile("rq", None))] + ([] if X in DABS else [("Bn", tile("dq", None))]))
                sums(B, [("Bp", tile("vb", None))])
                act(F("Bs"), B, AF.Identity, None, -BIG / 2.0)
                sums(O, [("Bp", tile("vo", None))])
                act(steps(t, X, 0), O, AF.Identity, None, TH)
                vtt(R("DB", 2, 512, 4), D, F("Bs"), OP.subtract)
                sums(C, [("Bp", tile("vc", None))])
                vtt(F("Cb"), C, F("Bs"), OP.subtract)
            else:
                for h in parts("vc"):
                    sums(C if h is None else part(C, h), [("Bp", tile("vc", h))] + ([("Bn", tile("dp", h))] if kind[h or 0] == "L" else []))
                for h in range(2):
                    sums(R("DB", 2 + 256 * h, 256 + 256 * h, 4), [("Be", tile("vb", h))], [(CX, ONE64)])
                if (t, X) in ONV["O"]:
                    vts(steps(t, X, 0), R("DB", 2, 512, 4), -BIG / 4.0, OP.mult, TH, OP.add)
                else:
                    act(steps(t, X, 0), R("DB", 2, 512, 4), AF.Identity, -BIG / 4.0, TH)
                vtt(F("Bs"), C, steps(t, X, 0), OP.subtract)
                vts(F("Cb"), F("Bs"), WHOLE23 * BIG * HUGE / 4.0, OP.add, (2.0 - WHOLE23) * BIG * HUGE / 4.0, OP.add)
            zc = group(Z, [(R("blk2", 0, 128), every(F("Cb"), 0)), (R("blk2", 0, 128), every(F("Cb"), 1))])
            zc[0] = zc[0][:3] + (False, False)
            pe(([m[:4] + (False,) for m in group(Z, zs)] if (t, X) in AST else []) + zc)
            for h in range(2):
                vtt(half_of(3, h), every(F("Cb"), h), Z, OP.max)
            vscan(R("res", 512 * X, 512 * X + 512), R("DB", 0, 512), steps(t, X), OP.min, OP.max)
            move = t == NV - 2
            home = rank + HOP * (NV - 1)
            NEW = R("L5", 128 * X, 128 * X + 128) if move else Ln(t + 1, X)
            vts(NEW, R("res", 512 * X + 3, 512 * X + 512, 4), 2047, OP.bitwise_and)
            if move:
                send(home, Ln(t + 1, X), NEW, "ml%d" % X)
            if not last:
                gcopy(Lu(t + 1, X), Ln(t + 1, X))
            EM, SG = R("emsg", sl * 128, sl * 128 + 64), R("emsg", sl * 128 + 64, sl * 128 + 128)
            act(SG, Z, AF.Sign)
            X1, X2 = R("MB", 320, 384), R("MB", 384, 448)
            pe(group(X1, [(I, E), (NM1 if t else NIDN, MR), (K5, SG)])
               + group(X2, [(HALF, E), (HM1 if t else HALF, MR), (CQ, ONE64), (CM, ONE64), (NK5, SG), (CN1 if t else CN, ONE64)]))
            act(F("ABE"), X1, AF.Abs, None, 384.0 if t else 512.0)
            vtt(EM, F("ABE"), X2, OP.min)
            if not last:
                send(rank + HOP * t if move else rank - HOP, R("eland", sl * 128, sl * 128 + 128), R("emsg", sl * 128, sl * 128 + 128),
                     "e%d" % sl)
                make_v(t + 1, X, Ln(t + 1, X))
                gcopy(steps(t + 1, X, 1), Vk(t + 1, X))
            if t == 0:
                vts(steps(1, X, 3), Ln(-1, X), voff(-1), OP.add)
            if t == NV - 3 and X == 1:
                send(home, R("LoffB", 0, 512), R("Loff", (t + 3) * 256, (t + 5) * 256), "mu", 4.5, use="bulk")
                send(home, R("VkB", 0, 512), R("Vk", (t + 3) * 256, (t + 5) * 256), "mv", 7.0, use="bulk")
                vts(R("fin", 0, 256), R("VkB", 256, 512), -voff(t + 1), OP.add)
                store("Y", "yp", 0, 256, R("fin", 0, 256), "st0")
                for j in range(4):
                    gcopy(steps(NV - 1, j % 2, 3 - j // 2), R("VkB", 128 * j, 128 * j + 128))
            if not last:
                gcopy(Lh(t + 1, X), NEW)
            if move:
                for h in range(2):
                    a, b = 768 * X + 384 * h, 768 * X + 384 * h + 384
                    pe([m for j in range(NV) for m in group(R("SB", 128 + j, 512, 6), [(I16, part(Lh(j - 1, X), h)), (N16, part(Lh(j, X), h))]
                                                            + ([] if j else [(CQ, ONE64)]))])
                    vts(R("eq", a, b), R("SB", 128, 512), 0.0, OP.is_equal)
                    vscan(R("Rq", a, b), R("eq", a, b), R("SB", 128, 512), OP.mult, OP.add)
                gcopy(R("R5", 128 * X, 128 * X + 128), slot("Rq", X, 5))
                send(home, R("R5B", 128 * X, 128 * X + 128), R("R5", 128 * X, 128 * X + 128), "mr%d" % X)
                gcopy(R("fin", 256 + 128 * X, 384 + 128 * X), Ln(t + 1, X))
                store("Y", "ys", 128 * X, 128 * X + 128, R("fin", 256 + 128 * X, 384 + 128 * X), "st%d" % (1 + 4 * X))
            if last:
                FL, FQ = R("fin", 512 + 128 * X, 640 + 128 * X), R("fin", 768 + 128 * X, 896 + 128 * X)
                vcopy(FL, NEW)
                PB = R("SB", 256, 384)
                vtt(PB, NEW, L, OP.is_equal)
                vtt(PB, R("R5B", 128 * X, 128 * X + 128), PB, OP.mult)
                vtt(FQ, L, PB, OP.add)
                store("Y", "yl", 128 * X, 128 * X + 128, FL, "st%d" % (2 + 4 * X))
                store("S", "yq", 128 * X, 128 * X + 128, FQ, "st%d" % (3 + 4 * X))
                store("Y", "ye", 64 * X, 64 * X + 64, EM, "st%d" % (4 + 4 * X))

    n = len(ops)
    succ = [[] for _ in range(n)]
    for k in range(n):
        for d in ops[k]["dep"]:
            succ[d].append(k)
    prio = [0.0] * n
    for k in range(n - 1, -1, -1):
        prio[k] = ops[k]["lat"] + max([prio[s] + 0.08 for s in succ[k]] + [0.0])

    KEPT["ops"], KEPT["prio"], KEPT["succ"] = ops, prio, succ

    def place(key, back):
        before, after = (succ, pred) if back else (pred, succ)
        at = [0.0] * n
        done = [0.0] * n
        used = {e: [] for e in ENG}
        held = {b: [] for x in bank for b in x}
        left = [len(x) for x in before]
        ready = [k for k in range(n) if not left[k]]
        while ready:
            k = min(ready, key=key.get)
            ready.remove(k)
            for q in after[k]:
                left[q] -= 1
                if not left[q]:
                    ready.append(q)
            s, e, c = 0.0, eng[k], occ[k]
            for q in before[k]:
                if done[q] > s:
                    s = done[q]
            if back:
                s += lat[k] - c
            if e != "N":
                u = used[e]
                lo, hi = (c - lat[k] - WAKE, c) if back else (0.0, lat[k] + WAKE)
                while True:
                    j = len(u)
                    while j > 0 and u[j - 1][1] > s:
                        j -= 1
                    while j < len(u) and u[j][0] < s + c - 1e-9:
                        s = max(s, u[j][1])
                        j += 1
                    s2 = s
                    for b in bank[k]:
                        h = held[b]
                        i = len(h) - 1
                        while i >= 0 and h[i][0] > s + lo - 4.0:
                            if h[i][2] != e and h[i][1] > s + lo + 1e-9 and h[i][0] < s + hi - 1e-9:
                                s2 = max(s2, h[i][1] - lo)
                            i -= 1
                    if s2 == s:
                        break
                    s = s2
                u.insert(j, (s, s + c))
                for b in bank[k]:
                    h = held[b]
                    i = len(h)
                    while i > 0 and h[i - 1][0] > s + lo:
                        i -= 1
                    h.insert(i, (s + lo, s + hi, e))
            at[k] = s
            done[k] = s + (c if back else lat[k]) + WAKE
        return at

    def replay(order, ties=None):
        waits, lastuse = [], {}
        for k in order:
            w = pred[k]
            for b in bank[k]:
                lu = lastuse.setdefault(b, {})
                w = w + [q for x, q in lu.items() if x != eng[k]]
                lu[eng[k]] = k
            waits.append(w)
        total = 0.0
        for (f, gam, dma, wake, ten), (oc, la) in zip(CASES, scaled):
            fin = [0.0] * n
            why = [None] * n
            free = {e: 0.0 for e in "VSPGYN"}
            prev = {}
            for k, w in zip(order, waits):
                e = eng[k]
                s, y = free[e], prev.get(e)
                for q in w:
                    if fin[q] > s:
                        s, y = fin[q], q
                if e != "N":
                    free[e] = s + oc[k]
                    prev[e] = k
                fin[k] = s + la[k]
                why[k] = y
            end = max(fin)
            total += end / (f * (0.6 + 0.4 * gam))
            if ties is not None:
                k = fin.index(end)
                while why[k] is not None:
                    if why[k] not in ops[k]["dep"] and "first" not in ops[k]:
                        ties.append((why[k], k))
                    k = why[k]
        return total / len(CASES)

    if "order" not in KEPT:
        pred = [sorted(o["dep"]) for o in ops]
        eng, occ, lat, bank = [[o[x] for o in ops] for x in ("eng", "occ", "lat", "banks")]
        early = [o["boost"] + (1e6 if "first" in o else 0.0) for o in ops]
        scaled = []
        for (f, gam, dma, wake, ten) in CASES:
            c = [dma if o["sem"] else f * (gam if o.get("gather") else ten if o["eng"] == "P" else 1.0) for o in ops]
            scaled.append(([occ[k] * c[k] for k in range(n)], [lat[k] * c[k] + wake for k in range(n)]))
        rng = np.random.default_rng(SEED)
        alone = [0.0] * n
        for tag in sorted({o["lead"] for o in ops}):
            mine = [k for k in range(n) if ops[k]["lead"] == tag]
            free, fin = {}, {}
            for k in sorted(mine, key=lambda q: (-prio[q], q)):
                s = max([free.get(eng[k], 0.0)] + [fin[q] for q in pred[k] if q in fin])
                if eng[k] != "N":
                    free[eng[k]] = s + occ[k]
                fin[k] = s + lat[k] + WAKE
                alone[k] = s
            t, X = tag
            for k in mine:
                alone[k] = alone[k] * (STRETCH if t else STRETCH0) + (OPEN + PACE * (t - 1) + LEAD * X if t > 0 else LEAD0 * X if t == 0 else -20.0)

        def packed():
            key = {k: (alone[k] * ("first" not in ops[k]) - early[k], k) for k in range(n)}
            best = None
            for sweep in range(SWEEPS):
                at = place(key, False)
                end = replay(sorted(range(n), key=lambda q: (at[q], q)))
                if best is None or end < best[0]:
                    best = (end, at)
                a = rng.random() * max(best[1]) - SPAN / 2
                shake = (rng.random(n) - 0.5) * SHAKE * (0.3 + rng.random()) * (rng.random(n) < SOME)
                was = [best[1][k] + (float(shake[k]) if sweep < 20 or a < best[1][k] < a + SPAN else 0.0) for k in range(n)]
                if sweep < 20 or sweep % 2 == 0:
                    bk = place({k: (-was[k], -k) for k in range(n)}, True)
                    was = [-(bk[k] + occ[k]) for k in range(n)]
                key = {k: (was[k] * ("first" not in ops[k]) - early[k], k) for k in range(n)}
            return sorted(range(n), key=lambda q: (best[1][q], q))

        (oc0, la0), (oc1, la1), (oc2, la2) = scaled
        wt = [1.0 / (3.0 * f * (0.6 + 0.4 * gam)) for (f, gam, dma, wake, ten) in CASES]
        seat = [[(b, eng[k]) for b in bank[k]] for k in range(n)]
        rival = [[(b, e) for b in bank[k] for e in "VSP" if e != eng[k]] for k in range(n)]

        def onward(order, a, was):
            f0, f1, f2, waits, ahead = [x[:] for x in was]
            last, lu = {}, {}
            for k in order[max(0, a - 120):a]:
                last[eng[k]] = k
                for x in seat[k]:
                    lu[x] = k
            for k in order[a:]:
                e, w = eng[k], pred[k]
                if seat[k]:
                    w = w + [lu[x] for x in rival[k] if x in lu]
                    for x in seat[k]:
                        lu[x] = k
                q = last.get(e) if e != "N" else None
                last[e] = k
                waits[k], ahead[k] = w, q
                if q is None:
                    s0 = s1 = s2 = 0.0
                else:
                    s0, s1, s2 = f0[q] - la0[q] + oc0[q], f1[q] - la1[q] + oc1[q], f2[q] - la2[q] + oc2[q]
                for q in w:
                    if f0[q] > s0:
                        s0 = f0[q]
                    if f1[q] > s1:
                        s1 = f1[q]
                    if f2[q] > s2:
                        s2 = f2[q]
                f0[k], f1[k], f2[k] = s0 + la0[k], s1 + la1[k], s2 + la2[k]
            return wt[0] * max(f0) + wt[1] * max(f1) + wt[2] * max(f2), (f0, f1, f2, waits, ahead)

        def tied(state):
            ties = []
            for fin, (oc, la) in zip(state, scaled):
                k = fin.index(max(fin))
                while True:
                    s, y = fin[k] - la[k] - 1e-9, None
                    for q in state[3][k]:
                        if fin[q] >= s:
                            y = q
                    if y is None:
                        y = state[4][k]
                        if y is None or fin[y] - la[y] + oc[y] < s:
                            break
                    if y not in ops[k]["dep"] and "first" not in ops[k]:
                        ties.append((y, k))
                    k = y
            return ties

        def moved_on(order, steps, heat):
            now, state = onward(order, 0, [[0.0] * n] * 5)
            ties = tied(state)
            best = (now, order)
            for step in range(steps):
                j, k = ties[int(rng.integers(len(ties)))]
                a, b = order.index(j), order.index(k)
                mid = order[a:b + 1]
                if rng.random() < 0.5:
                    take = {k}
                    for q in reversed(mid):
                        if q in take:
                            take.update(pred[q])
                    if j in take:
                        continue
                    mid = [q for q in mid if q in take] + [q for q in mid if q not in take]
                else:
                    take = {j}
                    for q in mid:
                        if q in take:
                            take.update(succ[q])
                    if k in take:
                        continue
                    mid = [q for q in mid if q not in take] + [q for q in mid if q in take]
                new = order[:a] + mid + order[b + 1:]
                end, st = onward(new, a, state)
                if end < now + heat * (1.0 - step / steps) * -math.log(1.0 - rng.random()):
                    order, now, state = new, end, st
                    ties = tied(state)
                    if end < best[0]:
                        best = (end, order)
            return best

        best = min(moved_on(packed(), STEPS[0], HEAT) for j in range(STARTS))
        for steps in STEPS[1:]:
            best = moved_on(best[1], steps, HEAT)
        KEPT["order"] = best[1]
        KEPT["end"] = best[0]
    order = KEPT["order"]
    lastuse = {}
    for k in order:
        for b in ops[k]["banks"]:
            lu = lastuse.setdefault(b, {})
            ops[k]["dep"].update(q for e, q in lu.items() if e != ops[k]["eng"])
            lu[ops[k]["eng"]] = k

    known = {e: {} for e in ENG}
    count = {"sV": 0, "sS": 0, "sP": 0, "sG": 0}
    event = [None] * n
    snap = [None] * n
    total = {}
    pos = {k: i for i, k in enumerate(order)}
    for k in order:
        o = ops[k]
        e = o["eng"]
        if e == "N":
            event[k] = (o["sem"], o["inc"])
            total[o["sem"]] = o["inc"]
            snap[k] = {}
            continue
        kn = known[e]
        for d in sorted(o["dep"], key=lambda q: -pos[q]):
            if event[d] is None:
                continue
            sm, v = event[d]
            if kn.get(sm, 0) >= v:
                continue
            ENG[e].wait_ge(T.sem[sm], v)
            kn[sm] = v
            for a, b in snap[d].items():
                if kn.get(a, 0) < b:
                    kn[a] = b
        ins = o["emit"](ENG[e])
        if o["sem"] is None:
            sm = ESEM[e]
            for x in ins:
                x.then_inc(T.sem[sm], 1)
            count[sm] += len(ins)
            event[k] = (sm, count[sm])
            total[sm] = count[sm]
        elif o["inc"]:
            for x in ins:
                x.then_inc(T.sem[o["sem"]], o["inc"])
            event[k] = (o["sem"], o["inc"])
            total[o["sem"]] = o["inc"]
        snap[k] = dict(kn)
    total["lsem"] = nsent[0]
    for sm in total:
        if known["G"].get(sm, 0) < total[sm]:
            g.wait_ge(T.sem[sm], total[sm])
